import numpy as np, ml_dtypes
CORES = [16,18,20,22]
N = 4
BF = ml_dtypes.bfloat16
def gentries(a):
    return np.ascontiguousarray(a.reshape(8, 16, -1).transpose(0, 2, 1)).reshape(8, -1)
def gtable(e):
    e = np.asarray(e); return np.ascontiguousarray(e.reshape(8, -1, 16).transpose(0, 2, 1)).reshape(128, -1).astype(np.int32)
S, K, SH, AC, RO, Z = 1024, 4096, 2, 9, 3, 1024
def one(w):
    c = np.add.accumulate(w, dtype=np.int64)
    return np.searchsorted(K * c, np.arange(K) * c[-1], side="right")
def ancestors(x, y, e):
    w = np.maximum(1, np.add.reduce(np.abs(x - y) <= e, axis=1, dtype=np.int64) >> SH)
    return np.stack([one(a) for a in w])
def parts(rng):
    fp = rng.random((N, 8, 16, S), dtype=np.float32); bp = rng.random((N, 8, 16, S), dtype=np.float32)
    nz = (rng.random((N, 8, 16, S), dtype=np.float32) - 0.5) * 0.125
    ob = 0.3 + 0.6 * rng.random((N, 8, 16, RO))
    lev = np.array([0.12, 0.18, 0.25, 0.36, 0.12, 0.18, 0.25, 0.36])[np.argsort(rng.random((N, 8)), axis=-1)][..., None]
    ep = lev * (0.7 + 0.6 * rng.random((N, 8, 16))); la = 0.2 + 0.6 * rng.random((N, 8, 16))
    r1 = 2.8 + 1.1 * rng.random((N, 8, 16)); r2 = 2.8 + 1.1 * rng.random((N, 8, 16))
    return fp, bp, nz, ob, ep, la, r1, r2, np.argsort(rng.random((N, 8, K)), axis=-1)
def pack(fp, bp, nz, ob, ep, la, r1, r2, p):
    d = {"f0": fp.reshape(N, 128, S).astype(BF), "b0": bp.reshape(N, 128, S).astype(BF), "nz": nz.reshape(N, 128, S).astype(BF), "obs": ob.reshape(N, 128, RO).astype(np.float32)}
    for k, v in (("eps", ep), ("lam", la), ("rf", r1), ("rb", r2)): d[k] = v.reshape(N, 128, 1).astype(np.float32)
    d["pi"] = np.stack([gtable(a) for a in p])
    return d
def pairing(rng, sf, sb, nand, n):
    h = max(1, AC >> SH)
    u = sf[one(np.where(sf != nand, h, 1))]; v = sb[one(np.where(sb != nand, h, 1))]
    a = rng.permutation(np.flatnonzero(u)); c = np.flatnonzero(~u); x = rng.permutation(np.flatnonzero(v)); z = rng.permutation(np.flatnonzero(~v))
    n = max(len(a) + len(x) - K, min(n, len(a), len(x))); p = np.zeros(K, np.int64)
    p[a[:n]] = x[:n]; p[a[n:]] = z[:len(a) - n]; p[c] = rng.permutation(np.concatenate([x[n:], z[len(a) - n:]]))
    return p
def setup_inputs(rng):
    return pack(*parts(rng))
def setup_inputs_spread(rng):
    fp, bp, nz, ob, ep, la, r1, r2, p = parts(rng); s = (N, 8, 1, S)
    fp = fp * np.exp2(-rng.integers(0, 4, s)) * (rng.random(s) > 0.0625); bp = bp * np.exp2(-rng.integers(0, 4, s)) * (rng.random(s) > 0.0625)
    nz = 2 * nz * np.exp2(-rng.integers(0, 4, s)) * (rng.random(s) > 0.0625)
    ob = 0.05 + 0.85 * rng.random(ob.shape); ep = np.exp2(-4 + 3 * rng.random((N, 8, 1))) * (0.7 + 0.3 * rng.random(ep.shape))
    la = rng.random(la.shape); r1 = 2 + 2 * rng.random(r1.shape); r2 = 2 + 2 * rng.random(r2.shape)
    return pack(fp, bp, nz, ob, ep, la, r1, r2, p)
def bits(rng, *s):
    return rng.integers(0, 2, s).astype(np.float32)
def setup_inputs_ends(rng):
    fp = bits(rng, N, 8, 16, S); bp = bits(rng, N, 8, 16, S); nz = 0.25 * bits(rng, N, 8, 16, S) - 0.125; ob = bits(rng, N, 8, 16, RO)
    cnt = rng.choice(np.array([7, 8, 9, 10]), (N, 8)); cnt[:, 0] = 0; cnt[:, 1] = 8; cnt[:, 2] = 9; cnt[:, 5] = 16; cnt[:, 7] = 16
    ep = (np.argsort(rng.random((N, 8, 16)), axis=-1) < cnt[..., None]).astype(np.float32)
    la = bits(rng, N, 8, 16); r1 = 4 * bits(rng, N, 8, 16); r2 = 4 * bits(rng, N, 8, 16)
    for x in (fp, bp):
        x[:, 0] = 1 - ob[:, 0, :, :1]
        for s in (0, S - 1): x[:, 0, :, s] = ob[:, 0, :, 0]
    mid = 1 + np.argsort(rng.random((N, 8, K - 2)), axis=-1); e = np.zeros((N, 8, 1), np.int64)
    p = np.concatenate([e + K - 1, mid, e], axis=2); p[:, 1::2] = p[:, 1::2, ::-1].copy()
    return pack(fp, bp, nz, ob, ep, la, r1, r2, p)
def crowd(rng):
    pools = []
    for turn in (0, 3):
        h = np.zeros((N, 8, S), np.int64)
        for q in range(N):
            for g in range(8):
                k = (g + q + turn) % 8
                if k == 0: h[q, g] = 16
                if k == 1: h[q, g] = 16; h[q, g, S - 1] = 15
                if k == 2: h[q, g] = rng.choice(np.array([0, 2 ** SH - 1, 2 ** SH, 15, 16]), S)
                if k == 3: h[q, g] = rng.integers(8, 10, S)
                if k == 4: h[q, g, 0] = 16
                if k == 6: h[q, g] = rng.integers(7, 10, S)
                if k == 7: h[q, g] = 16; h[q, g, 0] = 8
        order = np.argsort(rng.random((N, 8, 16, S), dtype=np.float32), axis=2)
        hit = rng.choice(np.array([0.375, 0.625], np.float32), (N, 8, 16, S)); miss = rng.choice(np.array([0.25, 0.75, 0.62890625], np.float32), (N, 8, 16, S))
        pools.append(np.where(order < h[:, :, None, :], hit, miss))
    return pools
def setup_inputs_corners(rng):
    fp, bp, nz, ob, ep, la, r1, r2, p = parts(rng); fp = 0.9 * fp; bp = 0.9 * bp; h = max(1, AC >> SH)
    for q in range(0, N, 2):
        for g in range(8):
            t = min(K, (0, 1, 2, K - 1, K, 2 * S - 1, 2 * S, 2 * S + 1)[(g + q) % 8]); nand = 4 * t > 3 * K; n = K - t if nand else t
            z = 3 * S // (2 * h + 3) if K <= 4 * t and not nand else S // (h + 2)
            sf = rng.permutation(S) < z; sb = rng.permutation(S) < z; m = rng.permutation(16) < AC
            fp[q, g, m] = np.where(sf, 0.625, 0.125); bp[q, g, m] = np.where(sb, 0.625, 0.125)
            ob[q, g, :, 0] = np.where(m, 0.125 if nand else 0.625, 1.0); ep[q, g] = np.where(m, 0.25 if nand else 0.125, 0.0); la[q, g] = np.where(m, 0.5, la[q, g])
            p[q, g] = pairing(rng, sf, sb, nand, n)
    cf, cb = crowd(rng)
    for q in range(1, N, 2):
        fp[q] = cf[q]; bp[q] = cb[q]; ob[q, :, :, 0] = 0.5; ep[q] = 0.125
        o = (q // 2) % 2; la[q, o::2] = 0.0; la[q, 1 - o::2] = 1.0
    return pack(fp, bp, nz, ob, ep, la, r1, r2, p)
def setup_inputs_calm(rng):
    fp, bp, nz, ob, ep, la, r1, r2, p = parts(rng); fp = 0.9 * fp; bp = 0.9 * bp; h = max(1, AC >> SH)
    r1 = 2.8 + 0.7 * rng.random(r1.shape); r2 = 2.8 + 0.7 * rng.random(r2.shape)
    m = rng.permutation(16) < AC; r1[..., m] = 0; r2[..., m] = 0
    zs = np.argsort(rng.random((N, 8, S)), axis=-1) < S // (h + 2)
    for q in range(N):
        for g in range(8):
            nand = (g // 4 + q) % 2 == 1; sf = zs[(q - 1) % N, g]; sb = zs[(q + 1) % N, (g - 1) % 8]
            nz[q, g, m] = np.where(zs[q, g], 0.125, -0.125 * rng.integers(0, 2, (AC, S)))
            fp[q, g, m] = np.where(sf, 0.125, 0.0); bp[q, g, m] = np.where(sb, 0.125, 0.0)
            ob[q, g] = np.where(m, 0.0 if nand else 0.125, 1.0)[:, None]; ep[q, g] = np.where(m, 0.0625 if nand else 0.03125, 0.0); la[q, g] = np.where(m, 0.5, la[q, g])
            p[q, g] = pairing(rng, sf, sb, nand, (g + q) % 4)
    return pack(fp, bp, nz, ob, ep, la, r1, r2, p)
def setup_inputs_rounding(rng):
    fp, bp, nz, ob, ep, la, r1, r2, p = parts(rng); ep[:] = 0.0; m = rng.permutation(16) < AC
    r1 = 2.8 + 0.7 * rng.random(r1.shape); r2 = 2.8 + 0.7 * rng.random(r2.shape); s = (N, 8, AC)
    kd = rng.permutation(np.array([0, 0, 0, 1, 1, 2, 2, 3]))[None, :, None]; none = np.float32(0)
    x, w, z = [a.astype(BF).astype(np.float32) for a in (0.1 + 0.8 * rng.random(s), 0.1 + 0.8 * rng.random(s), 0.125 * (rng.random(s) - 0.5))]
    x = np.where(kd == 3, none, x); z = np.where(kd == 3, none, z); la[:, :, m] = np.where(kd == 3, 0.0, la[:, :, m])
    e = (2.0 ** -6 + 2.0 ** -24 * rng.integers(1, 2 ** 18, s)).astype(np.float32)
    ep[:, :, m] = np.where(kd == 1, e, np.where(kd == 2, np.nextafter(e, none), none))
    fp[:, :, m] = x[..., None]; bp[:, :, m] = w[..., None]; nz[:, :, m] = z[..., None]
    j = rng.permutation(np.flatnonzero(~m))[:2]
    fp[:, :, j] = np.where(kd[..., None] < 2, np.float32(1), fp[:, :, j]); bp[:, :, j] = 0; nz[:, :, j] = 0
    la[:, :, j] = np.where(kd < 2, 0.5, la[:, :, j]); r1[:, :, j] = np.where(kd < 2, 4.0, r1[:, :, j]); r2[:, :, j] = 0
    l, u, v = [a[..., m].astype(np.float32) for a in (la, r1, r2)]
    for t in range(RO):
        if t > 0: x = np.roll(x, 1, axis=0); w = np.roll(np.roll(w, -1, axis=0), 1, axis=1)
        y = x + l * (w - x)
        ob[:, :, m, t] = np.where(kd == 3, np.exp2(-rng.integers(80, 111, s)), np.where(kd == 0, y, y - e))
        x = step(np.where(kd < 2, y, x), u, z); w = step(np.where(kd < 2, y, w), v, z)
    return pack(fp, bp, nz, ob, ep, la, r1, r2, p)
def check_ranges(d):
    bad = []
    for k, lo, hi in (("f0", 0, 1), ("b0", 0, 1), ("nz", -0.125, 0.125), ("obs", 0, 1), ("eps", 0, 1), ("lam", 0, 1), ("rf", 0, 4), ("rb", 0, 4), ("pi", 0, K - 1)):
        a = np.asarray(d[k]).astype(np.float64)
        if not (np.min(a) >= lo and np.max(a) <= hi): bad.append("range of " + k)
    x = np.stack([gentries(np.asarray(a)) for a in d["pi"]])
    if not np.array_equal(np.sort(x, axis=-1), np.broadcast_to(np.arange(K), x.shape)): bad.append("pi isn't a permutation in every group")
    return bad
def step(a, r, z):
    return np.minimum(np.maximum(r * (a - a * a) + z, np.float32(0)), np.float32(1))
def reference(f0, b0, nz, obs, eps, lam, rf, rb, pi):
    f = f0.astype(np.float32).reshape(N, 8, 16, S); b = b0.astype(np.float32).reshape(N, 8, 16, S); z = nz.astype(np.float32).reshape(N, 8, 16, S)
    y = obs.astype(np.float32).reshape(N, 8, 16, RO); e, la, r1, r2 = [a.astype(np.float32).reshape(N, 8, 16, 1) for a in (eps, lam, rf, rb)]
    pl = np.stack([gentries(a) for a in pi]).astype(np.int64); ye = []
    for t in range(RO):
        if t > 0:
            f = np.roll(f, 1, axis=0); b = np.roll(np.roll(b, -1, axis=0), 1, axis=1)
        nf, nb = [], []
        for q in range(N):
            yt = y[q, :, :, t:t + 1]; af = ancestors(f[q], yt, e[q]); ab = ancestors(b[q], yt, e[q])
            fi = np.take_along_axis(f[q], af[:, None, :], 2); bj = np.take_along_axis(b[q], np.take_along_axis(ab, pl[q], 1)[:, None, :], 2)
            m = fi + la[q] * (bj - fi)
            ok = np.add.reduce(np.abs(m - yt) <= e[q], axis=1, dtype=np.int64) >= AC
            kf = np.take_along_axis(f[q], af[:, None, ::K // S], 2); kb = np.take_along_axis(b[q], ab[:, None, ::K // S], 2)
            for g in range(8):
                w = np.flatnonzero(ok[g])[:2 * S]; u = w[0::2]; v = w[1::2]
                kf[g, :, :len(u)] = m[g][:, u]; kb[g, :, :len(v)] = m[g][:, v]
            nf.append(step(kf, r1[q], z[q])); nb.append(step(kb, r2[q], z[q]))
            if t == RO - 1:
                d = fi.astype(np.float64) - bj.astype(np.float64)
                ye.append(np.add.reduce(np.exp(-d * d).reshape(8, 16, K // Z, Z), axis=2).reshape(128, Z))
        f = np.stack(nf); b = np.stack(nb)
    return {"yf": f.reshape(N, 128, S).astype(np.float32), "yb": b.reshape(N, 128, S).astype(np.float32), "ye": np.stack(ye).astype(np.float32)}

def check_inputs(d):
    bad = list(check_ranges(d))
    if not bad:
        for name, y in reference(**d).items():
            for q in range(N):
                v = np.abs(np.asarray(y[q], np.float64))
                if v.max() > 4 * np.sqrt(np.mean(v * v)): bad.append('%s of rank %d is uneven' % (name, q))
    return bad

@@ -1,0 +1,620 @@
+from concourse.mybir import AluOpType as OP, ActivationFunctionType as AF
+
+S, K = 1024, 4096
+MAGIC = 12582912.0
+CWN = 8480
+KN = {
+    "loop": (512, 512, 512, 512, 512, 512, 512, 256, 256),
+    "sign": ((0, 1, 2, 3, 4, 5, 6),) * 3,
+    "sc": 256,
+    "miss": ((0, 0), (0, 1), (0, 0)),
+    "first": (1, 0, 0),
+    "bs": (512, 256, 256), "bn": (2048, 2048), "cmp": (512, 512), "cact": ((0, 1), (0, 1), ()), "yepe": 2, "yes": 256,
+    "ld": 512, "wc": 512,
+    "seed": 1, "tries": 100000, "heat": 0.3,
+}
+
+SCRATCH = {
+    "f16": ("sbuf", [128, S], "bfloat16"), "b16": ("sbuf", [128, S], "bfloat16"),
+    "nz0": ("sbuf", [128, S], "bfloat16"), "nz1": ("sbuf", [128, S], "bfloat16"),
+    "prm0": ("sbuf", [128, 8], "float32"), "prm1": ("sbuf", [128, 8], "float32"),
+    "pi32": ("sbuf", [128, 256], "int32"),
+    "pu0": ("sbuf", [128, 256], "uint16"), "pu1": ("sbuf", [128, 256], "uint16"),
+    "pf": ("sbuf", [128, S], "float32"), "pb": ("sbuf", [128, S], "float32"),
+    "snd": ("sbuf", [128, S], "float32"),
+    "lb": ("sbuf", [128, S], "float32"), "lf": ("sbuf", [128, S], "float32"),
+    "win": ("sbuf", [128, 3 * K], "float32"),
+    "dw": ("sbuf", [128, K], "float32"), "dd": ("sbuf", [128, K], "float32"),
+    "ab": ("sbuf", [128, 2048], "float32"), "sg": ("sbuf", [128, 2048], "bfloat16"),
+    "miss": ("sbuf", [128, K], "bfloat16"),
+    "mk": ("sbuf", [128, K], "bfloat16"), "cw": ("sbuf", [128, CWN], "bfloat16"),
+    "cn": ("sbuf", [128, 2048], "bfloat16"), "cmp": ("sbuf", [128, 2048], "bfloat16"),
+    "hit": ("sbuf", [128, 2048], "bfloat16"),
+    "hh": ("sbuf", [128, 2048], "float32"), "uu": ("sbuf", [128, 2048], "float32"),
+    "tt": ("sbuf", [128, 2048], "float32"), "yo": ("sbuf", [128, S], "float32"),
+    "wbf": ("sbuf", [128, 72], "bfloat16"), "wbb": ("sbuf", [128, 72], "bfloat16"),
+    "sm": ("sbuf", [128, 1024], "float32"),
+    "slf": ("sbuf", [128, 64], "uint16"), "slb": ("sbuf", [128, 64], "uint16"),
+    "mkw": ("sbuf", [128, 264], "bfloat16"), "okw": ("sbuf", [128, 264], "bfloat16"),
+    "okb": ("sbuf", [128, 256], "bfloat16"), "el": ("sbuf", [128, 264], "bfloat16"),
+    "aw": ("sbuf", [128, 256], "float32"), "al": ("sbuf", [128, 256], "uint16"),
+    "rk": ("sbuf", [128, 264], "float32"),
+    "emp": ("sbuf", [128, 64], "float32"), "pl": ("sbuf", [128, 18], "uint16"),
+    "cl": ("sbuf", [128, 128], "uint16"), "ix": ("sbuf", [128, 128], "float32"), "il": ("sbuf", [128, 128], "uint16"),
+    "sel": ("sbuf", [128, 144], "bfloat16"), "seln": ("sbuf", [128, 144], "bfloat16"),
+    "blk": ("sbuf", [128, 128], "bfloat16"), "tri": ("sbuf", [128, 512], "bfloat16"),
+    "qn": ("sbuf", [128, 144], "float32"), "qb": ("sbuf", [128, 144], "bfloat16"),
+    "off": ("sbuf", [128, 72], "bfloat16"), "one": ("sbuf", [128, 1032], "float32"),
+    "zer": ("sbuf", [128, 2048], "bfloat16"), "six": ("sbuf", [128, S], "bfloat16"),
+    "even": ("sbuf", [128, 1032], "float32"), "fb": ("sbuf", [128, 128], "float32"),
+    "kd": ("sbuf", [128, 24], "float32"), "cv": ("sbuf", [128, 272], "bfloat16"),
+    "ri": ("sbuf", [128, 8], "int32"), "rc": ("sbuf", [128, 8], "float32"),
+    "ps": ("psum", [128, 4096], "float32"),
+}
+NDMA = 60
+SEMAPHORES = (["pe", "dve", "act", "pool", "xp", "xz", "xl"] + ["x%s%d" % (h, c) for h in "bf" for c in range(4)]
+              + ["d%d" % i for i in range(NDMA)])
+PLAN = {}
+
+
+def rank_program(g, core, T, topo):
+    rank = T.rank_of(core)
+    if rank is None:
+        return
+    n = len(T.cores)
+    ops = []
+
+    def V(name, lo, hi, step=1):
+        return (name, lo, hi, step)
+
+    def P(bank, lo, hi, step=1):
+        return ("ps", 512 * bank + lo, 512 * bank + hi, step)
+
+    def num(v):
+        return isinstance(v, (int, float)) or v is None
+
+    def ap(v):
+        if num(v):
+            return v
+        if len(v) == 2:
+            return ap(v[0]).indirect(ap(v[1]))
+        t = T[v[0]]
+        return t[:, v[1]:v[2]] if v[3] == 1 else t[:, v[1]:v[2]:v[3]]
+
+    def size(v):
+        return 16 * size(v[1]) if len(v) == 2 else (v[2] - v[1] + v[3] - 1) // v[3]
+
+    def width(v):
+        return 2 if SCRATCH[v[0]][2] in ("bfloat16", "uint16") else 4
+
+    def regions(vs):
+        out = []
+        for v in vs:
+            if not num(v):
+                for w in (v if len(v) == 2 else (v,)):
+                    out.append(("ps", w[1] // 512 * 512, (w[2] + 511) // 512 * 512) if w[0] == "ps" else (w[0], w[1], w[2]))
+        return out
+
+    def rec(q, fn, rd, wr, cost, kind="c", sem=None):
+        r, w = regions(rd), []
+        for v in wr:
+            if len(v) == 2:
+                r += regions([v[1]])
+                w += regions([v[0]])
+            else:
+                w += regions([v])
+        ops.append({"q": q, "fn": fn, "r": r, "w": w, "kind": kind, "sem": sem, "cost": cost})
+
+    def price(out, ins, per=1.0, fast=False):
+        if len(out) == 2:
+            return ("sc", size(out))
+        if len(ins[0]) == 2:
+            return ("g", size(out))
+        if fast and all(width(v) == 2 for v in [out] + ins):
+            per = 0.5
+        return ("c", max(64.0, per * size(out)))
+
+    def ts(out, a, s1, s2, o0, o1=None, also=None):
+        if o1 is None:
+            rec("dve", lambda: g.vector.tensor_scalar(ap(out), ap(a), ap(s1), None, o0), [a, s1, also], [out], price(out, [a], 1.0, True))
+        else:
+            rec("dve", lambda: g.vector.tensor_scalar(ap(out), ap(a), ap(s1), ap(s2), o0, o1), [a, s1, s2], [out], price(out, [a], 1.0, True))
+
+    def tt(out, a, b, o):
+        rec("dve", lambda: g.vector.tensor_tensor(ap(out), ap(a), ap(b), o), [a, b], [out],
+            price(out, [a, b], 1.0 if "ps" in (a[0], b[0]) else 2.0))
+
+    def cp(out, a):
+        rec("dve", lambda: g.vector.tensor_copy(ap(out), ap(a)), [a], [out], price(out, [a], 1.0, True))
+
+    def ms(out, c):
+        rec("dve", lambda: g.vector.memset(ap(out), c), [], [out], price(out, [out], 1.0, True))
+
+    def scan(out, a, b, init, o0, o1):
+        rec("dve", lambda: g.vector.tensor_tensor_scan(ap(out), ap(a), ap(b), ap(init), o0, o1), [a, b, init], [out],
+            price(out, [a, b], 1.0, True))
+
+    def act(out, a, f, bias=0.0, scale=1.0, more=0.0):
+        k, c = price(out, [a])
+        rec("act", lambda: g.scalar.activation(ap(out), ap(a), f, bias=ap(bias), scale=ap(scale)), [a, bias, scale], [out], (k, c + more))
+
+    def mm(items):
+        def fn():
+            for (o, l, r, st, sp) in items:
+                last = g.tensor.matmul(ap(o), ap(l), ap(r), st, sp)
+            return last
+        rec("pe", fn, [x for it in items for x in it[1:3]], [it[0] for it in items],
+            ("pe", sum(max(64, size(it[2])) * (4 if width(it[1]) == 4 else 1) for it in items)))
+
+    def iota(out, pat, base, cm, small=True):
+        c = ("c", 160 + 2 * size(out))
+        if small:
+            rec("pool", lambda: g.iota(ap(out), pat, base, cm, allow_small_or_imprecise_dtypes=True), [], [out], c)
+        else:
+            rec("pool", lambda: g.iota(ap(out), pat, base, cm), [], [out], c)
+
+    def sel(out, a, pat, o, fill, base, cm):
+        rec("pool", lambda: g.affine_select(ap(out), ap(a), pat, o, fill, base, cm), [a], [out], ("c", 200 + 2 * size(out)))
+
+    def load(q, out, src):
+        eng = g.sync if q == "sp" else g.scalar
+        rec(q, lambda: eng.dma_start(ap(out), src), [], [out], ("dma", 128 * size(out) * width(out)), "dma")
+
+    def store(q, dst, a):
+        eng = g.sync if q == "sp" else g.scalar
+        rec(q, lambda: eng.dma_start(dst, ap(a)), [a], [], ("dma", 128 * size(a) * width(a)), "dma")
+
+    def move(out, a):
+        rec("sp", lambda: g.sync.dma_start(ap(out), ap(a)), [a], [out], ("dma", 128 * size(a) * width(a)), "dma")
+
+    def send(dst_rank, out, a, rsem):
+        dst = T.cores[dst_rank % n]
+        rid, pid, _ = topo.addr(dst)
+        m = topo.mask(core, dst)
+        rec("pool", lambda ls: g.remote_dma(ap(out), ap(a), T.sem[rsem], ls, pid, rid, m), [a], [],
+            ("dma", 128 * size(a) * width(a)), "remote", (rsem, len(topo.engines(core, dst))))
+
+    def arrives(src_rank, out, rsem):
+        rec("ext", None, [], [out], ("c", 0.0), "ext", (rsem, len(topo.engines(T.cores[src_rank % n], core))))
+
+    def cuts(sizes):
+        out, lo = [], 0
+        for z in sizes:
+            out.append((lo, lo + z))
+            lo += z
+        return out
+
+    def SEL(u, neg=False):
+        return V("seln" if neg else "sel", 15 - u, 143 - u)
+    T_LT, T_GE, T_LE, T_GT = (V("tri", 128 * i, 128 * i + 128) for i in range(4))
+    I_B, SH_B, I_N, SH_N = V("qb", 16, 144), V("qb", 0, 128), V("qn", 16, 144), V("qn", 0, 128)
+    F0, B0 = K, 2 * K
+
+    load("sp", V("prm0", 0, 3), T.obs[:])
+    load("sp", V("prm0", 3, 4), T.eps[:])
+    for nm, src in (("f16", T.f0), ("b16", T.b0)):
+        for lo in range(0, S, KN["ld"]):
+            load("act", V(nm, lo, lo + KN["ld"]), src[:, lo:lo + KN["ld"]])
+    load("sp", V("prm0", 4, 5), T.lam[:])
+    load("sp", V("prm0", 5, 6), T.rf[:])
+    load("sp", V("prm0", 6, 7), T.rb[:])
+    load("sp", V("pi32", 0, 256), T.pi[:])
+    load("sp", V("nz0", 0, S), T.nz[:])
+
+    ms(V("sel", 0, 144), 0.0)
+    ms(V("blk", 0, 128), 1.0)
+    ms(V("qn", 0, 144), 0.0)
+    sel(V("sel", 15, 143, 16), V("blk", 0, 8), [[-16, 8]], OP.is_ge, 0.0, 0, 1)
+    sel(V("sel", 15, 143, 16), V("sel", 15, 143, 16), [[16, 8]], OP.is_ge, 0.0, 15, -1)
+    sel(V("blk", 0, 128), V("blk", 0, 128), [[-16, 8], [0, 16]], OP.is_ge, 0.0, 0, 1)
+    sel(V("blk", 0, 128), V("blk", 0, 128), [[16, 8], [0, 16]], OP.is_ge, 0.0, 15, -1)
+    sel(T_LT, V("blk", 0, 128), [[1, 128]], OP.is_gt, 0.0, 0, -1)
+    sel(T_GE, V("blk", 0, 128), [[-1, 128]], OP.is_ge, 0.0, 0, 1)
+    sel(V("qn", 0, 144), V("qn", 0, 144), [[1, 144]], OP.not_equal, -1.0, -16, -1)
+    sel(V("qn", 0, 16), V("qn", 0, 16), [[1, 16]], OP.not_equal, -1.0, 112, -1)
+    for i in range(4):
+        ms(V("mk", S * i, S * i + S), 0.0)
+    ms(V("one", 0, 1031), 1.0)
+    ms(V("one", 1031, 1032), 2.0 ** -12)
+    ms(V("wbf", 0, 72), 128.0)
+    ms(V("wbb", 0, 72), 128.0)
+    ms(V("off", 0, 72), -2048.0)
+    ms(V("six", 0, S), 0.0625)
+    ts(V("qb", 0, 144), V("qn", 0, 144), -1.0, None, OP.mult)
+    if any(KN["miss"][t][h] for t in range(3) for h in range(2)):
+        ts(V("seln", 0, 144), V("sel", 0, 144), -1.0, None, OP.mult)
+    sel(T_LE, V("blk", 0, 128), [[1, 128]], OP.is_ge, 0.0, 0, -1)
+    sel(T_GT, V("blk", 0, 128), [[-1, 128]], OP.is_gt, 0.0, 0, 1)
+    iota(V("ri", 0, 1), [[0, 1]], 0, 1, small=False)
+    iota(V("cv", 0, 256), [[1, 16], [16, 16]], 0, 0)
+    iota(V("fb", 0, 128), [[K, 2], [64, 64]], K, 0)
+    iota(V("kd", 0, 17), [[1, 17]], K + 1, 0)
+    iota(V("even", 0, 1032), [[2, 1032]], 0, 0)
+    iota(V("zer", 0, 2048), [[0, 2048]], 0, 0)
+    move(V("cw", 0, 2048), V("zer", 0, 2048))
+    for i in range(8):
+        act(V("dw", 512 * i, 512 * i + 512), V("one", 0, 512), AF.Copy)
+    ts(V("prm0", 7, 8), V("prm0", 3, 4), -1.0, None, OP.mult, also=V("prm0", 4, 7))
+    cp(V("pu0", 0, 256), V("pi32", 0, 256))
+    send(rank - 1, V("nz1", 0, S), V("nz0", 0, S), "xz")
+    send(rank - 1, V("prm1", 0, 8), V("prm0", 0, 8), "xp")
+    send(rank - 1, V("pu1", 0, 256), V("pu0", 0, 256), "xl")
+    arrives(rank + 1, V("prm1", 0, 8), "xp")
+    arrives(rank + 1, V("nz1", 0, S), "xz")
+    arrives(rank + 1, V("pu1", 0, 256), "xl")
+    ms(V("mkw", 0, 8), 0.0)
+    ms(V("okw", 0, 8), 0.0)
+    ms(V("el", 0, 8), 0.0)
+    ms(V("rk", 256, 264), 0.0)
+    ms(V("emp", 16, 20), 1.0)
+    ms(V("cv", 256, 272), 1024.0)
+    ts(V("ri", 4, 5), V("ri", 0, 1), 15, None, OP.bitwise_and)
+    ts(V("rc", 0, 1), V("ri", 4, 5), 4.0, None, OP.mult)
+    ts(V("rc", 1, 2), V("ri", 4, 5), 17.0, None, OP.mult)
+    ts(V("rc", 2, 3), V("ri", 4, 5), 15.0, None, OP.is_lt)
+    ts(V("fb", 0, 128), V("fb", 0, 128), V("rc", 0, 1), None, OP.add)
+    ts(V("kd", 0, 17), V("kd", 0, 17), V("rc", 1, 2), None, OP.add)
+    ts(V("kd", 16, 17), V("kd", 16, 17), V("rc", 2, 3), None, OP.mult)
+
+    def who(t):
+        k = "1" if t == 1 else "0"
+        pr = "prm" + k
+        return {"y": V(pr, t, t + 1), "eps": V(pr, 3, 4), "lam": V(pr, 4, 5), "r": (V(pr, 5, 6), V(pr, 6, 7)),
+                "neps": V(pr, 7, 8), "nz": "nz" + k, "pu": "pu" + k}
+
+    def starts(t, h, pool, bk, bk2):
+        p, neg = who(t), KN["miss"][t][h]
+        for lo in range(0, S, KN["wc"]):
+            hi = lo + KN["wc"]
+            a, s, x = (V(nm, S * h + lo, S * h + hi) for nm in ("ab", "sg", "hit"))
+            act(a, V(pool, lo, hi), AF.Abs, p["y"], -1.0)
+            if neg:
+                act(s, a, AF.Sign, p["neps"], 1.0)
+                act(x, s, AF.Relu, 0.0, 0.25)
+            else:
+                ts(x, a, p["eps"], 0.25, OP.is_le, OP.mult)
+        mm([(P(bk, 0, 64), SEL(u, neg), V("hit", S * h + u, S * h + S, 16), u == 0, u == 15) for u in range(16)])
+        wb, o, sl = ("wbf", "wbb")[h], 512 * h, ("slf", "slb")[h]
+        C, CT, RHO = V("sm", o, o + 64), V("sm", o + 64, o + 65), V("sm", o + 72, o + 73)
+        E, Q, L = V("sm", o + 128, o + 192), V("sm", o + 192, o + 256), V("sm", o + 256, o + 320)
+        mm([(P(bk2, 0, 65), I_B, V("off", 0, 65), True, False)])
+        ts(V(wb, 1, 65), P(bk, 0, 64), 131.625 if neg else 127.625, 129.0, OP.add, OP.max)
+        mm([(P(bk2, 0, 65), T_LT, V(wb, 1, 66), False, False), (P(bk2, 0, 65), T_GE, V(wb, 0, 65), False, True)])
+        scan(V("sm", o, o + 65), P(bk2, 0, 65), V("one", 967, 1032), 0.0, OP.add, OP.mult)
+        rec("dve", lambda: g.vector.reciprocal(ap(RHO), ap(CT)), [CT], [RHO], ("c", 230.0))
+        ts(E, C, RHO, MAGIC, OP.mult, OP.add)
+        ts(Q, E, -MAGIC, CT, OP.add, OP.mult)
+        tt(L, Q, C, OP.is_lt)
+        tt(Q, E, L, OP.add)
+        ts(V(sl, 0, 64), Q, -MAGIC, None, OP.add)
+
+    def f_ancestors(pool):
+        cp((V("mk", 0, K), V("slf", 0, 64)), V("six", 0, S))
+        mm([(P(4, 0, 256), SEL(u), V("mk", u, K, 16), u == 0, u == 15) for u in range(16)])
+        act(V("mkw", 1, 257), P(4, 0, 256), AF.Copy)
+        mm([(P(5, 0, 256), T_LE, V("mkw", 1, 257), True, False), (P(5, 0, 256), T_GT, V("mkw", 0, 256), False, True)])
+        scan(V("aw", 0, 256), P(5, 0, 256), V("one", 0, 256), -1.0, OP.add, OP.mult)
+        cp(V("al", 0, 256), V("aw", 0, 256))
+        for lo, hi in cuts(KN["loop"]):
+            act(V("win", F0 + lo, F0 + hi), (V(pool, 0, S), V("al", lo // 16, hi // 16)), AF.Identity, 0.0, -1.0)
+
+    def b_ancestors(pool):
+        for lo, hi in cuts(KN["bs"]):
+            ts((V("dw", 0, K), V("slb", lo // 16, hi // 16)), V(pool, lo, hi), -1.0, 0.0, OP.mult, OP.add)
+        for lo, hi in cuts(KN["bn"]):
+            scan(V("win", B0 + lo, B0 + hi), V("dw", lo, hi), V("dw", lo, hi),
+                 V("win", B0 + lo - 1, B0 + lo) if lo else 0.0, OP.mult, OP.min)
+
+    def pairs(t):
+        p = who(t)
+        for i, (lo, hi) in enumerate(cuts(KN["loop"])):
+            z, o = hi - lo, 512 * (i % 4)
+            d, f, m, x = V("dd", lo, hi), V("win", F0 + lo, F0 + hi), V("win", lo, hi), V("miss", lo, hi)
+            a, s = V("ab", o, o + z), V("sg", o, o + z)
+            tt(d, (V("win", B0, B0 + K), V(p["pu"], lo // 16, hi // 16)), f, OP.subtract)
+            act(P(i % 4, 0, z), d, AF.Identity, 0.0, p["lam"])
+            tt(m, f, P(i % 4, 0, z), OP.add)
+            act(a, m, AF.Abs, p["y"], 1.0)
+            if i in KN["sign"][t]:
+                act(s, a, AF.Sign, p["neps"], 1.0)
+                ts(x, s, 0.0, None, OP.max)
+            else:
+                ts(x, a, p["eps"], None, OP.is_gt)
+            mm([(P(7, 0, 256), SEL(r), V("miss", 256 * r, 256 * r + 256), r == 0, r == 15) for r in range(lo // 256, hi // 256)])
+            mm([(P(6, lo // 16, hi // 16), SEL(u), V("miss", lo + u, hi, 16), u == 0, u == 15) for u in range(16)])
+        if t < 2:
+            for j in range(2):
+                move(V("mk", 2048 * j, 2048 * j + 2048), V("zer", 0, 2048))
+            for j in range(4):
+                move(V("dw", S * j, S * j + S), V("one", 0, S))
+
+    def places(t):
+        order = (KN["first"][t], 1 - KN["first"][t])
+        ts(V("okb", 0, 256), P(7, 0, 256), 7.5, None, OP.is_lt)
+        ops[-1]["mark"] = True
+        scan(V("el", 1, 257), V("okb", 0, 256), V("okb", 0, 256), 0.0, OP.add, OP.max)
+        mm([(P(4, 0, 1), T_LT, V("el", 256, 257), True, True)])
+        tt(V("emp", 0, 16), V("el", 0, 256, 16), V("el", 16, 257, 16), OP.is_equal)
+        tt(V("emp", 20, 37), V("emp", 0, 17), V("kd", 0, 17), OP.mult)
+        tt(V("emp", 40, 57), V("emp", 20, 37), V("el", 0, 257, 16), OP.add)
+        ts(V("pl", 0, 17), V("emp", 40, 57), P(4, 0, 1), None, OP.add)
+        cp((V("cw", 0, CWN), V("pl", 0, 17)), V("cv", 0, 272))
+        scan(V("cn", 0, 2048), V("cw", 0, 2048), V("cw", 0, 2048), 0.0, OP.max, OP.max)
+        if t < 2:
+            move(V("cw", 0, 2048), V("zer", 0, 2048))
+        ts(V("okw", 1, 257), P(6, 0, 256), 7.5, None, OP.is_lt)
+        mm([(P(5, 0, 256), T_LE, V("okw", 1, 257), True, False), (P(5, 0, 256), T_GT, V("okw", 0, 256), False, True)])
+        scan(V("rk", 0, 256), P(5, 0, 256), V("one", 0, 256), 0.0, OP.add, OP.mult)
+        for h in order:
+            for bk, stop in ((h, True), (2 + h, False)):
+                mm([(P(bk, 0, 64), SEL(u), V("cn", 2 * u + h, 2048, 32), u == 0, stop and u == 15) for u in range(16)])
+            ts(V("cl", 64 * h, 64 * h + 64), P(h, 0, 64), 0.0625, 256.0, OP.mult, OP.min)
+            for k, (lo, hi) in enumerate(cuts(KN["cmp"])):
+                gat = (V("rk", 0, 264), V("cl", 64 * h + lo // 16, 64 * h + hi // 16))
+                if h == order[1] and k in KN["cact"][t]:
+                    mm([(P(6, lo, hi), I_N, V("even", h + lo, h + hi), True, True)])
+                    act(V("tt", S * h + lo, S * h + hi), gat, AF.Identity, 0.0, -1.0)
+                    tt(V("cmp", S * h + lo, S * h + hi), V("tt", S * h + lo, S * h + hi), P(6, lo, hi), OP.is_gt if h else OP.is_ge)
+                else:
+                    tt(V("cmp", S * h + lo, S * h + hi), gat, V("even", h + lo, h + hi), OP.is_lt if h else OP.is_le)
+            mm([(P(2 + h, 0, 64), SEL(u), V("cmp", S * h + u, S * h + S, 16), False, u == 15) for u in range(16)])
+            tt(V("ix", 64 * h, 64 * h + 64), V("fb", 64 * h, 64 * h + 64), P(2 + h, 0, 64), OP.min)
+            cp(V("il", 64 * h, 64 * h + 64), V("ix", 64 * h, 64 * h + 64))
+
+    def step(t, h, dst, done):
+        p, z = who(t), KN["sc"]
+        bk = 0 if h == KN["first"][t] else 2
+        shift = h == 1 and t < 2
+        for lo in range(0, S, z):
+            hi = lo + z
+            gat = (V("win", 0, 3 * K), V("il", 64 * h + lo // 16, 64 * h + hi // 16))
+            hh, uu, tv = (V(nm, S * h + lo, S * h + hi) for nm in ("hh", "uu", "tt"))
+            act(hh, gat, AF.Square)
+            tt(uu, gat, hh, OP.add)
+            act(tv, uu, AF.Identity, 0.0, p["r"][h])
+            mm([(P(bk, lo, hi), SH_N if shift else I_N, tv, True, False),
+                (P(bk, lo, hi), SH_B if shift else I_B, V(p["nz"], lo, hi), False, True)])
+            if hi % 512 == 0:
+                ts(V(dst, hi - 512, hi), P(bk, hi - 512, hi), 0.0, 1.0, OP.max, OP.min)
+                done(hi - 512, hi)
+
+    def energy():
+        npe, z = KN["yepe"], KN["yes"]
+        for lo in range(0, S, 512):
+            for i in range(4):
+                v = V("dd", S * i + lo, S * i + lo + 512)
+                act(v, v, AF.Square)
+                act(P(4, lo, lo + 512) if i > npe else v, v, AF.Exp, 0.0, -1.0, 1500.0 if i + lo == 0 else 0.0)
+                if i < npe:
+                    w = z if i else 512
+                    for a in range(lo, lo + 512, w):
+                        mm([(P(6, a, a + w), I_N, V("dd", S * i + a, S * i + a + w), i == 0, i == npe - 1 and a + w == lo + 512)])
+                elif i == npe:
+                    tt(V("yo", lo, lo + 512), v, P(6, lo, lo + 512), OP.subtract)
+                else:
+                    tt(V("yo", lo, lo + 512), V("yo", lo, lo + 512), P(4, lo, lo + 512), OP.add)
+                if i == 3:
+                    store("sp", T.ye[:, lo:lo + 512], V("yo", lo, lo + 512))
+
+    def nothing(lo, hi):
+        return None
+
+    starts(0, 0, "f16", 2, 3)
+    starts(0, 1, "b16", 6, 7)
+    act(V("pb", 0, S), V("b16", 0, S), AF.Copy)
+    f_ancestors("f16")
+    b_ancestors("pb")
+    pairs(0)
+    places(0)
+
+    def b_goes(lo, hi):
+        send(rank - 2, V("lb", lo, hi), V("snd", lo, hi), "xb%d" % (lo // 512))
+        arrives(rank + 2, V("lb", lo, hi), "xb%d" % (lo // 512))
+    step(0, 1, "snd", b_goes)
+    step(0, 0, "pf", nothing)
+    starts(1, 0, "pf", 4, 5)
+    starts(1, 1, "lb", 6, 7)
+    f_ancestors("pf")
+    b_ancestors("lb")
+    pairs(1)
+    places(1)
+
+    def f_goes(lo, hi):
+        send(rank + 2, V("lf", lo, hi), V("snd", lo, hi), "xf%d" % (lo // 512))
+        arrives(rank - 2, V("lf", lo, hi), "xf%d" % (lo // 512))
+    step(1, 0, "snd", f_goes)
+    step(1, 1, "pb", nothing)
+    starts(2, 1, "pb", 4, 5)
+    starts(2, 0, "lf", 6, 7)
+    f_ancestors("lf")
+    b_ancestors("pb")
+    pairs(2)
+    places(2)
+    energy()
+    step(2, 0, "pf", lambda lo, hi: store("sp", T.yf[:, lo:hi], V("pf", lo, hi)))
+    step(2, 1, "pb", lambda lo, hi: store("sp", T.yb[:, lo:hi], V("pb", lo, hi)))
+
+    if "order" not in PLAN:
+        PLAN["deps"] = depends(ops)
+        PLAN["order"] = arrange(ops, PLAN["deps"], KN["seed"], KN["tries"])
+    emit(g, T, ops, PLAN["deps"], PLAN["order"])
+
+
+def depends(ops):
+    def hits(a, b):
+        return any(x[0] == y[0] and x[1] < y[2] and y[1] < x[2] for x in a for y in b)
+    deps = []
+    for i, o in enumerate(ops):
+        if o["kind"] == "ext":
+            deps.append([j for j in range(i) if ops[j]["kind"] == "remote" and ops[j]["sem"][0] == o["sem"][0]])
+            continue
+        bank = [x for x in o["r"] if x[0] == "ps"]
+        deps.append([j for j in range(i) if hits(o["r"], ops[j]["w"]) or hits(o["w"], ops[j]["w"]) or hits(o["w"], ops[j]["r"])
+                     or (ops[j]["q"] != o["q"] and hits(bank, ops[j]["r"]))])
+    return deps
+
+
+SPEEDS = ((1.56, 3.8, 2.4, 180e3, 0.06, 0.00042), (1.1, 2.0, 1.8, 250e3, 0.04, 0.00042), (2.0, 5.6, 3.2, 130e3, 0.10, 0.0006))
+
+
+def times(o, m):
+    k, c = o["cost"]
+    if k == "dma":
+        return (0.3 if o["kind"] == "remote" else 0.06), m[2] + c / m[3] + m[4], 0.05 + c / m[3]
+    t = 1.25 * {"c": c * 0.00083, "g": 0.055 + c * 0.00083 * m[0], "sc": 0.055 + c * 0.00083 * m[1], "pe": c * m[5]}[k]
+    return t, t + m[4], 0.0
+
+
+def arrange(ops, deps, seed, tries):
+    n = len(ops)
+    reach, near = [], []
+    for i in range(n):
+        r = 0
+        for j in deps[i]:
+            r |= reach[j]
+        near.append([j for j in deps[i] if not r >> j & 1])
+        for j in deps[i]:
+            r |= 1 << j
+        reach.append(r)
+    after = [[] for _ in range(n)]
+    for i in range(n):
+        for j in near[i]:
+            after[j].append(i)
+    q = [["dve", "act", "pe", "pool", "sp", "ext"].index(o["q"]) for o in ops]
+    tms = [[times(o, m) for o in ops] for m in SPEEDS]
+    tm = tms[0]
+    left, ready, free, order = [len(d) for d in near], [0.0] * n, [0.0] * 6, []
+    pool = [[i for i in range(n) if q[i] == k and not left[i]] for k in range(6)]
+    while len(order) < n:
+        best = None
+        for k in range(6):
+            if pool[k]:
+                t0 = max(free[k], min(ready[i] for i in pool[k]))
+                i = min(i for i in pool[k] if ready[i] <= t0 + 0.1)
+                t = max(free[k], ready[i])
+                if best is None or t < best[0]:
+                    best = (t, i)
+        t, i = best
+        pool[q[i]].remove(i)
+        order.append(i)
+        free[q[i]] = t + tm[i][0]
+        for j in after[i]:
+            ready[j] = max(ready[j], t + tm[i][1])
+            left[j] -= 1
+            if not left[j]:
+                pool[q[j]].append(j)
+
+    def span(part, tm, done, free, start):
+        free, total = list(free), 0.0
+        for i in part:
+            k = q[i]
+            t = free[k]
+            for j in near[i]:
+                if done[j] > t:
+                    t = done[j]
+            a, b, c = tm[i]
+            start[i] = t
+            free[k] = t + a
+            if c:
+                free[6] = done[i] = max(free[6] + c, t + b)
+            else:
+                done[i] = t + b
+            total += done[i]
+        end = done[part[-1]] if ops[part[-1]].get("mark") else max(free)
+        return end + 0.1 * total / len(part) + 0.5 * sum(max(0.0, f - end) for f in free[:3]), free, end
+
+    head = [i for i in range(n) if ops[i]["kind"] == "dma" and not near[i]]
+    order = [i for i in order if i not in head]
+    ends = [0] + [z + 1 for z, i in enumerate(order) if ops[i].get("mark")] + [len(order)]
+    start, dones = [0.0] * n, [[0.0] * n for _ in tms]
+    frees = [span(head, t, d, [0.0] * 7, start)[1] for t, d in zip(tms, dones)]
+    out = list(head)
+    for lo, hi in zip(ends, ends[1:]):
+        part = order[lo:hi]
+        m = len(part) - (1 if ops[part[-1]].get("mark") else 0)
+        now = [span(part, t, d, f, start)[0] for t, d, f in zip(tms, dones, frees)]
+        turns = tries * m // n
+        for k in range(turns):
+            seed = (seed * 1103515245 + 12345) % 2147483648
+            a = (seed >> 8) % m
+            i = part[a]
+            if q[i] == 5:
+                continue
+            seed = (seed * 1103515245 + 12345) % 2147483648
+            hops, b, block, rest = 1 + (seed >> 8) % 4, a, [i], []
+            up = seed >> 20 & 1
+            while hops and (0 < b if up else b < m - 1):
+                b += -1 if up else 1
+                j = part[b]
+                if (reach[i] >> j if up else reach[j] >> i) & 1:
+                    block.append(j)
+                else:
+                    rest.append(j)
+                    hops -= q[j] == q[i]
+            new = part[:b] + block[::-1] + rest[::-1] + part[a + 1:] if up else part[:a] + rest + block + part[b + 1:]
+            heat = KN["heat"] * (1.0 - k / turns)
+            if span(new, tm, dones[0], frees[0], start)[0] > now[0] + heat + 0.2:
+                continue
+            at = {j: z for z, j in enumerate(new)}
+            new = sorted(new[:m], key=lambda j: (start[j], at[j])) + new[m:]
+            c = [span(new, t, d, f, start)[0] for t, d, f in zip(tms, dones, frees)]
+            if c[0] + sum(c) <= now[0] + sum(now) + heat:
+                now, part = c, new
+        last = [span(part, t, d, f, start) for t, d, f in zip(tms, dones, frees)]
+        frees = [x[1] for x in last]
+        PLAN.setdefault("parts", []).append([round(x[2], 1) for x in last])
+        out += part
+    return out
+
+
+def emit(g, T, ops, deps, order):
+    queue = {"dve": g.vector, "act": g.scalar, "pe": g.tensor, "pool": g, "sp": g.sync}
+    known = {q: set() for q in queue}
+    issued = {q: [] for q in queue}
+    place = {i: k for k, i in enumerate(order)}
+    before, waits, needed = {}, {}, set()
+    for i in order:
+        o = ops[i]
+        before[i], waits[i] = set(), []
+        if o["kind"] == "ext":
+            continue
+        kn = known[o["q"]]
+        for j in sorted(deps[i], key=lambda k: -place[k]):
+            if j not in kn and not (o["q"] == "pe" and ops[j]["q"] == "pe"):
+                waits[i].append(j)
+                kn.add(j)
+                kn.update(before[j])
+        before[i] = set(kn)
+        if o["kind"] == "c":
+            before[i].update(issued[o["q"]])
+            issued[o["q"]].append(i)
+        needed.update(waits[i])
+    count = {q: 0 for q in queue}
+    token, dmas, ends = {}, 0, []
+    for i in order:
+        o = ops[i]
+        if o["kind"] == "ext":
+            token[i] = (T.sem[o["sem"][0]], o["sem"][1])
+            continue
+        q = queue[o["q"]]
+        for j in waits[i]:
+            q.wait_ge(*token[j])
+        if o["kind"] == "c":
+            ins = o["fn"]()
+            if i in needed:
+                count[o["q"]] += 1
+                ins.then_inc(T.sem[o["q"]], 1)
+                token[i] = (T.sem[o["q"]], count[o["q"]])
+            continue
+        s = T.sem["d%d" % dmas]
+        dmas += 1
+        if o["kind"] == "dma":
+            o["fn"]().then_inc(s, 16)
+            token[i] = (s, 16)
+        else:
+            o["fn"](s)
+            token[i] = (s, o["sem"][1])
+        if i not in needed:
+            ends.append(token[i])
+    for tk in ends:
+        g.sync.wait_ge(*tk)

@@ -8,10 +8,10 @@ KN = {
     "sign": ((0, 1, 2, 3, 4, 5, 6),) * 3,
     "sc": 256,
     "miss": ((0, 0), (0, 1), (0, 0)),
-    "first": (1, 0, 0),
-    "bs": (512, 256, 256), "bn": (2048, 2048), "cmp": (512, 512), "cact": ((0, 1), (0, 1), ()), "yepe": 2, "yes": 256,
-    "ld": 512, "wc": 512,
-    "seed": 1, "tries": 100000, "heat": 0.3,
+    "first": (0, 0, 0),
+    "bs": (512, 256, 256), "bn": (4096,), "cmp": (512, 512), "cact": ((1, 2, 3), (1, 2, 3), ()), "oka": (1, 1, 0), "yepe": 2, "yes": 256,
+    "ld": 512, "wc": 512, "fill": (), "macc": ((), (), ()),
+    "seed": 1, "tries": 150000, "heat": 0.3,
 }
 
 SCRATCH = {
@@ -167,6 +167,9 @@ def rank_program(g, core, T, topo):
     def move(out, a):
         rec("sp", lambda: g.sync.dma_start(ap(out), ap(a)), [a], [out], ("dma", 128 * size(a) * width(a)), "dma")
 
+    def adds(out, a):
+        rec("pool", lambda: g.dma_start(ap(out), ap(a), accum_op=OP.add), [a, out], [out], ("dma", 256 * size(a) * width(a)), "dma")
+
     def send(dst_rank, out, a, rsem):
         dst = T.cores[dst_rank % n]
         rid, pid, _ = topo.addr(dst)
@@ -230,8 +233,16 @@ def rank_program(g, core, T, topo):
     iota(V("fb", 0, 128), [[K, 2], [64, 64]], K, 0)
     iota(V("kd", 0, 17), [[1, 17]], K + 1, 0)
     iota(V("even", 0, 1032), [[2, 1032]], 0, 0)
-    iota(V("zer", 0, 2048), [[0, 2048]], 0, 0)
-    move(V("cw", 0, 2048), V("zer", 0, 2048))
+
+    def clear_cw():
+        if "cw" in KN["fill"]:
+            for j in range(2):
+                iota(V("cw", S * j, S * j + S), [[0, S]], 0, 0)
+        else:
+            move(V("cw", 0, 2048), V("zer", 0, 2048))
+    if "cw" not in KN["fill"] or "mk" not in KN["fill"]:
+        iota(V("zer", 0, 2048), [[0, 2048]], 0, 0)
+    clear_cw()
     for i in range(8):
         act(V("dw", 512 * i, 512 * i + 512), V("one", 0, 512), AF.Copy)
     ts(V("prm0", 7, 8), V("prm0", 3, 4), -1.0, None, OP.mult, also=V("prm0", 4, 7))
@@ -244,6 +255,7 @@ def rank_program(g, core, T, topo):
     arrives(rank + 1, V("pu1", 0, 256), "xl")
     ms(V("mkw", 0, 8), 0.0)
     ms(V("okw", 0, 8), 0.0)
+    ms(V("rc", 3, 4), 7.5)
     ms(V("el", 0, 8), 0.0)
     ms(V("rk", 256, 264), 0.0)
     ms(V("emp", 16, 20), 1.0)
@@ -312,8 +324,12 @@ def rank_program(g, core, T, topo):
             d, f, m, x = V("dd", lo, hi), V("win", F0 + lo, F0 + hi), V("win", lo, hi), V("miss", lo, hi)
             a, s = V("ab", o, o + z), V("sg", o, o + z)
             tt(d, (V("win", B0, B0 + K), V(p["pu"], lo // 16, hi // 16)), f, OP.subtract)
-            act(P(i % 4, 0, z), d, AF.Identity, 0.0, p["lam"])
-            tt(m, f, P(i % 4, 0, z), OP.add)
+            if i in KN["macc"][t]:
+                act(m, d, AF.Identity, 0.0, p["lam"])
+                adds(m, f)
+            else:
+                act(P(i % 4, 0, z), d, AF.Identity, 0.0, p["lam"])
+                tt(m, f, P(i % 4, 0, z), OP.add)
             act(a, m, AF.Abs, p["y"], 1.0)
             if i in KN["sign"][t]:
                 act(s, a, AF.Sign, p["neps"], 1.0)
@@ -323,15 +339,24 @@ def rank_program(g, core, T, topo):
             mm([(P(7, 0, 256), SEL(r), V("miss", 256 * r, 256 * r + 256), r == 0, r == 15) for r in range(lo // 256, hi // 256)])
             mm([(P(6, lo // 16, hi // 16), SEL(u), V("miss", lo + u, hi, 16), u == 0, u == 15) for u in range(16)])
         if t < 2:
-            for j in range(2):
-                move(V("mk", 2048 * j, 2048 * j + 2048), V("zer", 0, 2048))
             for j in range(4):
-                move(V("dw", S * j, S * j + S), V("one", 0, S))
+                if j % 2 == 0 and "mk" not in KN["fill"]:
+                    move(V("mk", S * j, S * j + 2048), V("zer", 0, 2048))
+                if "dw" not in KN["fill"] and not KN["macc"][t]:
+                    move(V("dw", S * j, S * j + S), V("one", 0, S))
+            for nm, c in (("mk", 0), ("dw", 1)):
+                if nm in KN["fill"]:
+                    for j in range(4):
+                        iota(V(nm, S * j, S * j + S), [[0, S]], c, 0)
 
     def places(t):
         order = (KN["first"][t], 1 - KN["first"][t])
         ts(V("okb", 0, 256), P(7, 0, 256), 7.5, None, OP.is_lt)
         ops[-1]["mark"] = True
+        if t < 2 and KN["macc"][t]:
+            for j in range(4):
+                move(V("dw", S * j, S * j + S), V("one", 0, S))
+                ops[-1]["r"].append(("okb", 0, 8))
         scan(V("el", 1, 257), V("okb", 0, 256), V("okb", 0, 256), 0.0, OP.add, OP.max)
         mm([(P(4, 0, 1), T_LT, V("el", 256, 257), True, True)])
         tt(V("emp", 0, 16), V("el", 0, 256, 16), V("el", 16, 257, 16), OP.is_equal)
@@ -341,8 +366,12 @@ def rank_program(g, core, T, topo):
         cp((V("cw", 0, CWN), V("pl", 0, 17)), V("cv", 0, 272))
         scan(V("cn", 0, 2048), V("cw", 0, 2048), V("cw", 0, 2048), 0.0, OP.max, OP.max)
         if t < 2:
-            move(V("cw", 0, 2048), V("zer", 0, 2048))
-        ts(V("okw", 1, 257), P(6, 0, 256), 7.5, None, OP.is_lt)
+            clear_cw()
+        if KN["oka"][t]:
+            act(V("sg", 0, 256), P(6, 0, 256), AF.Sign, V("rc", 3, 4), -1.0)
+            act(V("okw", 1, 257), V("sg", 0, 256), AF.Relu)
+        else:
+            ts(V("okw", 1, 257), P(6, 0, 256), 7.5, None, OP.is_lt)
         mm([(P(5, 0, 256), T_LE, V("okw", 1, 257), True, False), (P(5, 0, 256), T_GT, V("okw", 0, 256), False, True)])
         scan(V("rk", 0, 256), P(5, 0, 256), V("one", 0, 256), 0.0, OP.add, OP.mult)
         for h in order:
@@ -351,10 +380,12 @@ def rank_program(g, core, T, topo):
             ts(V("cl", 64 * h, 64 * h + 64), P(h, 0, 64), 0.0625, 256.0, OP.mult, OP.min)
             for k, (lo, hi) in enumerate(cuts(KN["cmp"])):
                 gat = (V("rk", 0, 264), V("cl", 64 * h + lo // 16, 64 * h + hi // 16))
-                if h == order[1] and k in KN["cact"][t]:
-                    mm([(P(6, lo, hi), I_N, V("even", h + lo, h + hi), True, True)])
+                k += 2 * order.index(h)
+                if k in KN["cact"][t]:
+                    nb = P((5, 4, 6, 7)[k], 0, hi - lo)
+                    mm([(nb, I_N, V("even", h + lo, h + hi), True, True)])
                     act(V("tt", S * h + lo, S * h + hi), gat, AF.Identity, 0.0, -1.0)
-                    tt(V("cmp", S * h + lo, S * h + hi), V("tt", S * h + lo, S * h + hi), P(6, lo, hi), OP.is_gt if h else OP.is_ge)
+                    tt(V("cmp", S * h + lo, S * h + hi), V("tt", S * h + lo, S * h + hi), nb, OP.is_gt if h else OP.is_ge)
                 else:
                     tt(V("cmp", S * h + lo, S * h + hi), gat, V("even", h + lo, h + hi), OP.is_lt if h else OP.is_le)
             mm([(P(2 + h, 0, 64), SEL(u), V("cmp", S * h + u, S * h + S, 16), False, u == 15) for u in range(16)])
@@ -454,13 +485,13 @@ def depends(ops):
     return deps
 
 
-SPEEDS = ((1.56, 3.8, 2.4, 180e3, 0.06, 0.00042), (1.1, 2.0, 1.8, 250e3, 0.04, 0.00042), (2.0, 5.6, 3.2, 130e3, 0.10, 0.0006))
+SPEEDS = ((1.56, 3.8, 2.4, 250e3, 0.2, 0.00045), (1.1, 2.0, 1.8, 300e3, 0.1, 0.00042), (2.0, 5.6, 3.0, 200e3, 0.25, 0.0006))
 
 
 def times(o, m):
     k, c = o["cost"]
     if k == "dma":
-        return (0.3 if o["kind"] == "remote" else 0.06), m[2] + c / m[3] + m[4], 0.05 + c / m[3]
+        return (0.3 if o["kind"] == "remote" else 1.0 if o["q"] == "pool" else 0.06), m[2] + c / m[3] + m[4], 0.05 + c / m[3]
     t = 1.25 * {"c": c * 0.00083, "g": 0.055 + c * 0.00083 * m[0], "sc": 0.055 + c * 0.00083 * m[1], "pe": c * m[5]}[k]
     return t, t + m[4], 0.0
 

@@ -3,15 +3,22 @@ from concourse.mybir import AluOpType as OP, ActivationFunctionType as AF
 S, K = 1024, 4096
 MAGIC = 12582912.0
 CWN = 8480
+F0, BA, BB, BC = K, 2 * K, 2 * K + S, 2 * K + 2 * S
 KN = {
     "loop": (512, 512, 512, 512, 512, 512, 512, 256, 256),
-    "sign": ((0, 1, 2, 3, 4, 5, 6),) * 3,
+    "cnt": (1024, 1024, 1024, 512, 256, 256),
+    "fl": (1024, 1024, 1024, 1024), "bl": (512, 512, 1024, 1024, 1024),
+    "fs": (1025, 1024, 2048), "bs": (2048, 2048),
+    "fx": "ppp",
+    "cmp": ("ddddddddd",) * 3,
+    "mul": ("aaaaaaaaa",) * 3, "add": ("ddddddddd",) * 3, "look": ("aadaadaa",) * 3, "fg": ("aaaaaaaaa",) * 3,
     "sc": 256,
-    "miss": ((0, 0), (0, 1), (0, 0)),
-    "first": (0, 0, 0),
-    "bs": (512, 256, 256), "bn": (4096,), "cmp": (512, 512), "cact": ((1, 2, 3), (1, 2, 3), ()), "oka": (1, 1, 0), "yepe": 2, "yes": 256,
-    "ld": 512, "wc": 512, "fill": (), "macc": ((), (), ()),
-    "seed": 1, "tries": 150000, "heat": 0.3,
+    "miss": ("dd", "dd", "dd"),
+    "first": (1, 0, 0),
+    "oka": (1, 1, 0), "yepe": 3, "yes": 256, "px": ("dda", "dda", "ddd"), "bx": "aaa", "clr": "s",
+    "pp": ((512, 512), (1024,)), "side": (1, 1), "fh": (1024, 1024, 2048), "bh": (1024, 1024, 2048),
+    "ld": 512, "wc": (512, 512),
+    "seed": 1, "tries": 100000, "heat": 0.1, "packs": 1500, "shake": 0.5, "reach": 10.0,
 }
 
 SCRATCH = {
@@ -20,40 +27,40 @@ SCRATCH = {
     "prm0": ("sbuf", [128, 8], "float32"), "prm1": ("sbuf", [128, 8], "float32"),
     "pi32": ("sbuf", [128, 256], "int32"),
     "pu0": ("sbuf", [128, 256], "uint16"), "pu1": ("sbuf", [128, 256], "uint16"),
-    "pf": ("sbuf", [128, S], "float32"), "pb": ("sbuf", [128, S], "float32"),
-    "snd": ("sbuf", [128, S], "float32"),
-    "lb": ("sbuf", [128, S], "float32"), "lf": ("sbuf", [128, S], "float32"),
-    "win": ("sbuf", [128, 3 * K], "float32"),
-    "dw": ("sbuf", [128, K], "float32"), "dd": ("sbuf", [128, K], "float32"),
+    "pf": ("sbuf", [128, S], "float32"), "snd": ("sbuf", [128, S], "float32"), "lf": ("sbuf", [128, S], "float32"),
+    "win": ("sbuf", [128, 2 * K + 3 * S], "float32"), "dd": ("sbuf", [128, K], "float32"),
     "ab": ("sbuf", [128, 2048], "float32"), "sg": ("sbuf", [128, 2048], "bfloat16"),
     "miss": ("sbuf", [128, K], "bfloat16"),
-    "mk": ("sbuf", [128, K], "bfloat16"), "cw": ("sbuf", [128, CWN], "bfloat16"),
-    "cn": ("sbuf", [128, 2048], "bfloat16"), "cmp": ("sbuf", [128, 2048], "bfloat16"),
+    "wf": ("sbuf", [128, K + 16], "bfloat16"), "wb": ("sbuf", [128, K + 16], "bfloat16"),
+    "sf": ("sbuf", [128, K + 16], "bfloat16"), "sb": ("sbuf", [128, K + 16], "bfloat16"),
+    "xf": ("sbuf", [128, K], "bfloat16"), "xl": ("sbuf", [128, K], "bfloat16"), "xb": ("sbuf", [128, S], "bfloat16"),
+    "cw": ("sbuf", [128, CWN], "bfloat16"), "cn": ("sbuf", [128, 2048], "bfloat16"), "cmp": ("sbuf", [128, 2048], "bfloat16"),
     "hit": ("sbuf", [128, 2048], "bfloat16"),
     "hh": ("sbuf", [128, 2048], "float32"), "uu": ("sbuf", [128, 2048], "float32"),
     "tt": ("sbuf", [128, 2048], "float32"), "yo": ("sbuf", [128, S], "float32"),
-    "wbf": ("sbuf", [128, 72], "bfloat16"), "wbb": ("sbuf", [128, 72], "bfloat16"),
-    "sm": ("sbuf", [128, 1024], "float32"),
-    "slf": ("sbuf", [128, 64], "uint16"), "slb": ("sbuf", [128, 64], "uint16"),
-    "mkw": ("sbuf", [128, 264], "bfloat16"), "okw": ("sbuf", [128, 264], "bfloat16"),
-    "okb": ("sbuf", [128, 256], "bfloat16"), "el": ("sbuf", [128, 264], "bfloat16"),
-    "aw": ("sbuf", [128, 256], "float32"), "al": ("sbuf", [128, 256], "uint16"),
-    "rk": ("sbuf", [128, 264], "float32"),
-    "emp": ("sbuf", [128, 64], "float32"), "pl": ("sbuf", [128, 18], "uint16"),
-    "cl": ("sbuf", [128, 128], "uint16"), "ix": ("sbuf", [128, 128], "float32"), "il": ("sbuf", [128, 128], "uint16"),
+    "wt": ("sbuf", [128, 144], "bfloat16"), "sm": ("sbuf", [128, 1024], "float32"),
+    "lb": ("sbuf", [128, 128], "bfloat16"), "sv": ("sbuf", [128, 128], "bfloat16"), "sl": ("sbuf", [128, 8], "uint16"),
+    "okw": ("sbuf", [128, 256], "bfloat16"), "okb": ("sbuf", [128, 256], "bfloat16"), "el": ("sbuf", [128, 264], "bfloat16"),
+    "al": ("sbuf", [128, 256], "uint16"), "jl": ("sbuf", [128, 256], "uint16"),
+    "al2": ("sbuf", [128, 256], "uint16"), "jl1": ("sbuf", [128, 256], "uint16"), "fb1": ("sbuf", [128, 128], "float32"),
+    "prm2": ("sbuf", [128, 8], "float32"), "prm3": ("sbuf", [128, 8], "float32"),
+    "emp": ("sbuf", [128, 64], "float32"), "pl": ("sbuf", [128, 18], "uint16"), "pv": ("sbuf", [128, 272], "bfloat16"),
+    "ix": ("sbuf", [128, 128], "float32"), "il": ("sbuf", [128, 128], "uint16"),
     "sel": ("sbuf", [128, 144], "bfloat16"), "seln": ("sbuf", [128, 144], "bfloat16"),
-    "blk": ("sbuf", [128, 128], "bfloat16"), "tri": ("sbuf", [128, 512], "bfloat16"),
-    "qn": ("sbuf", [128, 144], "float32"), "qb": ("sbuf", [128, 144], "bfloat16"),
-    "off": ("sbuf", [128, 72], "bfloat16"), "one": ("sbuf", [128, 1032], "float32"),
-    "zer": ("sbuf", [128, 2048], "bfloat16"), "six": ("sbuf", [128, S], "bfloat16"),
-    "even": ("sbuf", [128, 1032], "float32"), "fb": ("sbuf", [128, 128], "float32"),
-    "kd": ("sbuf", [128, 24], "float32"), "cv": ("sbuf", [128, 272], "bfloat16"),
-    "ri": ("sbuf", [128, 8], "int32"), "rc": ("sbuf", [128, 8], "float32"),
+    "sla": ("sbuf", [128, 144], "bfloat16"), "slb": ("sbuf", [128, 144], "bfloat16"),
+    "slc": ("sbuf", [128, 144], "bfloat16"), "sld": ("sbuf", [128, 160], "bfloat16"),
+    "blk": ("sbuf", [128, 128], "bfloat16"), "tri": ("sbuf", [128, 256], "bfloat16"),
+    "q": ("sbuf", [128, 144], "float32"), "qb": ("sbuf", [128, 144], "bfloat16"),
+    "top": ("sbuf", [128, 256], "float32"), "topb": ("sbuf", [128, 256], "bfloat16"),
+    "off": ("sbuf", [128, 72], "bfloat16"), "one": ("sbuf", [128, 72], "float32"),
+    "zer": ("sbuf", [128, 2048], "bfloat16"), "dec": ("sbuf", [128, 2064], "bfloat16"),
+    "kk": ("sbuf", [128, 128], "bfloat16"), "fb": ("sbuf", [128, 128], "float32"),
+    "kd": ("sbuf", [128, 24], "float32"), "cv": ("sbuf", [128, 256], "bfloat16"),
+    "ri": ("sbuf", [128, 8], "int32"), "rc": ("sbuf", [128, 16], "float32"),
     "ps": ("psum", [128, 4096], "float32"),
 }
-NDMA = 60
-SEMAPHORES = (["pe", "dve", "act", "pool", "xp", "xz", "xl"] + ["x%s%d" % (h, c) for h in "bf" for c in range(4)]
-              + ["d%d" % i for i in range(NDMA)])
+NDMA = 70
+SEMAPHORES = ["pe", "dve", "act", "pool"] + ["x%d" % i for i in range(30)] + ["d%d" % i for i in range(NDMA)]
 PLAN = {}
 
 
@@ -69,6 +76,9 @@ def rank_program(g, core, T, topo):
 
     def P(bank, lo, hi, step=1):
         return ("ps", 512 * bank + lo, 512 * bank + hi, step)
+
+    def W(pool, lo, hi):
+        return V(pool[0], pool[1] + lo, pool[1] + hi)
 
     def num(v):
         return isinstance(v, (int, float)) or v is None
@@ -157,7 +167,7 @@ def rank_program(g, core, T, topo):
         rec("pool", lambda: g.affine_select(ap(out), ap(a), pat, o, fill, base, cm), [a], [out], ("c", 200 + 2 * size(out)))
 
     def load(q, out, src):
-        eng = g.sync if q == "sp" else g.scalar
+        eng = {"sp": g.sync, "act": g.scalar, "pool": g}[q]
         rec(q, lambda: eng.dma_start(ap(out), src), [], [out], ("dma", 128 * size(out) * width(out)), "dma")
 
     def store(q, dst, a):
@@ -180,6 +190,14 @@ def rank_program(g, core, T, topo):
     def arrives(src_rank, out, rsem):
         rec("ext", None, [], [out], ("c", 0.0), "ext", (rsem, len(topo.engines(T.cores[src_rank % n], core))))
 
+    sent = [0]
+
+    def hand(by, out, a):
+        rsem = "x%d" % sent[0]
+        sent[0] += 1
+        send(rank + by, out, a, rsem)
+        arrives(rank - by, out, rsem)
+
     def cuts(sizes):
         out, lo = [], 0
         for z in sizes:
@@ -187,15 +205,25 @@ def rank_program(g, core, T, topo):
             lo += z
         return out
 
-    def SEL(u, neg=False):
-        return V("seln" if neg else "sel", 15 - u, 143 - u)
-    T_LT, T_GE, T_LE, T_GT = (V("tri", 128 * i, 128 * i + 128) for i in range(4))
-    I_B, SH_B, I_N, SH_N = V("qb", 16, 144), V("qb", 0, 128), V("qn", 16, 144), V("qn", 0, 128)
-    F0, B0 = K, 2 * K
+    def SEL(u, name="sel"):
+        return V(name, 15 - u, 143 - u)
+
+    def rows(out, name, lo, hi, step=16):
+        mm([(out, SEL(u), V(name, lo + u * step // 16, hi, step), u == 0, u == 15) for u in range(16)])
+
+    def cut(eng, out, a):
+        if eng == "a":
+            act(out, a, AF.Relu, 0.0, SCL)
+        else:
+            ts(out, a, SCL, 0.0, OP.mult, OP.max)
+
+    T_LT, T_GE = V("tri", 0, 128), V("tri", 128, 256)
+    I_B, SH_B, I_F, SH_F = V("qb", 16, 144), V("qb", 0, 128), V("q", 16, 144), V("q", 0, 128)
+    ROW, IS0, DEC, SCL = (V("rc", i, i + 1) for i in (4, 5, 6, 7))
 
     load("sp", V("prm0", 0, 3), T.obs[:])
     load("sp", V("prm0", 3, 4), T.eps[:])
-    for nm, src in (("f16", T.f0), ("b16", T.b0)):
+    for nm, src in (("b16", T.b0), ("f16", T.f0)):
         for lo in range(0, S, KN["ld"]):
             load("act", V(nm, lo, lo + KN["ld"]), src[:, lo:lo + KN["ld"]])
     load("sp", V("prm0", 4, 5), T.lam[:])
@@ -206,65 +234,74 @@ def rank_program(g, core, T, topo):
 
     ms(V("sel", 0, 144), 0.0)
     ms(V("blk", 0, 128), 1.0)
-    ms(V("qn", 0, 144), 0.0)
+    ms(V("q", 0, 144), 0.0)
+    iota(V("ri", 0, 1), [[0, 1]], 0, 1, small=False)
     sel(V("sel", 15, 143, 16), V("blk", 0, 8), [[-16, 8]], OP.is_ge, 0.0, 0, 1)
     sel(V("sel", 15, 143, 16), V("sel", 15, 143, 16), [[16, 8]], OP.is_ge, 0.0, 15, -1)
+    sel(V("topb", 0, 128), V("blk", 0, 128), [[-16, 8], [0, 16]], OP.is_equal, 0.0, 0, 1)
     sel(V("blk", 0, 128), V("blk", 0, 128), [[-16, 8], [0, 16]], OP.is_ge, 0.0, 0, 1)
     sel(V("blk", 0, 128), V("blk", 0, 128), [[16, 8], [0, 16]], OP.is_ge, 0.0, 15, -1)
     sel(T_LT, V("blk", 0, 128), [[1, 128]], OP.is_gt, 0.0, 0, -1)
     sel(T_GE, V("blk", 0, 128), [[-1, 128]], OP.is_ge, 0.0, 0, 1)
-    sel(V("qn", 0, 144), V("qn", 0, 144), [[1, 144]], OP.not_equal, -1.0, -16, -1)
-    sel(V("qn", 0, 16), V("qn", 0, 16), [[1, 16]], OP.not_equal, -1.0, 112, -1)
-    for i in range(4):
-        ms(V("mk", S * i, S * i + S), 0.0)
-    ms(V("one", 0, 1031), 1.0)
-    ms(V("one", 1031, 1032), 2.0 ** -12)
-    ms(V("wbf", 0, 72), 128.0)
-    ms(V("wbb", 0, 72), 128.0)
-    ms(V("off", 0, 72), -2048.0)
-    ms(V("six", 0, S), 0.0625)
-    ts(V("qb", 0, 144), V("qn", 0, 144), -1.0, None, OP.mult)
-    if any(KN["miss"][t][h] for t in range(3) for h in range(2)):
-        ts(V("seln", 0, 144), V("sel", 0, 144), -1.0, None, OP.mult)
-    sel(T_LE, V("blk", 0, 128), [[1, 128]], OP.is_ge, 0.0, 0, -1)
-    sel(T_GT, V("blk", 0, 128), [[-1, 128]], OP.is_gt, 0.0, 0, 1)
-    iota(V("ri", 0, 1), [[0, 1]], 0, 1, small=False)
+    sel(V("q", 0, 144), V("q", 0, 144), [[1, 144]], OP.not_equal, 1.0, -16, -1)
+    sel(V("q", 0, 16), V("q", 0, 16), [[1, 16]], OP.not_equal, 1.0, 112, -1)
+    iota(V("kk", 0, 128), [[0, 2], [0, 4], [1, 16]], 0, 0)
+    iota(V("kk", 64, 128), [[1, 64]], 0, 0)
     iota(V("cv", 0, 256), [[1, 16], [16, 16]], 0, 0)
-    iota(V("fb", 0, 128), [[K, 2], [64, 64]], K, 0)
+    iota(V("fb", 0, 64), [[64, 64]], K, 0)
     iota(V("kd", 0, 17), [[1, 17]], K + 1, 0)
-    iota(V("even", 0, 1032), [[2, 1032]], 0, 0)
-
-    def clear_cw():
-        if "cw" in KN["fill"]:
-            for j in range(2):
-                iota(V("cw", S * j, S * j + S), [[0, S]], 0, 0)
-        else:
-            move(V("cw", 0, 2048), V("zer", 0, 2048))
-    if "cw" not in KN["fill"] or "mk" not in KN["fill"]:
-        iota(V("zer", 0, 2048), [[0, 2048]], 0, 0)
-    clear_cw()
-    for i in range(8):
-        act(V("dw", 512 * i, 512 * i + 512), V("one", 0, 512), AF.Copy)
+    load("pool", V("win", BA, BA + S), T.b0[:])
+    for lo in range(0, 2048, 1024):
+        ms(V("zer", lo, lo + 1024), 0.0)
+    for nm in ("wb", "wf"):
+        move(V(nm, 0, 2048), V("zer", 0, 2048))
+        for lo, hi in ((2048, 3072), (3072, K + 16)):
+            ms(V(nm, lo, hi), 0.0)
+    move(V("cw", 0, 2048), V("zer", 0, 2048))
+    ms(V("one", 0, 64), 1.0)
+    ms(V("one", 64, 65), 2.0 ** -12)
+    ms(V("wt", 0, 144), 128.0)
+    ms(V("off", 0, 72), -2048.0)
+    cp(V("qb", 0, 144), V("q", 0, 144))
+    cp(V("top", 0, 128), V("topb", 0, 128))
+    tt(V("top", 128, 256), I_F, V("top", 0, 128), OP.subtract)
+    cp(V("topb", 128, 256), V("top", 128, 256))
+    if "a" in "".join(KN["miss"]):
+        ts(V("seln", 0, 144), V("sel", 0, 144), -1.0, None, OP.mult)
+    ts(V("ri", 4, 5), V("ri", 0, 1), 15, None, OP.bitwise_and)
+    cp(ROW, V("ri", 4, 5))
+    ts(IS0, ROW, 0.0, None, OP.is_equal)
+    ts(DEC, IS0, -1.0, None, OP.add)
+    ts(SCL, IS0, 17.0, -1.0, OP.mult, OP.add)
+    for lo, hi in ((0, 1024), (1024, 2048), (2048, 2064)):
+        ts(V("dec", lo, hi), V("zer", 0, hi - lo), DEC, None, OP.add)
+    ts(V("kk", 0, 64), V("kk", 0, 64), ROW, -8192.0, OP.not_equal, OP.mult)
+    ts(V("kk", 64, 128), V("kk", 64, 128), IS0, None, OP.mult)
+    if "p" in KN["fx"]:
+        ts(V("slb", 0, 144), V("sel", 0, 144), SCL, None, OP.mult)
+        ts(V("slc", 0, 144), V("sel", 0, 144), DEC, None, OP.mult)
+        ms(V("sld", 144, 160), 0.0)
+        ts(V("sld", 0, 144), V("slc", 0, 144), -1.0, None, OP.mult)
+        tt(V("sla", 0, 144), V("slb", 0, 144), V("sld", 1, 145), OP.add)
     ts(V("prm0", 7, 8), V("prm0", 3, 4), -1.0, None, OP.mult, also=V("prm0", 4, 7))
     cp(V("pu0", 0, 256), V("pi32", 0, 256))
-    send(rank - 1, V("nz1", 0, S), V("nz0", 0, S), "xz")
-    send(rank - 1, V("prm1", 0, 8), V("prm0", 0, 8), "xp")
-    send(rank - 1, V("pu1", 0, 256), V("pu0", 0, 256), "xl")
-    arrives(rank + 1, V("prm1", 0, 8), "xp")
-    arrives(rank + 1, V("nz1", 0, S), "xz")
-    arrives(rank + 1, V("pu1", 0, 256), "xl")
-    ms(V("mkw", 0, 8), 0.0)
-    ms(V("okw", 0, 8), 0.0)
+    hand(-1, V("nz1", 0, S), V("nz0", 0, S))
+    hand(-1, V("prm1", 0, 8), V("prm0", 0, 8))
+    hand(1 if KN["side"][0] else -1, V("pu1", 0, 256), V("pu0", 0, 256))
+    if KN["side"][0]:
+        hand(1, V("prm2", 0, 8), V("prm0", 0, 8))
+    if KN["side"][1]:
+        hand(2, V("prm3", 0, 8), V("prm0", 0, 8))
     ms(V("rc", 3, 4), 7.5)
     ms(V("el", 0, 8), 0.0)
-    ms(V("rk", 256, 264), 0.0)
     ms(V("emp", 16, 20), 1.0)
-    ms(V("cv", 256, 272), 1024.0)
-    ts(V("ri", 4, 5), V("ri", 0, 1), 15, None, OP.bitwise_and)
-    ts(V("rc", 0, 1), V("ri", 4, 5), 4.0, None, OP.mult)
-    ts(V("rc", 1, 2), V("ri", 4, 5), 17.0, None, OP.mult)
-    ts(V("rc", 2, 3), V("ri", 4, 5), 15.0, None, OP.is_lt)
-    ts(V("fb", 0, 128), V("fb", 0, 128), V("rc", 0, 1), None, OP.add)
+    ts(V("rc", 0, 1), ROW, 4.0, None, OP.mult)
+    ts(V("rc", 1, 2), ROW, 17.0, None, OP.mult)
+    ts(V("rc", 2, 3), ROW, 15.0, None, OP.is_lt)
+    ts(V("rc", 8, 9), IS0, 1024.0, None, OP.mult)
+    ts(V("pv", 256, 272), V("zer", 0, 16), V("rc", 8, 9), None, OP.add)
+    ts(V("cv", 0, 256), V("cv", 0, 256), IS0, None, OP.mult)
+    ts(V("fb", 0, 64), V("fb", 0, 64), V("rc", 0, 1), None, OP.add)
     ts(V("kd", 0, 17), V("kd", 0, 17), V("rc", 1, 2), None, OP.add)
     ts(V("kd", 16, 17), V("kd", 16, 17), V("rc", 2, 3), None, OP.mult)
 
@@ -274,139 +311,176 @@ def rank_program(g, core, T, topo):
         return {"y": V(pr, t, t + 1), "eps": V(pr, 3, 4), "lam": V(pr, 4, 5), "r": (V(pr, 5, 6), V(pr, 6, 7)),
                 "neps": V(pr, 7, 8), "nz": "nz" + k, "pu": "pu" + k}
 
+    def far(t, h):
+        return t + h == 2 and t > 0 and h == 2 - t and KN["side"][t - 1]
+
     def starts(t, h, pool, bk, bk2):
-        p, neg = who(t), KN["miss"][t][h]
-        for lo in range(0, S, KN["wc"]):
-            hi = lo + KN["wc"]
+        p, how = who(t), KN["miss"][t][h]
+        if far(t, h):
+            pr = "prm%d" % (t + 1)
+            p = {"y": V(pr, t, t + 1), "eps": V(pr, 3, 4), "neps": V(pr, 7, 8)}
+        for lo, hi in cuts(KN["wc"]):
             a, s, x = (V(nm, S * h + lo, S * h + hi) for nm in ("ab", "sg", "hit"))
-            act(a, V(pool, lo, hi), AF.Abs, p["y"], -1.0)
-            if neg:
-                act(s, a, AF.Sign, p["neps"], 1.0)
-                act(x, s, AF.Relu, 0.0, 0.25)
-            else:
+            act(a, W(pool, lo, hi), AF.Abs, p["y"], -1.0)
+            if how == "d":
                 ts(x, a, p["eps"], 0.25, OP.is_le, OP.mult)
-        mm([(P(bk, 0, 64), SEL(u, neg), V("hit", S * h + u, S * h + S, 16), u == 0, u == 15) for u in range(16)])
-        wb, o, sl = ("wbf", "wbb")[h], 512 * h, ("slf", "slb")[h]
+            else:
+                act(s, a, AF.Sign, p["neps"], 1.0)
+                if how == "a":
+                    act(x, s, AF.Relu, 0.0, 0.25)
+                else:
+                    ts(x, s, 0.5, 0.25, OP.is_lt, OP.mult)
+        neg = how == "a"
+        mm([(P(bk, 0, 64), SEL(u, "seln" if neg else "sel"), V("hit", S * h + u, S * h + S, 16), u == 0, u == 15) for u in range(16)])
+        o, w, c = 512 * h, 72 * h, 64 * h
         C, CT, RHO = V("sm", o, o + 64), V("sm", o + 64, o + 65), V("sm", o + 72, o + 73)
-        E, Q, L = V("sm", o + 128, o + 192), V("sm", o + 192, o + 256), V("sm", o + 256, o + 320)
+        E, Q, E0, M = (V("sm", o + z, o + z + 64) for z in (128, 192, 256, 320))
+        L, vals, sl = V("lb", c, c + 64), V("sv", c, c + 64), V("sl", 4 * h, 4 * h + 4)
         mm([(P(bk2, 0, 65), I_B, V("off", 0, 65), True, False)])
-        ts(V(wb, 1, 65), P(bk, 0, 64), 131.625 if neg else 127.625, 129.0, OP.add, OP.max)
-        mm([(P(bk2, 0, 65), T_LT, V(wb, 1, 66), False, False), (P(bk2, 0, 65), T_GE, V(wb, 0, 65), False, True)])
-        scan(V("sm", o, o + 65), P(bk2, 0, 65), V("one", 967, 1032), 0.0, OP.add, OP.mult)
+        ts(V("wt", w + 1, w + 65), P(bk, 0, 64), 131.625 if neg else 127.625, 129.0, OP.add, OP.max)
+        mm([(P(bk2, 0, 65), T_LT, V("wt", w + 1, w + 66), False, False), (P(bk2, 0, 65), T_GE, V("wt", w, w + 65), False, True)])
+        scan(V("sm", o, o + 65), P(bk2, 0, 65), V("one", 0, 65), 0.0, OP.add, OP.mult)
         rec("dve", lambda: g.vector.reciprocal(ap(RHO), ap(CT)), [CT], [RHO], ("c", 230.0))
         ts(E, C, RHO, MAGIC, OP.mult, OP.add)
         ts(Q, E, -MAGIC, CT, OP.add, OP.mult)
+        ts(E0, E, -MAGIC, None, OP.add)
         tt(L, Q, C, OP.is_lt)
-        tt(Q, E, L, OP.add)
-        ts(V(sl, 0, 64), Q, -MAGIC, None, OP.add)
+        for out, z in ((P(bk2, 128, 192), 0), (P(bk, 128, 192), 1)):
+            mm([(out, V("top", 128 * z, 128 * z + 128), E0, True, False), (out, I_B, V("kk", 64 * z, 64 * z + 64), False, False)])
+            mm([(out, V("topb", 128 * z, 128 * z + 128), L, False, True)])
+        scan(M, P(bk2, 128, 192), V("zer", 0, 64), 0.0, OP.max, OP.add)
+        cp(sl, V("sm", o + 335, o + 384, 16))
+        act(vals, P(bk, 128, 192), AF.Copy)
+        wn, sn = ("wf", "wb")[h], ("sf", "sb")[h]
+        cp((V(wn, 0, K), sl), vals)
+        for lo, hi in cuts(KN["bs" if h else "fs"]):
+            scan(V(sn, lo, hi), V(wn, lo, hi), V("dec", 0, hi - lo), V(sn, lo - 1, lo) if lo else -1.0, OP.max, OP.add)
 
-    def f_ancestors(pool):
-        cp((V("mk", 0, K), V("slf", 0, 64)), V("six", 0, S))
-        mm([(P(4, 0, 256), SEL(u), V("mk", u, K, 16), u == 0, u == 15) for u in range(16)])
-        act(V("mkw", 1, 257), P(4, 0, 256), AF.Copy)
-        mm([(P(5, 0, 256), T_LE, V("mkw", 1, 257), True, False), (P(5, 0, 256), T_GT, V("mkw", 0, 256), False, True)])
-        scan(V("aw", 0, 256), P(5, 0, 256), V("one", 0, 256), -1.0, OP.add, OP.mult)
-        cp(V("al", 0, 256), V("aw", 0, 256))
-        for lo, hi in cuts(KN["loop"]):
-            act(V("win", F0 + lo, F0 + hi), (V(pool, 0, S), V("al", lo // 16, hi // 16)), AF.Identity, 0.0, -1.0)
+    def clear(t, h):
+        if t < 2:
+            wn = ("wf", "wb")[h]
+            if KN["clr"] == "s":
+                cp((V(wn, 0, K), V("sl", 4 * h, 4 * h + 4)), V("zer", 0, 64))
+            else:
+                for lo in (0, 2048):
+                    move(V(wn, lo, lo + 2048), V("zer", 0, 2048))
 
-    def b_ancestors(pool):
-        for lo, hi in cuts(KN["bs"]):
-            ts((V("dw", 0, K), V("slb", lo // 16, hi // 16)), V(pool, lo, hi), -1.0, 0.0, OP.mult, OP.add)
-        for lo, hi in cuts(KN["bn"]):
-            scan(V("win", B0 + lo, B0 + hi), V("dw", lo, hi), V("dw", lo, hi),
-                 V("win", B0 + lo - 1, B0 + lo) if lo else 0.0, OP.mult, OP.min)
+    def f_ancestors(t, pool):
+        how = KN["fx"][t]
+        for lo, hi in cuts(KN["fl"]):
+            out = P(4, lo // 16, hi // 16)
+            if how == "p":
+                mm([(out, SEL(u, "sla" if u else "slb"), V("sf", lo + u, hi, 16), u == 0, False) for u in range(16)]
+                   + [(out, SEL(15, "sld"), V("sf", lo + 16, hi + 1, 16), False, False)]
+                   + [(out, SEL(u, "slc"), V("wf", lo + u + 1, hi + 1, 16), False, u == 15) for u in range(16)])
+                ts(V("al", lo // 16, hi // 16), out, 15.0, None, OP.add)
+            else:
+                cut(how, V("xf", lo, hi), V("sf", lo, hi))
+                rows(out, "xf", lo, hi)
+                cp(V("al", lo // 16, hi // 16), out)
+        if far(t, 0):
+            for lo, hi in cuts(KN["fh"]):
+                hand(2, V("al2", lo // 16, hi // 16), V("al", lo // 16, hi // 16))
+        clear(t, 0)
+        for i, (lo, hi) in enumerate(cuts(KN["loop"])):
+            gat = (W(pool, 0, S), V("al2" if far(t, 0) else "al", lo // 16, hi // 16))
+            if KN["fg"][t][i] == "a":
+                act(V("win", F0 + lo, F0 + hi), gat, AF.Copy)
+            else:
+                cp(V("win", F0 + lo, F0 + hi), gat)
 
-    def pairs(t):
+    def b_ancestors(t, base):
         p = who(t)
+        clear(t, 1)
+        for lo, hi in cuts(KN["bl"]):
+            for z in range(lo, hi, 512):
+                cut(KN["look"][t][z // 512], V("xl", z, z + 512), (V("sb", 0, K), V(p["pu"], z // 16, z // 16 + 32)))
+            rows(P(5, lo // 16, hi // 16), "xl", lo, hi)
+            cp(V("jl", lo // 16, hi // 16), P(5, lo // 16, hi // 16))
+        cut(KN["bx"][t], V("xb", 0, S), V("sb", 0, K, 4))
+        rows(P(5, 256, 320), "xb", 0, S)
+        ts(V("fb", 64, 128), P(5, 256, 320), float(base), None, OP.add)
+        if far(t, 1):
+            for lo, hi in cuts(KN["bh"]):
+                hand(-2, V("jl1", lo // 16, hi // 16), V("jl", lo // 16, hi // 16))
+            hand(-2, V("fb1", 64, 128), V("fb", 64, 128))
+
+    def pairs(t, pool):
+        p = who(t)
+        ends = {hi: lo for lo, hi in cuts(KN["cnt"])}
         for i, (lo, hi) in enumerate(cuts(KN["loop"])):
             z, o = hi - lo, 512 * (i % 4)
             d, f, m, x = V("dd", lo, hi), V("win", F0 + lo, F0 + hi), V("win", lo, hi), V("miss", lo, hi)
             a, s = V("ab", o, o + z), V("sg", o, o + z)
-            tt(d, (V("win", B0, B0 + K), V(p["pu"], lo // 16, hi // 16)), f, OP.subtract)
-            if i in KN["macc"][t]:
-                act(m, d, AF.Identity, 0.0, p["lam"])
-                adds(m, f)
+            tt(d, (W(pool, 0, S), V("jl1" if far(t, 1) else "jl", lo // 16, hi // 16)), f, OP.subtract)
+            prod = P(i % 4, 0, z) if KN["add"][t][i] == "d" else m
+            if KN["mul"][t][i] == "a":
+                act(prod, d, AF.Identity, 0.0, p["lam"])
             else:
-                act(P(i % 4, 0, z), d, AF.Identity, 0.0, p["lam"])
-                tt(m, f, P(i % 4, 0, z), OP.add)
-            act(a, m, AF.Abs, p["y"], 1.0)
-            if i in KN["sign"][t]:
+                ts(prod, d, p["lam"], None, OP.mult)
+            if KN["add"][t][i] == "d":
+                tt(m, f, prod, OP.add)
+            else:
+                adds(m, f)
+            act(a, m, AF.Abs, p["y"], -1.0)
+            if KN["cmp"][t][i] == "s":
                 act(s, a, AF.Sign, p["neps"], 1.0)
                 ts(x, s, 0.0, None, OP.max)
             else:
                 ts(x, a, p["eps"], None, OP.is_gt)
             mm([(P(7, 0, 256), SEL(r), V("miss", 256 * r, 256 * r + 256), r == 0, r == 15) for r in range(lo // 256, hi // 256)])
-            mm([(P(6, lo // 16, hi // 16), SEL(u), V("miss", lo + u, hi, 16), u == 0, u == 15) for u in range(16)])
-        if t < 2:
-            for j in range(4):
-                if j % 2 == 0 and "mk" not in KN["fill"]:
-                    move(V("mk", S * j, S * j + 2048), V("zer", 0, 2048))
-                if "dw" not in KN["fill"] and not KN["macc"][t]:
-                    move(V("dw", S * j, S * j + S), V("one", 0, S))
-            for nm, c in (("mk", 0), ("dw", 1)):
-                if nm in KN["fill"]:
-                    for j in range(4):
-                        iota(V(nm, S * j, S * j + S), [[0, S]], c, 0)
+            if hi in ends:
+                rows(P(6, ends[hi] // 16, hi // 16), "miss", ends[hi], hi)
 
     def places(t):
         order = (KN["first"][t], 1 - KN["first"][t])
         ts(V("okb", 0, 256), P(7, 0, 256), 7.5, None, OP.is_lt)
         ops[-1]["mark"] = True
-        if t < 2 and KN["macc"][t]:
-            for j in range(4):
-                move(V("dw", S * j, S * j + S), V("one", 0, S))
-                ops[-1]["r"].append(("okb", 0, 8))
         scan(V("el", 1, 257), V("okb", 0, 256), V("okb", 0, 256), 0.0, OP.add, OP.max)
         mm([(P(4, 0, 1), T_LT, V("el", 256, 257), True, True)])
         tt(V("emp", 0, 16), V("el", 0, 256, 16), V("el", 16, 257, 16), OP.is_equal)
         tt(V("emp", 20, 37), V("emp", 0, 17), V("kd", 0, 17), OP.mult)
         tt(V("emp", 40, 57), V("emp", 20, 37), V("el", 0, 257, 16), OP.add)
         ts(V("pl", 0, 17), V("emp", 40, 57), P(4, 0, 1), None, OP.add)
-        cp((V("cw", 0, CWN), V("pl", 0, 17)), V("cv", 0, 272))
-        scan(V("cn", 0, 2048), V("cw", 0, 2048), V("cw", 0, 2048), 0.0, OP.max, OP.max)
-        if t < 2:
-            clear_cw()
         if KN["oka"][t]:
             act(V("sg", 0, 256), P(6, 0, 256), AF.Sign, V("rc", 3, 4), -1.0)
-            act(V("okw", 1, 257), V("sg", 0, 256), AF.Relu)
+            act(V("okw", 0, 256), V("sg", 0, 256), AF.Relu)
         else:
-            ts(V("okw", 1, 257), P(6, 0, 256), 7.5, None, OP.is_lt)
-        mm([(P(5, 0, 256), T_LE, V("okw", 1, 257), True, False), (P(5, 0, 256), T_GT, V("okw", 0, 256), False, True)])
-        scan(V("rk", 0, 256), P(5, 0, 256), V("one", 0, 256), 0.0, OP.add, OP.mult)
-        for h in order:
-            for bk, stop in ((h, True), (2 + h, False)):
-                mm([(P(bk, 0, 64), SEL(u), V("cn", 2 * u + h, 2048, 32), u == 0, stop and u == 15) for u in range(16)])
-            ts(V("cl", 64 * h, 64 * h + 64), P(h, 0, 64), 0.0625, 256.0, OP.mult, OP.min)
-            for k, (lo, hi) in enumerate(cuts(KN["cmp"])):
-                gat = (V("rk", 0, 264), V("cl", 64 * h + lo // 16, 64 * h + hi // 16))
-                k += 2 * order.index(h)
-                if k in KN["cact"][t]:
-                    nb = P((5, 4, 6, 7)[k], 0, hi - lo)
-                    mm([(nb, I_N, V("even", h + lo, h + hi), True, True)])
-                    act(V("tt", S * h + lo, S * h + hi), gat, AF.Identity, 0.0, -1.0)
-                    tt(V("cmp", S * h + lo, S * h + hi), V("tt", S * h + lo, S * h + hi), nb, OP.is_gt if h else OP.is_ge)
-                else:
-                    tt(V("cmp", S * h + lo, S * h + hi), gat, V("even", h + lo, h + hi), OP.is_lt if h else OP.is_le)
-            mm([(P(2 + h, 0, 64), SEL(u), V("cmp", S * h + u, S * h + S, 16), False, u == 15) for u in range(16)])
-            tt(V("ix", 64 * h, 64 * h + 64), V("fb", 64 * h, 64 * h + 64), P(2 + h, 0, 64), OP.min)
-            cp(V("il", 64 * h, 64 * h + 64), V("ix", 64 * h, 64 * h + 64))
+            ts(V("okw", 0, 256), P(6, 0, 256), 7.5, None, OP.is_lt)
+        mm([(P(5, 0, 256), I_B, V("cv", 0, 256), True, False)])
+        mm([(P(5, 16 * i, 16 * i + 16), T_LT, V("okw", i, 256, 16), False, i == 15) for i in range(16)])
+        act(V("pv", 0, 256), P(5, 0, 256), AF.Copy)
+        cp((V("cw", 0, CWN), V("pl", 0, 17)), V("pv", 0, 272))
+        for lo, hi in cuts(KN["pp"][0]):
+            scan(V("cn", 2 * lo, 2 * hi), V("cw", 2 * lo, 2 * hi), V("dec", 0, 2 * (hi - lo)),
+                 V("cn", 2 * lo - 1, 2 * lo) if lo else -1.0, OP.max, OP.add)
+        if t < 2:
+            move(V("cw", 0, 2048), V("zer", 0, 2048))
+        z = 0
+        for k, h in enumerate(order):
+            for lo, hi in cuts(KN["pp"][k]):
+                a, b = 64 * h + lo // 16, 64 * h + hi // 16
+                cut(KN["px"][t][z], V("cmp", S * h + lo, S * h + hi), V("cn", 2 * lo + h, 2 * hi, 2))
+                rows(P(2 + z, 0, b - a), "cmp", S * h + lo, S * h + hi)
+                tt(V("ix", a, b), V("fb1" if h and far(t, 1) else "fb", a, b), P(2 + z, 0, b - a), OP.min)
+                cp(V("il", a, b), V("ix", a, b))
+                z += 1
 
-    def step(t, h, dst, done):
+    def step(t, h, end, dst, done):
         p, z = who(t), KN["sc"]
         bk = 0 if h == KN["first"][t] else 2
         shift = h == 1 and t < 2
         for lo in range(0, S, z):
             hi = lo + z
-            gat = (V("win", 0, 3 * K), V("il", 64 * h + lo // 16, 64 * h + hi // 16))
+            gat = (V("win", 0, end), V("il", 64 * h + lo // 16, 64 * h + hi // 16))
             hh, uu, tv = (V(nm, S * h + lo, S * h + hi) for nm in ("hh", "uu", "tt"))
             act(hh, gat, AF.Square)
-            tt(uu, gat, hh, OP.add)
+            tt(uu, gat, hh, OP.subtract)
             act(tv, uu, AF.Identity, 0.0, p["r"][h])
-            mm([(P(bk, lo, hi), SH_N if shift else I_N, tv, True, False),
+            mm([(P(bk, lo, hi), SH_F if shift else I_F, tv, True, False),
                 (P(bk, lo, hi), SH_B if shift else I_B, V(p["nz"], lo, hi), False, True)])
             if hi % 512 == 0:
-                ts(V(dst, hi - 512, hi), P(bk, hi - 512, hi), 0.0, 1.0, OP.max, OP.min)
+                ts(W(dst, hi - 512, hi), P(bk, hi - 512, hi), 0.0, 1.0, OP.max, OP.min)
                 done(hi - 512, hi)
 
     def energy():
@@ -419,9 +493,9 @@ def rank_program(g, core, T, topo):
                 if i < npe:
                     w = z if i else 512
                     for a in range(lo, lo + 512, w):
-                        mm([(P(6, a, a + w), I_N, V("dd", S * i + a, S * i + a + w), i == 0, i == npe - 1 and a + w == lo + 512)])
+                        mm([(P(6, a, a + w), I_F, V("dd", S * i + a, S * i + a + w), i == 0, i == npe - 1 and a + w == lo + 512)])
                 elif i == npe:
-                    tt(V("yo", lo, lo + 512), v, P(6, lo, lo + 512), OP.subtract)
+                    tt(V("yo", lo, lo + 512), v, P(6, lo, lo + 512), OP.add)
                 else:
                     tt(V("yo", lo, lo + 512), V("yo", lo, lo + 512), P(4, lo, lo + 512), OP.add)
                 if i == 3:
@@ -430,42 +504,37 @@ def rank_program(g, core, T, topo):
     def nothing(lo, hi):
         return None
 
-    starts(0, 0, "f16", 2, 3)
-    starts(0, 1, "b16", 6, 7)
-    act(V("pb", 0, S), V("b16", 0, S), AF.Copy)
-    f_ancestors("f16")
-    b_ancestors("pb")
-    pairs(0)
-    places(0)
+    def ancestors(t, f, b, base):
+        f_ancestors(t, f)
+        b_ancestors(t, base)
+        pairs(t, b)
+        places(t)
+
+    starts(0, 1, ("b16", 0), 6, 7)
+    starts(0, 0, ("f16", 0), 2, 3)
+    ancestors(0, ("f16", 0), ("b16", 0), BA)
 
     def b_goes(lo, hi):
-        send(rank - 2, V("lb", lo, hi), V("snd", lo, hi), "xb%d" % (lo // 512))
-        arrives(rank + 2, V("lb", lo, hi), "xb%d" % (lo // 512))
-    step(0, 1, "snd", b_goes)
-    step(0, 0, "pf", nothing)
-    starts(1, 0, "pf", 4, 5)
-    starts(1, 1, "lb", 6, 7)
-    f_ancestors("pf")
-    b_ancestors("lb")
-    pairs(1)
-    places(1)
+        hand(-2, V("win", BB + lo, BB + hi), V("snd", lo, hi))
+    step(0, 1, BB, ("snd", 0), b_goes)
+    step(0, 0, BA, ("pf", 0), nothing)
+    starts(1, 1, ("snd", 0) if far(1, 1) else ("win", BB), 6, 7)
+    starts(1, 0, ("pf", 0), 4, 5)
+    ancestors(1, ("pf", 0), ("win", BB), BB)
 
     def f_goes(lo, hi):
-        send(rank + 2, V("lf", lo, hi), V("snd", lo, hi), "xf%d" % (lo // 512))
-        arrives(rank - 2, V("lf", lo, hi), "xf%d" % (lo // 512))
-    step(1, 0, "snd", f_goes)
-    step(1, 1, "pb", nothing)
-    starts(2, 1, "pb", 4, 5)
-    starts(2, 0, "lf", 6, 7)
-    f_ancestors("lf")
-    b_ancestors("pb")
-    pairs(2)
-    places(2)
+        hand(2, V("lf", lo, hi), V("snd", lo, hi))
+    step(1, 0, BA, ("snd", 0), f_goes)
+    step(1, 1, BC, ("win", BC), nothing)
+    starts(2, 0, ("snd", 0) if far(2, 0) else ("lf", 0), 6, 7)
+    starts(2, 1, ("win", BC), 4, 5)
+    ancestors(2, ("lf", 0), ("win", BC), BC)
     energy()
-    step(2, 0, "pf", lambda lo, hi: store("sp", T.yf[:, lo:hi], V("pf", lo, hi)))
-    step(2, 1, "pb", lambda lo, hi: store("sp", T.yb[:, lo:hi], V("pb", lo, hi)))
+    step(2, 0, BA, ("pf", 0), lambda lo, hi: store("sp", T.yf[:, lo:hi], V("pf", lo, hi)))
+    step(2, 1, BC + S, ("snd", 0), lambda lo, hi: store("sp", T.yb[:, lo:hi], V("snd", lo, hi)))
 
     if "order" not in PLAN:
+        PLAN["ops"] = ops
         PLAN["deps"] = depends(ops)
         PLAN["order"] = arrange(ops, PLAN["deps"], KN["seed"], KN["tries"])
     emit(g, T, ops, PLAN["deps"], PLAN["order"])
@@ -485,14 +554,15 @@ def depends(ops):
     return deps
 
 
-SPEEDS = ((1.56, 3.8, 2.4, 250e3, 0.2, 0.00045), (1.1, 2.0, 1.8, 300e3, 0.1, 0.00042), (2.0, 5.6, 3.0, 200e3, 0.25, 0.0006))
+SPEEDS = ((1.56, 3.8, 2.4, 250e3, 0.2, 0.00045, 1.25), (1.1, 2.0, 1.8, 300e3, 0.1, 0.00042, 1.1),
+          (2.0, 5.6, 3.0, 200e3, 0.25, 0.0005, 1.4))
 
 
 def times(o, m):
     k, c = o["cost"]
     if k == "dma":
         return (0.3 if o["kind"] == "remote" else 1.0 if o["q"] == "pool" else 0.06), m[2] + c / m[3] + m[4], 0.05 + c / m[3]
-    t = 1.25 * {"c": c * 0.00083, "g": 0.055 + c * 0.00083 * m[0], "sc": 0.055 + c * 0.00083 * m[1], "pe": c * m[5]}[k]
+    t = m[6] * {"c": c * 0.00083, "g": 0.055 + c * 0.00083 * m[0], "sc": 0.055 + c * 0.00083 * m[1], "pe": c * m[5]}[k]
     return t, t + m[4], 0.0
 
 
@@ -514,6 +584,9 @@ def arrange(ops, deps, seed, tries):
     q = [["dve", "act", "pe", "pool", "sp", "ext"].index(o["q"]) for o in ops]
     tms = [[times(o, m) for o in ops] for m in SPEEDS]
     tm = tms[0]
+    tail = [0.0] * n
+    for i in range(n - 1, -1, -1):
+        tail[i] = tm[i][1] + max([tail[j] for j in after[i]] + [0.0])
     left, ready, free, order = [len(d) for d in near], [0.0] * n, [0.0] * 6, []
     pool = [[i for i in range(n) if q[i] == k and not left[i]] for k in range(6)]
     while len(order) < n:
@@ -521,7 +594,7 @@ def arrange(ops, deps, seed, tries):
         for k in range(6):
             if pool[k]:
                 t0 = max(free[k], min(ready[i] for i in pool[k]))
-                i = min(i for i in pool[k] if ready[i] <= t0 + 0.1)
+                i = max((i for i in pool[k] if ready[i] <= t0 + 0.1), key=lambda j: tail[j])
                 t = max(free[k], ready[i])
                 if best is None or t < best[0]:
                     best = (t, i)
@@ -554,7 +627,55 @@ def arrange(ops, deps, seed, tries):
         end = done[part[-1]] if ops[part[-1]].get("mark") else max(free)
         return end + 0.1 * total / len(part) + 0.5 * sum(max(0.0, f - end) for f in free[:3]), free, end
 
-    head = [i for i in range(n) if ops[i]["kind"] == "dma" and not near[i]]
+    def pack(seq, links, back):
+        at, lows, highs = [0.0] * n, [[] for _ in range(6)], [[] for _ in range(6)]
+        for i in seq:
+            a, b = tm[i][0], tm[i][1]
+            t = b - a if back else 0.0
+            for j in links[i]:
+                u = at[j] + (tm[j][0] + b - a if back else tm[j][1])
+                if u > t:
+                    t = u
+            lo, hi = lows[q[i]], highs[q[i]]
+            z = len(hi)
+            while z and hi[z - 1] > t:
+                z -= 1
+            while z < len(lo) and lo[z] < t + a:
+                t = max(t, hi[z])
+                z += 1
+            lo.insert(z, t)
+            hi.insert(z, t + a)
+            at[i] = t
+        return at
+
+    def worth(seq):
+        c = [span(seq, t, [0.0] * n, [0.0] * 7, [0.0] * n)[2] for t in tms]
+        return c[0] + sum(c)
+
+    best, key = (worth(order), order), {i: float(z) for z, i in enumerate(order)}
+    base = None
+    for k in range(KN["packs"]):
+        if base is not None:
+            key = list(base)
+            seed = (seed * 1103515245 + 12345) % 2147483648
+            mid, amp = (seed >> 8) % 1000 * max(base) / 1000.0, KN["shake"] * (1 + (seed >> 4) % 4)
+            for i in range(n):
+                seed = (seed * 1103515245 + 12345) % 2147483648
+                if abs(key[i] - mid) < KN["reach"]:
+                    key[i] += amp * ((seed >> 8) % 1000) / 1000.0
+                for j in near[i]:
+                    key[i] = max(key[i], key[j] + 1e-6)
+        for turn in range(2):
+            at = pack(sorted(range(n), key=lambda i: (key[i], i)), near, False)
+            bk = pack(sorted(range(n), key=lambda i: (-at[i] - tm[i][1], -i)), after, True)
+            key = [-bk[i] - tm[i][0] for i in range(n)]
+        at = pack(sorted(range(n), key=lambda i: (key[i], i)), near, False)
+        seq = sorted(range(n), key=lambda i: (at[i], i))
+        c = worth(seq)
+        if base is None or c <= best[0]:
+            best, base = (c, seq), at
+    order = best[1]
+    head = [i for i in range(n) if ops[i]["kind"] == "dma" and not near[i] and q[i] != 3]
     order = [i for i in order if i not in head]
     ends = [0] + [z + 1 for z, i in enumerate(order) if ops[i].get("mark")] + [len(order)]
     start, dones = [0.0] * n, [[0.0] * n for _ in tms]

@@ -11,14 +11,15 @@ KN = {
     "fs": (1025, 1024, 2048), "bs": (2048, 2048),
     "fx": "ppp",
     "cmp": ("ddddddddd",) * 3,
-    "mul": ("aaaaaaaaa",) * 3, "add": ("ddddddddd",) * 3, "look": ("aadaadaa",) * 3, "fg": ("aaaaaaaaa",) * 3,
+    "mul": ("aaaaaaaaa",) * 3, "add": ("mmmmmmddd",) * 3, "look": ("dadadada",) * 3, "fg": ("aaaaaaaaa",) * 3,
     "sc": 256,
     "miss": ("dd", "dd", "dd"),
     "first": (1, 0, 0),
-    "oka": (1, 1, 0), "yepe": 3, "yes": 256, "px": ("dda", "dda", "ddd"), "bx": "aaa", "clr": "s",
+    "parts": (3072, 1024), "cl": ((512, 512), (512, 512), (512, 512)), "yedma": 0, "acc": 1,
+    "oka": ("ad", "ad", "dd"), "yepe": 3, "yes": 256, "px": ("dda", "dda", "ddd"), "bx": "aaa", "clr": "s",
     "pp": ((512, 512), (1024,)), "side": (1, 1), "fh": (1024, 1024, 2048), "bh": (1024, 1024, 2048),
     "ld": 512, "wc": (512, 512),
-    "seed": 1, "tries": 100000, "heat": 0.1, "packs": 1500, "shake": 0.5, "reach": 10.0,
+    "seed": 1, "tries": 150000, "heat": 1.0, "aim": 6, "packs": 300, "shake": 0.5, "reach": 10.0,
 }
 
 SCRATCH = {
@@ -40,11 +41,12 @@ SCRATCH = {
     "tt": ("sbuf", [128, 2048], "float32"), "yo": ("sbuf", [128, S], "float32"),
     "wt": ("sbuf", [128, 144], "bfloat16"), "sm": ("sbuf", [128, 1024], "float32"),
     "lb": ("sbuf", [128, 128], "bfloat16"), "sv": ("sbuf", [128, 128], "bfloat16"), "sl": ("sbuf", [128, 8], "uint16"),
-    "okw": ("sbuf", [128, 256], "bfloat16"), "okb": ("sbuf", [128, 256], "bfloat16"), "el": ("sbuf", [128, 264], "bfloat16"),
+    "okw": ("sbuf", [128, 256], "bfloat16"), "okb": ("sbuf", [128, 256], "bfloat16"), "el": ("sbuf", [128, 280], "bfloat16"),
+    "oks": ("sbuf", [128, 256], "bfloat16"),
     "al": ("sbuf", [128, 256], "uint16"), "jl": ("sbuf", [128, 256], "uint16"),
     "al2": ("sbuf", [128, 256], "uint16"), "jl1": ("sbuf", [128, 256], "uint16"), "fb1": ("sbuf", [128, 128], "float32"),
     "prm2": ("sbuf", [128, 8], "float32"), "prm3": ("sbuf", [128, 8], "float32"),
-    "emp": ("sbuf", [128, 64], "float32"), "pl": ("sbuf", [128, 18], "uint16"), "pv": ("sbuf", [128, 272], "bfloat16"),
+    "emp": ("sbuf", [128, 128], "float32"), "pl": ("sbuf", [128, 36], "uint16"), "pv": ("sbuf", [128, 272], "bfloat16"),
     "ix": ("sbuf", [128, 128], "float32"), "il": ("sbuf", [128, 128], "uint16"),
     "sel": ("sbuf", [128, 144], "bfloat16"), "seln": ("sbuf", [128, 144], "bfloat16"),
     "sla": ("sbuf", [128, 144], "bfloat16"), "slb": ("sbuf", [128, 144], "bfloat16"),
@@ -55,7 +57,7 @@ SCRATCH = {
     "off": ("sbuf", [128, 72], "bfloat16"), "one": ("sbuf", [128, 72], "float32"),
     "zer": ("sbuf", [128, 2048], "bfloat16"), "dec": ("sbuf", [128, 2064], "bfloat16"),
     "kk": ("sbuf", [128, 128], "bfloat16"), "fb": ("sbuf", [128, 128], "float32"),
-    "kd": ("sbuf", [128, 24], "float32"), "cv": ("sbuf", [128, 256], "bfloat16"),
+    "kd": ("sbuf", [128, 48], "float32"), "cv": ("sbuf", [128, 256], "bfloat16"),
     "ri": ("sbuf", [128, 8], "int32"), "rc": ("sbuf", [128, 16], "float32"),
     "ps": ("psum", [128, 4096], "float32"),
 }
@@ -212,10 +214,19 @@ def rank_program(g, core, T, topo):
         mm([(out, SEL(u), V(name, lo + u * step // 16, hi, step), u == 0, u == 15) for u in range(16)])
 
     def cut(eng, out, a):
-        if eng == "a":
-            act(out, a, AF.Relu, 0.0, SCL)
-        else:
-            ts(out, a, SCL, 0.0, OP.mult, OP.max)
+        either(eng, lambda: act(out, a, AF.Relu, 0.0, SCL), lambda: ts(out, a, SCL, 0.0, OP.mult, OP.max))
+
+    def either(eng, on_act, on_dve):
+        for fn in ((on_dve, on_act) if eng == "a" else (on_act, on_dve)):
+            fn()
+        alt = ops.pop(-2)
+        ops[-1]["alt"] = {k: alt[k] for k in ("q", "fn", "cost")}
+
+    def copy(eng, out, a):
+        either(eng, lambda: act(out, a, AF.Copy), lambda: cp(out, a))
+
+    def scale(eng, out, a, s):
+        either(eng, lambda: act(out, a, AF.Identity, 0.0, s), lambda: ts(out, a, s, None, OP.mult))
 
     T_LT, T_GE = V("tri", 0, 128), V("tri", 128, 256)
     I_B, SH_B, I_F, SH_F = V("qb", 16, 144), V("qb", 0, 128), V("q", 16, 144), V("q", 0, 128)
@@ -247,9 +258,11 @@ def rank_program(g, core, T, topo):
     sel(V("q", 0, 16), V("q", 0, 16), [[1, 16]], OP.not_equal, 1.0, 112, -1)
     iota(V("kk", 0, 128), [[0, 2], [0, 4], [1, 16]], 0, 0)
     iota(V("kk", 64, 128), [[1, 64]], 0, 0)
-    iota(V("cv", 0, 256), [[1, 16], [16, 16]], 0, 0)
+    PARTS = cuts(KN["parts"])
+    for a, b in PARTS:
+        iota(V("cv", a // 16, b // 16), [[1, (b - a) // 256], [(b - a) // 256, 16]], a // 16, 0)
     iota(V("fb", 0, 64), [[64, 64]], K, 0)
-    iota(V("kd", 0, 17), [[1, 17]], K + 1, 0)
+    iota(V("kd", 0, 48), [[0, 2], [1, 24]], K + 1, 0)
     load("pool", V("win", BA, BA + S), T.b0[:])
     for lo in range(0, 2048, 1024):
         ms(V("zer", lo, lo + 1024), 0.0)
@@ -293,8 +306,8 @@ def rank_program(g, core, T, topo):
     if KN["side"][1]:
         hand(2, V("prm3", 0, 8), V("prm0", 0, 8))
     ms(V("rc", 3, 4), 7.5)
-    ms(V("el", 0, 8), 0.0)
-    ms(V("emp", 16, 20), 1.0)
+    ms(V("el", 0, 280), 0.0)
+    ms(V("emp", 0, 128), 1.0)
     ts(V("rc", 0, 1), ROW, 4.0, None, OP.mult)
     ts(V("rc", 1, 2), ROW, 17.0, None, OP.mult)
     ts(V("rc", 2, 3), ROW, 15.0, None, OP.is_lt)
@@ -302,8 +315,9 @@ def rank_program(g, core, T, topo):
     ts(V("pv", 256, 272), V("zer", 0, 16), V("rc", 8, 9), None, OP.add)
     ts(V("cv", 0, 256), V("cv", 0, 256), IS0, None, OP.mult)
     ts(V("fb", 0, 64), V("fb", 0, 64), V("rc", 0, 1), None, OP.add)
-    ts(V("kd", 0, 17), V("kd", 0, 17), V("rc", 1, 2), None, OP.add)
-    ts(V("kd", 16, 17), V("kd", 16, 17), V("rc", 2, 3), None, OP.mult)
+    ts(V("kd", 0, 48), V("kd", 0, 48), V("rc", 1, 2), None, OP.add)
+    z = 24 * (len(PARTS) - 1) + KN["parts"][-1] // 256
+    ts(V("kd", z, z + 1), V("kd", z, z + 1), V("rc", 2, 3), None, OP.mult)
 
     def who(t):
         k = "1" if t == 1 else "0"
@@ -350,7 +364,7 @@ def rank_program(g, core, T, topo):
             mm([(out, V("topb", 128 * z, 128 * z + 128), L, False, True)])
         scan(M, P(bk2, 128, 192), V("zer", 0, 64), 0.0, OP.max, OP.add)
         cp(sl, V("sm", o + 335, o + 384, 16))
-        act(vals, P(bk, 128, 192), AF.Copy)
+        copy("a", vals, P(bk, 128, 192))
         wn, sn = ("wf", "wb")[h], ("sf", "sb")[h]
         cp((V(wn, 0, K), sl), vals)
         for lo, hi in cuts(KN["bs" if h else "fs"]):
@@ -384,10 +398,7 @@ def rank_program(g, core, T, topo):
         clear(t, 0)
         for i, (lo, hi) in enumerate(cuts(KN["loop"])):
             gat = (W(pool, 0, S), V("al2" if far(t, 0) else "al", lo // 16, hi // 16))
-            if KN["fg"][t][i] == "a":
-                act(V("win", F0 + lo, F0 + hi), gat, AF.Copy)
-            else:
-                cp(V("win", F0 + lo, F0 + hi), gat)
+            copy(KN["fg"][t][i], V("win", F0 + lo, F0 + hi), gat)
 
     def b_ancestors(t, base):
         p = who(t)
@@ -413,11 +424,8 @@ def rank_program(g, core, T, topo):
             d, f, m, x = V("dd", lo, hi), V("win", F0 + lo, F0 + hi), V("win", lo, hi), V("miss", lo, hi)
             a, s = V("ab", o, o + z), V("sg", o, o + z)
             tt(d, (W(pool, 0, S), V("jl1" if far(t, 1) else "jl", lo // 16, hi // 16)), f, OP.subtract)
-            prod = P(i % 4, 0, z) if KN["add"][t][i] == "d" else m
-            if KN["mul"][t][i] == "a":
-                act(prod, d, AF.Identity, 0.0, p["lam"])
-            else:
-                ts(prod, d, p["lam"], None, OP.mult)
+            prod = P(i % 2, 0, z) if KN["add"][t][i] == "d" else m
+            scale(KN["mul"][t][i], prod, d, p["lam"])
             if KN["add"][t][i] == "d":
                 tt(m, f, prod, OP.add)
             else:
@@ -428,32 +436,47 @@ def rank_program(g, core, T, topo):
                 ts(x, s, 0.0, None, OP.max)
             else:
                 ts(x, a, p["eps"], None, OP.is_gt)
-            mm([(P(7, 0, 256), SEL(r), V("miss", 256 * r, 256 * r + 256), r == 0, r == 15) for r in range(lo // 256, hi // 256)])
+            s = max(k for k in range(len(PARTS)) if PARTS[k][0] <= lo)
+            a, b = PARTS[s]
+            w = (b - a) // 16
+            mm([(P(7 - 4 * s, 0, w), SEL(r), V("miss", a + w * r, a + w * r + w), r == 0, r == 15)
+                for r in range((lo - a) // w, (hi - a) // w)])
             if hi in ends:
-                rows(P(6, ends[hi] // 16, hi // 16), "miss", ends[hi], hi)
+                rows(P(6 - 4 * s, ends[hi] // 16, hi // 16), "miss", ends[hi], hi)
+            if hi == b:
+                columns(t, s)
+
+    def columns(t, s):
+        a, b = PARTS[s]
+        w, c, last = (b - a) // 16, a // 16, s == len(PARTS) - 1
+        nc, e, o = w // 16, c + 8 * s, 64 * s
+        ne = nc + last
+        ts(V("okb", c, c + w), P(7 - 4 * s, 0, w), 7.5, None, OP.is_lt)
+        scan(V("el", e + 1, e + w + 1), V("okb", c, c + w), V("okb", c, c + w), 0.0, OP.add, OP.max)
+        tot = [V("el", PARTS[k][1] // 16 + 8 * k, PARTS[k][1] // 16 + 8 * k + 1) for k in range(s + 1)]
+        if s:
+            mm([(P(5, 400 + s, 401 + s), V("blk", 0, 128), tot[k], k == 0, False) for k in range(s)])
+        mm([(P(5, 400 + s, 401 + s), T_LT, tot[s], s == 0, True)])
+        tt(V("emp", o, o + nc), V("el", e, e + w, 16), V("el", e + 16, e + w + 1, 16), OP.is_equal)
+        tt(V("emp", o + 20, o + 20 + ne), V("emp", o, o + ne), V("kd", 24 * s, 24 * s + ne), OP.mult)
+        tt(V("emp", o + 40, o + 40 + ne), V("emp", o + 20, o + 20 + ne), V("el", e, e + 16 * ne - 15, 16), OP.add)
+        ts(V("pl", 18 * s, 18 * s + ne), V("emp", o + 40, o + 40 + ne), P(5, 400 + s, 401 + s), None, OP.add)
+        if KN["oka"][t][s] == "a":
+            act(V("oks", c, c + w), P(6 - 4 * s, c, c + w), AF.Sign, V("rc", 3, 4), -1.0)
+            act(V("okw", c, c + w), V("oks", c, c + w), AF.Relu)
+        else:
+            ts(V("okw", c, c + w), P(6 - 4 * s, c, c + w), 7.5, None, OP.is_lt)
+        mm([(P(4, 256 + c, 256 + c + w), I_B, V("cv", c, c + w), True, False)])
+        mm([(P(4, 256 + c + 16 * i, 272 + c + 16 * i), T_LT, V("okw", c + i, c + w, nc), False, i == nc - 1) for i in range(nc)])
+        copy("a", V("pv", c, c + w), P(4, 256 + c, 256 + c + w))
+        cp((V("cw", 0, CWN), V("pl", 18 * s, 18 * s + ne)), V("pv", c, c + 16 * ne))
 
     def places(t):
         order = (KN["first"][t], 1 - KN["first"][t])
-        ts(V("okb", 0, 256), P(7, 0, 256), 7.5, None, OP.is_lt)
-        ops[-1]["mark"] = True
-        scan(V("el", 1, 257), V("okb", 0, 256), V("okb", 0, 256), 0.0, OP.add, OP.max)
-        mm([(P(4, 0, 1), T_LT, V("el", 256, 257), True, True)])
-        tt(V("emp", 0, 16), V("el", 0, 256, 16), V("el", 16, 257, 16), OP.is_equal)
-        tt(V("emp", 20, 37), V("emp", 0, 17), V("kd", 0, 17), OP.mult)
-        tt(V("emp", 40, 57), V("emp", 20, 37), V("el", 0, 257, 16), OP.add)
-        ts(V("pl", 0, 17), V("emp", 40, 57), P(4, 0, 1), None, OP.add)
-        if KN["oka"][t]:
-            act(V("sg", 0, 256), P(6, 0, 256), AF.Sign, V("rc", 3, 4), -1.0)
-            act(V("okw", 0, 256), V("sg", 0, 256), AF.Relu)
-        else:
-            ts(V("okw", 0, 256), P(6, 0, 256), 7.5, None, OP.is_lt)
-        mm([(P(5, 0, 256), I_B, V("cv", 0, 256), True, False)])
-        mm([(P(5, 16 * i, 16 * i + 16), T_LT, V("okw", i, 256, 16), False, i == 15) for i in range(16)])
-        act(V("pv", 0, 256), P(5, 0, 256), AF.Copy)
-        cp((V("cw", 0, CWN), V("pl", 0, 17)), V("pv", 0, 272))
         for lo, hi in cuts(KN["pp"][0]):
             scan(V("cn", 2 * lo, 2 * hi), V("cw", 2 * lo, 2 * hi), V("dec", 0, 2 * (hi - lo)),
                  V("cn", 2 * lo - 1, 2 * lo) if lo else -1.0, OP.max, OP.add)
+            ops[-1]["mark"] = lo == 0
         if t < 2:
             move(V("cw", 0, 2048), V("zer", 0, 2048))
         z = 0
@@ -476,15 +499,37 @@ def rank_program(g, core, T, topo):
             hh, uu, tv = (V(nm, S * h + lo, S * h + hi) for nm in ("hh", "uu", "tt"))
             act(hh, gat, AF.Square)
             tt(uu, gat, hh, OP.subtract)
-            act(tv, uu, AF.Identity, 0.0, p["r"][h])
-            mm([(P(bk, lo, hi), SH_F if shift else I_F, tv, True, False),
-                (P(bk, lo, hi), SH_B if shift else I_B, V(p["nz"], lo, hi), False, True)])
-            if hi % 512 == 0:
-                ts(W(dst, hi - 512, hi), P(bk, hi - 512, hi), 0.0, 1.0, OP.max, OP.min)
-                done(hi - 512, hi)
+            if KN["acc"] and not shift:
+                if lo % 512 == 0:
+                    mm([(P(bk, lo, lo + 512), I_B, V("zer", 0, 512), True, False)])
+                scale("a", P(bk, lo, hi), uu, p["r"][h])
+                mm([(P(bk, lo, hi), I_B, V(p["nz"], lo, hi), False, hi % 512 == 0)])
+            else:
+                scale("a", tv, uu, p["r"][h])
+                mm([(P(bk, lo, hi), SH_F if shift else I_F, tv, True, False),
+                    (P(bk, lo, hi), SH_B if shift else I_B, V(p["nz"], lo, hi), False, True)])
+            for a, b in cuts(KN["cl"][t]):
+                if b == hi:
+                    ts(W(dst, a, b), P(bk, a, b), 0.0, 1.0, OP.max, OP.min)
+                    if t == 2 or b % 512 == 0:
+                        done(a if t == 2 else b - 512, b)
 
     def energy():
         npe, z = KN["yepe"], KN["yes"]
+        if KN["yedma"]:
+            for i in range(4):
+                for lo in range(0, S, 512):
+                    v = V("dd", S * i + lo, S * i + lo + 512)
+                    act(v, v, AF.Square)
+                    act(v, v, AF.Exp, 0.0, -1.0, 1500.0 if i + lo == 0 else 0.0)
+                if i % 2:
+                    adds(V("dd", S * i - S, S * i), V("dd", S * i, S * i + S))
+            store("sp", T.ye[:], V("dd", 0, S))
+            ops[-1]["w"].append(("ye", 0, S))
+            a = V("dd", 2 * S, 3 * S)
+            rec("pool", lambda: g.dma_start(T.ye[:], ap(a), accum_op=OP.add), [a], [], ("dma", 256 * 4 * S), "dma")
+            ops[-1]["w"].append(("ye", 0, S))
+            return
         for lo in range(0, S, 512):
             for i in range(4):
                 v = V("dd", S * i + lo, S * i + lo + 512)
@@ -536,7 +581,9 @@ def rank_program(g, core, T, topo):
     if "order" not in PLAN:
         PLAN["ops"] = ops
         PLAN["deps"] = depends(ops)
-        PLAN["order"] = arrange(ops, PLAN["deps"], KN["seed"], KN["tries"])
+        PLAN["order"], PLAN["over"] = arrange(ops, PLAN["deps"], KN["seed"], KN["tries"])
+    for i in PLAN["over"]:
+        ops[i].update(ops[i]["alt"])
     emit(g, T, ops, PLAN["deps"], PLAN["order"])
 
 
@@ -550,12 +597,12 @@ def depends(ops):
             continue
         bank = [x for x in o["r"] if x[0] == "ps"]
         deps.append([j for j in range(i) if hits(o["r"], ops[j]["w"]) or hits(o["w"], ops[j]["w"]) or hits(o["w"], ops[j]["r"])
-                     or (ops[j]["q"] != o["q"] and hits(bank, ops[j]["r"]))])
+                     or ((ops[j]["q"] != o["q"] or "alt" in o or "alt" in ops[j]) and hits(bank, ops[j]["r"]))])
     return deps
 
 
-SPEEDS = ((1.56, 3.8, 2.4, 250e3, 0.2, 0.00045, 1.25), (1.1, 2.0, 1.8, 300e3, 0.1, 0.00042, 1.1),
-          (2.0, 5.6, 3.0, 200e3, 0.25, 0.0005, 1.4))
+SPEEDS = ((1.56, 3.8, 1.8, 450e3, 0.2, 0.00045, 1.25), (1.1, 2.0, 1.6, 500e3, 0.1, 0.00042, 1.1),
+          (2.0, 5.6, 2.0, 400e3, 0.25, 0.0005, 1.4))
 
 
 def times(o, m):
@@ -627,6 +674,32 @@ def arrange(ops, deps, seed, tries):
         end = done[part[-1]] if ops[part[-1]].get("mark") else max(free)
         return end + 0.1 * total / len(part) + 0.5 * sum(max(0.0, f - end) for f in free[:3]), free, end
 
+    def critical(part, tm, done, free):
+        free, prev, why = list(free), [None] * 7, {}
+        for i in part:
+            k = q[i]
+            t, w = free[k], (prev[k], True)
+            for j in near[i]:
+                if done[j] > t:
+                    t, w = done[j], (j, False)
+            a, b, c = tm[i]
+            free[k], prev[k], why[i] = t + a, i, w
+            if c:
+                if free[6] + c > t + b:
+                    why[i] = (prev[6], False)
+                free[6] = done[i] = max(free[6] + c, t + b)
+                prev[6] = i
+            else:
+                done[i] = t + b
+        i = part[-1] if ops[part[-1]].get("mark") else max(part, key=lambda j: done[j])
+        pairs = []
+        while i in why:
+            j, same = why[i]
+            if same and j is not None and not reach[i] >> j & 1:
+                pairs.append((j, i))
+            i = j
+        return pairs
+
     def pack(seq, links, back):
         at, lows, highs = [0.0] * n, [[] for _ in range(6)], [[] for _ in range(6)]
         for i in seq:
@@ -680,21 +753,40 @@ def arrange(ops, deps, seed, tries):
     ends = [0] + [z + 1 for z, i in enumerate(order) if ops[i].get("mark")] + [len(order)]
     start, dones = [0.0] * n, [[0.0] * n for _ in tms]
     frees = [span(head, t, d, [0.0] * 7, start)[1] for t, d in zip(tms, dones)]
-    out = list(head)
+    out, over = list(head), set()
+
+    def turn_over(i):
+        over.symmetric_difference_update([i])
+        o = dict(ops[i], **ops[i]["alt"]) if i in over else ops[i]
+        q[i] = ["dve", "act"].index(o["q"])
+        for t, sp in zip(tms, SPEEDS):
+            t[i] = times(o, sp)
     for lo, hi in zip(ends, ends[1:]):
         part = order[lo:hi]
         m = len(part) - (1 if ops[part[-1]].get("mark") else 0)
         now = [span(part, t, d, f, start)[0] for t, d, f in zip(tms, dones, frees)]
-        turns = tries * m // n
+        turns, tight, top = tries * m // n, None, (now[0] + sum(now), part, set(over))
         for k in range(turns):
             seed = (seed * 1103515245 + 12345) % 2147483648
             a = (seed >> 8) % m
+            seed = (seed * 1103515245 + 12345) % 2147483648
+            hops, up = 1 + (seed >> 8) % 4, seed >> 20 & 1
+            if tight is None:
+                z = (seed >> 12) % len(tms)
+                tight = critical(part, tms[z], dones[z], frees[z])
+            if tight and (seed >> 14) % 8 < KN["aim"]:
+                a = part.index(tight[a % len(tight)][up])
+                hops = 1 + (hops > 2) + (hops > 3)
+                if a >= m:
+                    continue
             i = part[a]
             if q[i] == 5:
                 continue
-            seed = (seed * 1103515245 + 12345) % 2147483648
-            hops, b, block, rest = 1 + (seed >> 8) % 4, a, [i], []
-            up = seed >> 20 & 1
+            other = "alt" in ops[i] and (seed >> 24) % 4 == 0
+            if other:
+                turn_over(i)
+                hops -= 1
+            b, block, rest = a, [i], []
             while hops and (0 < b if up else b < m - 1):
                 b += -1 if up else 1
                 j = part[b]
@@ -705,18 +797,24 @@ def arrange(ops, deps, seed, tries):
                     hops -= q[j] == q[i]
             new = part[:b] + block[::-1] + rest[::-1] + part[a + 1:] if up else part[:a] + rest + block + part[b + 1:]
             heat = KN["heat"] * (1.0 - k / turns)
-            if span(new, tm, dones[0], frees[0], start)[0] > now[0] + heat + 0.2:
-                continue
-            at = {j: z for z, j in enumerate(new)}
-            new = sorted(new[:m], key=lambda j: (start[j], at[j])) + new[m:]
-            c = [span(new, t, d, f, start)[0] for t, d, f in zip(tms, dones, frees)]
-            if c[0] + sum(c) <= now[0] + sum(now) + heat:
-                now, part = c, new
+            if span(new, tm, dones[0], frees[0], start)[0] <= now[0] + heat + 0.2:
+                at = {j: z for z, j in enumerate(new)}
+                new = sorted(new[:m], key=lambda j: (start[j], at[j])) + new[m:]
+                c = [span(new, t, d, f, start)[0] for t, d, f in zip(tms, dones, frees)]
+                if c[0] + sum(c) <= now[0] + sum(now) + heat:
+                    now, part, tight, other = c, new, None, False
+                    if c[0] + sum(c) < top[0]:
+                        top = (c[0] + sum(c), new, set(over))
+            if other:
+                turn_over(i)
+        part = top[1]
+        for i in over ^ top[2]:
+            turn_over(i)
         last = [span(part, t, d, f, start) for t, d, f in zip(tms, dones, frees)]
         frees = [x[1] for x in last]
         PLAN.setdefault("parts", []).append([round(x[2], 1) for x in last])
         out += part
-    return out
+    return out, over
 
 
 def emit(g, T, ops, deps, order):

@@ -3,66 +3,65 @@ from concourse.mybir import AluOpType as OP, ActivationFunctionType as AF
 S, K = 1024, 4096
 MAGIC = 12582912.0
 CWN = 8480
+JUNK = 16 * 1024 + 15
 F0, BA, BB, BC = K, 2 * K, 2 * K + S, 2 * K + 2 * S
 KN = {
     "loop": (512, 512, 512, 512, 512, 512, 512, 256, 256),
-    "cnt": (1024, 1024, 1024, 512, 256, 256),
+    "add": ("mmmmmmddd",) * 3,
+    "cnt": (1024, 1024, 512, 1024, 512), "parts": (2560, 1536),
     "fl": (1024, 1024, 1024, 1024), "bl": (512, 512, 1024, 1024, 1024),
     "fs": (1025, 1024, 2048), "bs": (2048, 2048),
-    "fx": "ppp",
-    "cmp": ("ddddddddd",) * 3,
-    "mul": ("aaaaaaaaa",) * 3, "add": ("mmmmmmddd",) * 3, "look": ("dadadada",) * 3, "fg": ("aaaaaaaaa",) * 3,
-    "sc": 256,
-    "miss": ("dd", "dd", "dd"),
+    "fc": (512,) * 7 + (256, 256), "lc": (512,) * 8, "look": "dadadada",
+    "fh": (1024, 1024, 2048), "bh": (1024, 1024, 2048),
+    "sc": (256,) * 4, "cl": ((256,) * 4,) * 3, "wc": (256,) * 4, "ld": 512,
     "first": (1, 0, 0),
-    "parts": (3072, 1024), "cl": ((512, 512), (512, 512), (512, 512)), "yedma": 0, "acc": 1,
-    "oka": ("ad", "ad", "dd"), "yepe": 3, "yes": 256, "px": ("dda", "dda", "ddd"), "bx": "aaa", "clr": "s",
-    "pp": ((512, 512), (1024,)), "side": (1, 1), "fh": (1024, 1024, 2048), "bh": (1024, 1024, 2048),
-    "ld": 512, "wc": (512, 512),
-    "seed": 1, "tries": 150000, "heat": 1.0, "aim": 6, "packs": 300, "shake": 0.5, "reach": 10.0,
+    "oka": ("ad", "ad", "dd"), "yepe": 3, "yem": 3, "gee": 1, "late": 4096, "zed": 0, "yes": 256, "pp": ((512, 512), (1024,)), "zero": "aa", "rule": 0, "ahead": 0.1, "lazy": 0.0, "lag": (0, 0, 0), "hold": (1024, 1024),
+    "seed": 1, "tries": 400000, "heat": 1.0, "aim": 6, "wide": 120, "sweeps": 24, "soft": 0.3,
+    "packs": 300, "shake": 0.5, "reach": 10.0,
 }
 
 SCRATCH = {
     "f16": ("sbuf", [128, S], "bfloat16"), "b16": ("sbuf", [128, S], "bfloat16"),
     "nz0": ("sbuf", [128, S], "bfloat16"), "nz1": ("sbuf", [128, S], "bfloat16"),
-    "prm0": ("sbuf", [128, 8], "float32"), "prm1": ("sbuf", [128, 8], "float32"),
+    "prm0": ("sbuf", [128, 8], "float32"), "prm1": ("sbuf", [128, 8], "float32"), "prm2": ("sbuf", [128, 8], "float32"),
+    "prs1": ("sbuf", [128, 4], "float32"), "prs2": ("sbuf", [128, 4], "float32"),
     "pi32": ("sbuf", [128, 256], "int32"),
-    "pu0": ("sbuf", [128, 256], "uint16"), "pu1": ("sbuf", [128, 256], "uint16"),
-    "pf": ("sbuf", [128, S], "float32"), "snd": ("sbuf", [128, S], "float32"), "lf": ("sbuf", [128, S], "float32"),
+    "pu0": ("sbuf", [128, 256], "uint16"), "pu1": ("sbuf", [128, 256], "uint16"), "pu2": ("sbuf", [128, 256], "uint16"),
+    "pf": ("sbuf", [128, S], "float32"), "snd": ("sbuf", [128, S], "float32"),
+    "lf": ("sbuf", [128, S], "float32"), "lb": ("sbuf", [128, S], "float32"), "nb": ("sbuf", [128, S], "float32"),
     "win": ("sbuf", [128, 2 * K + 3 * S], "float32"), "dd": ("sbuf", [128, K], "float32"),
-    "ab": ("sbuf", [128, 2048], "float32"), "sg": ("sbuf", [128, 2048], "bfloat16"),
-    "miss": ("sbuf", [128, K], "bfloat16"),
+    "ab": ("sbuf", [128, 2048], "float32"), "miss": ("sbuf", [128, K], "bfloat16"),
     "wf": ("sbuf", [128, K + 16], "bfloat16"), "wb": ("sbuf", [128, K + 16], "bfloat16"),
     "sf": ("sbuf", [128, K + 16], "bfloat16"), "sb": ("sbuf", [128, K + 16], "bfloat16"),
-    "xf": ("sbuf", [128, K], "bfloat16"), "xl": ("sbuf", [128, K], "bfloat16"), "xb": ("sbuf", [128, S], "bfloat16"),
+    "xl": ("sbuf", [128, K], "bfloat16"),
     "cw": ("sbuf", [128, CWN], "bfloat16"), "cn": ("sbuf", [128, 2048], "bfloat16"), "cmp": ("sbuf", [128, 2048], "bfloat16"),
     "hit": ("sbuf", [128, 2048], "bfloat16"),
-    "hh": ("sbuf", [128, 2048], "float32"), "uu": ("sbuf", [128, 2048], "float32"),
-    "tt": ("sbuf", [128, 2048], "float32"), "yo": ("sbuf", [128, S], "float32"),
+    "hh": ("sbuf", [128, 2048], "float32"), "uu": ("sbuf", [128, 2048], "float32"), "yo": ("sbuf", [128, S], "float32"),
     "wt": ("sbuf", [128, 144], "bfloat16"), "sm": ("sbuf", [128, 1024], "float32"),
-    "lb": ("sbuf", [128, 128], "bfloat16"), "sv": ("sbuf", [128, 128], "bfloat16"), "sl": ("sbuf", [128, 8], "uint16"),
-    "okw": ("sbuf", [128, 256], "bfloat16"), "okb": ("sbuf", [128, 256], "bfloat16"), "el": ("sbuf", [128, 280], "bfloat16"),
-    "oks": ("sbuf", [128, 256], "bfloat16"),
+    "low": ("sbuf", [128, 128], "bfloat16"), "sv": ("sbuf", [128, 128], "bfloat16"), "sl": ("sbuf", [128, 8], "uint16"),
+    "okw": ("sbuf", [128, 256], "bfloat16"), "okb": ("sbuf", [128, 256], "bfloat16"), "oks": ("sbuf", [128, 256], "bfloat16"),
+    "el": ("sbuf", [128, 280], "bfloat16"),
     "al": ("sbuf", [128, 256], "uint16"), "jl": ("sbuf", [128, 256], "uint16"),
-    "al2": ("sbuf", [128, 256], "uint16"), "jl1": ("sbuf", [128, 256], "uint16"), "fb1": ("sbuf", [128, 128], "float32"),
-    "prm2": ("sbuf", [128, 8], "float32"), "prm3": ("sbuf", [128, 8], "float32"),
+    "al2": ("sbuf", [128, 256], "uint16"), "jl1": ("sbuf", [128, 256], "uint16"),
+    "fbu": ("sbuf", [128, 64], "float32"), "fb1": ("sbuf", [128, 64], "float32"),
     "emp": ("sbuf", [128, 128], "float32"), "pl": ("sbuf", [128, 36], "uint16"), "pv": ("sbuf", [128, 272], "bfloat16"),
     "ix": ("sbuf", [128, 128], "float32"), "il": ("sbuf", [128, 128], "uint16"),
-    "sel": ("sbuf", [128, 144], "bfloat16"), "seln": ("sbuf", [128, 144], "bfloat16"),
+    "sel": ("sbuf", [128, 144], "bfloat16"), "sls": ("sbuf", [128, 144], "bfloat16"),
     "sla": ("sbuf", [128, 144], "bfloat16"), "slb": ("sbuf", [128, 144], "bfloat16"),
-    "slc": ("sbuf", [128, 144], "bfloat16"), "sld": ("sbuf", [128, 160], "bfloat16"),
+    "slc": ("sbuf", [128, 144], "bfloat16"), "sld": ("sbuf", [128, 144], "bfloat16"),
     "blk": ("sbuf", [128, 128], "bfloat16"), "tri": ("sbuf", [128, 256], "bfloat16"),
-    "q": ("sbuf", [128, 144], "float32"), "qb": ("sbuf", [128, 144], "bfloat16"),
+    "eye": ("sbuf", [128, 128], "float32"), "eyb": ("sbuf", [128, 128], "bfloat16"),
     "top": ("sbuf", [128, 256], "float32"), "topb": ("sbuf", [128, 256], "bfloat16"),
     "off": ("sbuf", [128, 72], "bfloat16"), "one": ("sbuf", [128, 72], "float32"),
-    "zer": ("sbuf", [128, 2048], "bfloat16"), "dec": ("sbuf", [128, 2064], "bfloat16"),
+    "zer": ("sbuf", [128, 2064], "bfloat16"), "dec": ("sbuf", [128, 4112], "bfloat16"),
+    "big": ("sbuf", [128, 256], "bfloat16"), "nl": ("sbuf", [128, 128], "float32"),
     "kk": ("sbuf", [128, 128], "bfloat16"), "fb": ("sbuf", [128, 128], "float32"),
     "kd": ("sbuf", [128, 48], "float32"), "cv": ("sbuf", [128, 256], "bfloat16"),
     "ri": ("sbuf", [128, 8], "int32"), "rc": ("sbuf", [128, 16], "float32"),
     "ps": ("psum", [128, 4096], "float32"),
 }
-NDMA = 70
-SEMAPHORES = ["pe", "dve", "act", "pool"] + ["x%d" % i for i in range(30)] + ["d%d" % i for i in range(NDMA)]
+NDMA = 110
+SEMAPHORES = ["pe", "dve", "act", "pool"] + ["x%d" % i for i in range(24)] + ["d%d" % i for i in range(NDMA)]
 PLAN = {}
 
 
@@ -115,7 +114,12 @@ def rank_program(g, core, T, topo):
                 w += regions([v[0]])
             else:
                 w += regions([v])
-        ops.append({"q": q, "fn": fn, "r": r, "w": w, "kind": kind, "sem": sem, "cost": cost})
+        ops.append({"q": q, "fn": fn, "r": r, "w": w, "kind": kind, "sem": sem, "cost": cost, "rank": tuple(now)})
+
+    now = [0, 0]
+
+    def phase(k, at=0):
+        now[:] = [k, at]
 
     def price(out, ins, per=1.0, fast=False):
         if len(out) == 2:
@@ -126,9 +130,9 @@ def rank_program(g, core, T, topo):
             per = 0.5
         return ("c", max(64.0, per * size(out)))
 
-    def ts(out, a, s1, s2, o0, o1=None, also=None):
+    def ts(out, a, s1, s2, o0, o1=None):
         if o1 is None:
-            rec("dve", lambda: g.vector.tensor_scalar(ap(out), ap(a), ap(s1), None, o0), [a, s1, also], [out], price(out, [a], 1.0, True))
+            rec("dve", lambda: g.vector.tensor_scalar(ap(out), ap(a), ap(s1), None, o0), [a, s1], [out], price(out, [a], 1.0, True))
         else:
             rec("dve", lambda: g.vector.tensor_scalar(ap(out), ap(a), ap(s1), ap(s2), o0, o1), [a, s1, s2], [out], price(out, [a], 1.0, True))
 
@@ -172,33 +176,35 @@ def rank_program(g, core, T, topo):
         eng = {"sp": g.sync, "act": g.scalar, "pool": g}[q]
         rec(q, lambda: eng.dma_start(ap(out), src), [], [out], ("dma", 128 * size(out) * width(out)), "dma")
 
-    def store(q, dst, a):
-        eng = g.sync if q == "sp" else g.scalar
-        rec(q, lambda: eng.dma_start(dst, ap(a)), [a], [], ("dma", 128 * size(a) * width(a)), "dma")
+    def store(dst, a):
+        rec("sp", lambda: g.sync.dma_start(dst, ap(a)), [a], [], ("dma", 128 * size(a) * width(a)), "dma")
 
     def move(out, a):
         rec("sp", lambda: g.sync.dma_start(ap(out), ap(a)), [a], [out], ("dma", 128 * size(a) * width(a)), "dma")
 
+    def turn(out, a, by):
+        def piece(src, dst, m, mark):
+            rec("sp", lambda: g.sync.dma_start(T[out[0]][dst:dst + m, out[1]:out[2]], T[a[0]][src:src + m, a[1]:a[2]]),
+                [a], [out], ("dma", m * size(a) * width(a)), "dma")
+            ops[-1]["rows"] = mark
+        sent[1] += 1
+        piece(0, by % 128, 128 - by % 128, sent[1])
+        piece(128 - by % 128, 0, by % 128, sent[1])
+
     def adds(out, a):
         rec("pool", lambda: g.dma_start(ap(out), ap(a), accum_op=OP.add), [a, out], [out], ("dma", 256 * size(a) * width(a)), "dma")
 
-    def send(dst_rank, out, a, rsem):
-        dst = T.cores[dst_rank % n]
-        rid, pid, _ = topo.addr(dst)
-        m = topo.mask(core, dst)
-        rec("pool", lambda ls: g.remote_dma(ap(out), ap(a), T.sem[rsem], ls, pid, rid, m), [a], [],
-            ("dma", 128 * size(a) * width(a)), "remote", (rsem, len(topo.engines(core, dst))))
-
-    def arrives(src_rank, out, rsem):
-        rec("ext", None, [], [out], ("c", 0.0), "ext", (rsem, len(topo.engines(T.cores[src_rank % n], core))))
-
-    sent = [0]
+    sent = [0, 0]
 
     def hand(by, out, a):
         rsem = "x%d" % sent[0]
         sent[0] += 1
-        send(rank + by, out, a, rsem)
-        arrives(rank - by, out, rsem)
+        dst = T.cores[(rank + by) % n]
+        rid, pid, _ = topo.addr(dst)
+        m = topo.mask(core, dst)
+        rec("pool", lambda ls: g.remote_dma(ap(out), ap(a), T.sem[rsem], ls, pid, rid, m), [a], [],
+            ("dma", 128 * size(a) * width(a)), "remote", (rsem, len(topo.engines(core, dst))))
+        rec("ext", None, [], [out], ("c", 0.0), "ext", (rsem, len(topo.engines(T.cores[(rank - by) % n], core))))
 
     def cuts(sizes):
         out, lo = [], 0
@@ -210,11 +216,8 @@ def rank_program(g, core, T, topo):
     def SEL(u, name="sel"):
         return V(name, 15 - u, 143 - u)
 
-    def rows(out, name, lo, hi, step=16):
-        mm([(out, SEL(u), V(name, lo + u * step // 16, hi, step), u == 0, u == 15) for u in range(16)])
-
-    def cut(eng, out, a):
-        either(eng, lambda: act(out, a, AF.Relu, 0.0, SCL), lambda: ts(out, a, SCL, 0.0, OP.mult, OP.max))
+    def rows(out, name, lo, hi, by="sel"):
+        mm([(out, SEL(u, by), V(name, lo + u, hi, 16), u == 0, u == 15) for u in range(16)])
 
     def either(eng, on_act, on_dve):
         for fn in ((on_dve, on_act) if eng == "a" else (on_act, on_dve)):
@@ -222,142 +225,146 @@ def rank_program(g, core, T, topo):
         alt = ops.pop(-2)
         ops[-1]["alt"] = {k: alt[k] for k in ("q", "fn", "cost")}
 
+    def cut(eng, out, a):
+        either(eng, lambda: act(out, a, AF.Relu, 0.0, SCL), lambda: ts(out, a, SCL, 0.0, OP.mult, OP.max))
+
     def copy(eng, out, a):
         either(eng, lambda: act(out, a, AF.Copy), lambda: cp(out, a))
+
+    def shift(eng, out, a, s):
+        either(eng, lambda: act(out, a, AF.Identity, s), lambda: ts(out, a, s, None, OP.add))
 
     def scale(eng, out, a, s):
         either(eng, lambda: act(out, a, AF.Identity, 0.0, s), lambda: ts(out, a, s, None, OP.mult))
 
     T_LT, T_GE = V("tri", 0, 128), V("tri", 128, 256)
-    I_B, SH_B, I_F, SH_F = V("qb", 16, 144), V("qb", 0, 128), V("q", 16, 144), V("q", 0, 128)
+    I_B, I_F = V("eyb", 0, 128), V("eye", 0, 128)
     ROW, IS0, DEC, SCL = (V("rc", i, i + 1) for i in (4, 5, 6, 7))
+    PARTS = cuts(KN["parts"])
 
     load("sp", V("prm0", 0, 3), T.obs[:])
     load("sp", V("prm0", 3, 4), T.eps[:])
     for nm, src in (("b16", T.b0), ("f16", T.f0)):
         for lo in range(0, S, KN["ld"]):
             load("act", V(nm, lo, lo + KN["ld"]), src[:, lo:lo + KN["ld"]])
+    load("sp", V("pi32", 0, 256), T.pi[:])
     load("sp", V("prm0", 4, 5), T.lam[:])
     load("sp", V("prm0", 5, 6), T.rf[:])
     load("sp", V("prm0", 6, 7), T.rb[:])
-    load("sp", V("pi32", 0, 256), T.pi[:])
     load("sp", V("nz0", 0, S), T.nz[:])
 
     ms(V("sel", 0, 144), 0.0)
     ms(V("blk", 0, 128), 1.0)
-    ms(V("q", 0, 144), 0.0)
     iota(V("ri", 0, 1), [[0, 1]], 0, 1, small=False)
     sel(V("sel", 15, 143, 16), V("blk", 0, 8), [[-16, 8]], OP.is_ge, 0.0, 0, 1)
     sel(V("sel", 15, 143, 16), V("sel", 15, 143, 16), [[16, 8]], OP.is_ge, 0.0, 15, -1)
+    sel(I_B, V("blk", 0, 128), [[-1, 128]], OP.is_equal, 0.0, 0, 1)
     sel(V("topb", 0, 128), V("blk", 0, 128), [[-16, 8], [0, 16]], OP.is_equal, 0.0, 0, 1)
     sel(V("blk", 0, 128), V("blk", 0, 128), [[-16, 8], [0, 16]], OP.is_ge, 0.0, 0, 1)
     sel(V("blk", 0, 128), V("blk", 0, 128), [[16, 8], [0, 16]], OP.is_ge, 0.0, 15, -1)
     sel(T_LT, V("blk", 0, 128), [[1, 128]], OP.is_gt, 0.0, 0, -1)
     sel(T_GE, V("blk", 0, 128), [[-1, 128]], OP.is_ge, 0.0, 0, 1)
-    sel(V("q", 0, 144), V("q", 0, 144), [[1, 144]], OP.not_equal, 1.0, -16, -1)
-    sel(V("q", 0, 16), V("q", 0, 16), [[1, 16]], OP.not_equal, 1.0, 112, -1)
     iota(V("kk", 0, 128), [[0, 2], [0, 4], [1, 16]], 0, 0)
     iota(V("kk", 64, 128), [[1, 64]], 0, 0)
-    PARTS = cuts(KN["parts"])
     for a, b in PARTS:
         iota(V("cv", a // 16, b // 16), [[1, (b - a) // 256], [(b - a) // 256, 16]], a // 16, 0)
-    iota(V("fb", 0, 64), [[64, 64]], K, 0)
+    iota(V("fb", 0, 64), [[64, 64]], K - JUNK * KN["gee"], 0)
+    if KN["gee"]:
+        iota(V("nl", 0, 128), [[1, 2], [32, 64]], 0, 0)
     iota(V("kd", 0, 48), [[0, 2], [1, 24]], K + 1, 0)
     load("pool", V("win", BA, BA + S), T.b0[:])
-    for lo in range(0, 2048, 1024):
-        ms(V("zer", lo, lo + 1024), 0.0)
-    for nm in ("wb", "wf"):
+    for lo, hi in ((0, 1040), (1040, 2064)):
+        ms(V("zer", lo, hi), 0.0)
+    for nm, how in zip(("wb", "wf"), KN["zero"]):
         move(V(nm, 0, 2048), V("zer", 0, 2048))
-        for lo, hi in ((2048, 3072), (3072, K + 16)):
-            ms(V(nm, lo, hi), 0.0)
+        if how == "m":
+            move(V(nm, 2048, K + 16), V("zer", 0, 2064))
+        else:
+            for lo, hi in ((2048, 3072), (3072, K + 16)):
+                copy(how, V(nm, lo, hi), V("zer", 0, hi - lo))
     move(V("cw", 0, 2048), V("zer", 0, 2048))
     ms(V("one", 0, 64), 1.0)
     ms(V("one", 64, 65), 2.0 ** -12)
     ms(V("wt", 0, 144), 128.0)
     ms(V("off", 0, 72), -2048.0)
-    cp(V("qb", 0, 144), V("q", 0, 144))
-    cp(V("top", 0, 128), V("topb", 0, 128))
-    tt(V("top", 128, 256), I_F, V("top", 0, 128), OP.subtract)
-    cp(V("topb", 128, 256), V("top", 128, 256))
-    if "a" in "".join(KN["miss"]):
-        ts(V("seln", 0, 144), V("sel", 0, 144), -1.0, None, OP.mult)
+    copy("a", I_F, I_B)
+    copy("a", V("top", 0, 128), V("topb", 0, 128))
+    tt(V("topb", 128, 256), I_B, V("topb", 0, 128), OP.subtract)
+    copy("a", V("top", 128, 256), V("topb", 128, 256))
     ts(V("ri", 4, 5), V("ri", 0, 1), 15, None, OP.bitwise_and)
     cp(ROW, V("ri", 4, 5))
     ts(IS0, ROW, 0.0, None, OP.is_equal)
     ts(DEC, IS0, -1.0, None, OP.add)
     ts(SCL, IS0, 17.0, -1.0, OP.mult, OP.add)
     for lo, hi in ((0, 1024), (1024, 2048), (2048, 2064)):
-        ts(V("dec", lo, hi), V("zer", 0, hi - lo), DEC, None, OP.add)
+        shift("a", V("dec", lo, hi), V("zer", 0, hi - lo), DEC)
+    if max(KN["bs"] + KN["fs"]) > 2064:
+        move(V("dec", 2064, 4112), V("dec", 0, 2048))
     ts(V("kk", 0, 64), V("kk", 0, 64), ROW, -8192.0, OP.not_equal, OP.mult)
-    ts(V("kk", 64, 128), V("kk", 64, 128), IS0, None, OP.mult)
-    if "p" in KN["fx"]:
-        ts(V("slb", 0, 144), V("sel", 0, 144), SCL, None, OP.mult)
-        ts(V("slc", 0, 144), V("sel", 0, 144), DEC, None, OP.mult)
-        ms(V("sld", 144, 160), 0.0)
-        ts(V("sld", 0, 144), V("slc", 0, 144), -1.0, None, OP.mult)
-        tt(V("sla", 0, 144), V("slb", 0, 144), V("sld", 1, 145), OP.add)
-    ts(V("prm0", 7, 8), V("prm0", 3, 4), -1.0, None, OP.mult, also=V("prm0", 4, 7))
+    scale("a", V("kk", 64, 128), V("kk", 64, 128), IS0)
+    scale("a", V("slb", 0, 144), V("sel", 0, 144), SCL)
+    scale("a", V("slc", 0, 144), V("sel", 0, 144), DEC)
+    scale("a", V("sld", 0, 144), V("slc", 0, 144), -1.0)
+    copy("a", V("sla", 0, 144), V("slb", 0, 144))
+    copy("a", V("sla", 14, 142, 16), V("sld", 15, 143, 16))
     cp(V("pu0", 0, 256), V("pi32", 0, 256))
+    phase(2, 1)
+    copy("a", V("sls", 16, 144), V("sel", 0, 128))
+    copy("a", V("sls", 0, 16), V("sel", 112, 128))
+    copy("a", V("sls", 143, 144), V("sel", 0, 1))
+    turn(V("pu2", 0, 256), V("pu0", 0, 256), -16)
+    turn(V("prs2", 0, 4), V("prm0", 0, 4), -16)
+    hand(1, V("prs1", 0, 4), V("prs2", 0, 4))
+    hand(1, V("pu1", 0, 256), V("pu2", 0, 256))
     hand(-1, V("nz1", 0, S), V("nz0", 0, S))
-    hand(-1, V("prm1", 0, 8), V("prm0", 0, 8))
-    hand(1 if KN["side"][0] else -1, V("pu1", 0, 256), V("pu0", 0, 256))
-    if KN["side"][0]:
-        hand(1, V("prm2", 0, 8), V("prm0", 0, 8))
-    if KN["side"][1]:
-        hand(2, V("prm3", 0, 8), V("prm0", 0, 8))
+    hand(-1, V("prm1", 0, 7), V("prm0", 0, 7))
+    hand(2, V("prm2", 0, 4), V("prm0", 0, 4))
     ms(V("rc", 3, 4), 7.5)
     ms(V("el", 0, 280), 0.0)
     ms(V("emp", 0, 128), 1.0)
-    ts(V("rc", 0, 1), ROW, 4.0, None, OP.mult)
-    ts(V("rc", 1, 2), ROW, 17.0, None, OP.mult)
+    scale("a", V("rc", 0, 1), ROW, 4.0)
+    scale("a", V("rc", 1, 2), ROW, 17.0)
     ts(V("rc", 2, 3), ROW, 15.0, None, OP.is_lt)
-    ts(V("rc", 8, 9), IS0, 1024.0, None, OP.mult)
-    ts(V("pv", 256, 272), V("zer", 0, 16), V("rc", 8, 9), None, OP.add)
-    ts(V("cv", 0, 256), V("cv", 0, 256), IS0, None, OP.mult)
-    ts(V("fb", 0, 64), V("fb", 0, 64), V("rc", 0, 1), None, OP.add)
-    ts(V("kd", 0, 48), V("kd", 0, 48), V("rc", 1, 2), None, OP.add)
+    scale("a", V("rc", 8, 9), IS0, 1024.0)
+    shift("a", V("pv", 256, 272), V("zer", 0, 16), V("rc", 8, 9))
+    scale("a", V("cv", 0, 256), V("cv", 0, 256), IS0)
+    shift("a", V("fb", 0, 64), V("fb", 0, 64), V("rc", 0, 1))
+    if KN["gee"]:
+        scale("a", V("rc", 10, 11), ROW, 2.0)
+        shift("a", V("nl", 0, 128), V("nl", 0, 128), V("rc", 10, 11))
+    if KN["zed"]:
+        scale("a", V("big", 0, 128), I_B, 8192.0)
+        scale("a", V("big", 128, 256), I_B, -8192.0)
+    shift("a", V("kd", 0, 48), V("kd", 0, 48), V("rc", 1, 2))
     z = 24 * (len(PARTS) - 1) + KN["parts"][-1] // 256
-    ts(V("kd", z, z + 1), V("kd", z, z + 1), V("rc", 2, 3), None, OP.mult)
+    scale("a", V("kd", z, z + 1), V("kd", z, z + 1), V("rc", 2, 3))
 
     def who(t):
         k = "1" if t == 1 else "0"
         pr = "prm" + k
-        return {"y": V(pr, t, t + 1), "eps": V(pr, 3, 4), "lam": V(pr, 4, 5), "r": (V(pr, 5, 6), V(pr, 6, 7)),
-                "neps": V(pr, 7, 8), "nz": "nz" + k, "pu": "pu" + k}
-
-    def far(t, h):
-        return t + h == 2 and t > 0 and h == 2 - t and KN["side"][t - 1]
+        return {"y": V(pr, t, t + 1), "eps": V(pr, 3, 4), "lam": V(pr, 4, 5), "r": (V(pr, 5, 6), V(pr, 6, 7)), "nz": "nz" + k}
 
     def starts(t, h, pool, bk, bk2):
-        p, how = who(t), KN["miss"][t][h]
-        if far(t, h):
-            pr = "prm%d" % (t + 1)
-            p = {"y": V(pr, t, t + 1), "eps": V(pr, 3, 4), "neps": V(pr, 7, 8)}
+        pr = (("prm0", "prm0"), ("prm1", "prs1"), ("prm2", "prs2"))[t][h]
         for lo, hi in cuts(KN["wc"]):
-            a, s, x = (V(nm, S * h + lo, S * h + hi) for nm in ("ab", "sg", "hit"))
-            act(a, W(pool, lo, hi), AF.Abs, p["y"], -1.0)
-            if how == "d":
-                ts(x, a, p["eps"], 0.25, OP.is_le, OP.mult)
-            else:
-                act(s, a, AF.Sign, p["neps"], 1.0)
-                if how == "a":
-                    act(x, s, AF.Relu, 0.0, 0.25)
-                else:
-                    ts(x, s, 0.5, 0.25, OP.is_lt, OP.mult)
-        neg = how == "a"
-        mm([(P(bk, 0, 64), SEL(u, "seln" if neg else "sel"), V("hit", S * h + u, S * h + S, 16), u == 0, u == 15) for u in range(16)])
+            a, x = (V(nm, S * h + lo, S * h + hi) for nm in ("ab", "hit"))
+            act(a, W(pool, lo, hi), AF.Abs, V(pr, t, t + 1), -1.0)
+            ts(x, a, V(pr, 3, 4), 0.25, OP.is_le, OP.mult)
+        if t and h == KN["first"][t - 1]:
+            ops[-1]["w"].append(("hold", t - 1, t))
+        rows(P(bk, 0, 64), "hit", S * h, S * h + S)
         o, w, c = 512 * h, 72 * h, 64 * h
         C, CT, RHO = V("sm", o, o + 64), V("sm", o + 64, o + 65), V("sm", o + 72, o + 73)
         E, Q, E0, M = (V("sm", o + z, o + z + 64) for z in (128, 192, 256, 320))
-        L, vals, sl = V("lb", c, c + 64), V("sv", c, c + 64), V("sl", 4 * h, 4 * h + 4)
+        L, vals, sl = V("low", c, c + 64), V("sv", c, c + 64), V("sl", 4 * h, 4 * h + 4)
         mm([(P(bk2, 0, 65), I_B, V("off", 0, 65), True, False)])
-        ts(V("wt", w + 1, w + 65), P(bk, 0, 64), 131.625 if neg else 127.625, 129.0, OP.add, OP.max)
+        ts(V("wt", w + 1, w + 65), P(bk, 0, 64), 127.625, 129.0, OP.add, OP.max)
         mm([(P(bk2, 0, 65), T_LT, V("wt", w + 1, w + 66), False, False), (P(bk2, 0, 65), T_GE, V("wt", w, w + 65), False, True)])
         scan(V("sm", o, o + 65), P(bk2, 0, 65), V("one", 0, 65), 0.0, OP.add, OP.mult)
         rec("dve", lambda: g.vector.reciprocal(ap(RHO), ap(CT)), [CT], [RHO], ("c", 230.0))
         ts(E, C, RHO, MAGIC, OP.mult, OP.add)
         ts(Q, E, -MAGIC, CT, OP.add, OP.mult)
-        ts(E0, E, -MAGIC, None, OP.add)
+        shift("a", E0, E, V("rc", 9, 10))
         tt(L, Q, C, OP.is_lt)
         for out, z in ((P(bk2, 128, 192), 0), (P(bk, 128, 192), 1)):
             mm([(out, V("top", 128 * z, 128 * z + 128), E0, True, False), (out, I_B, V("kk", 64 * z, 64 * z + 64), False, False)])
@@ -368,74 +375,76 @@ def rank_program(g, core, T, topo):
         wn, sn = ("wf", "wb")[h], ("sf", "sb")[h]
         cp((V(wn, 0, K), sl), vals)
         for lo, hi in cuts(KN["bs" if h else "fs"]):
+            if lo and not h:
+                phase(10 * t + 3, lo - KN["lag"][0] - 1)
             scan(V(sn, lo, hi), V(wn, lo, hi), V("dec", 0, hi - lo), V(sn, lo - 1, lo) if lo else -1.0, OP.max, OP.add)
+    phase(0)
+    ms(V("rc", 9, 10), -MAGIC)
 
     def clear(t, h):
         if t < 2:
-            wn = ("wf", "wb")[h]
-            if KN["clr"] == "s":
-                cp((V(wn, 0, K), V("sl", 4 * h, 4 * h + 4)), V("zer", 0, 64))
-            else:
-                for lo in (0, 2048):
-                    move(V(wn, lo, lo + 2048), V("zer", 0, 2048))
+            phase(10 * t + 4, 1)
+            cp((V(("wf", "wb")[h], 0, K), V("sl", 4 * h, 4 * h + 4)), V("zer", 0, 64))
 
     def f_ancestors(t, pool):
-        how = KN["fx"][t]
-        for lo, hi in cuts(KN["fl"]):
-            out = P(4, lo // 16, hi // 16)
-            if how == "p":
-                mm([(out, SEL(u, "sla" if u else "slb"), V("sf", lo + u, hi, 16), u == 0, False) for u in range(16)]
-                   + [(out, SEL(15, "sld"), V("sf", lo + 16, hi + 1, 16), False, False)]
-                   + [(out, SEL(u, "slc"), V("wf", lo + u + 1, hi + 1, 16), False, u == 15) for u in range(16)])
-                ts(V("al", lo // 16, hi // 16), out, 15.0, None, OP.add)
-            else:
-                cut(how, V("xf", lo, hi), V("sf", lo, hi))
-                rows(out, "xf", lo, hi)
-                cp(V("al", lo // 16, hi // 16), out)
-        if far(t, 0):
+        for i, (lo, hi) in enumerate(cuts(KN["fl"])):
+            phase(10 * t + 3, lo - KN["lag"][0])
+            out = P((4, 2)[i % 2], lo // 16, hi // 16)
+            mm([(out, SEL(u, "sla" if u else "slb"), V("sf", lo + u, hi, 16), u == 0, False) for u in range(16)]
+               + [(out, SEL(15, "sld"), V("sf", lo + 16, hi + 1, 16), False, False)]
+               + [(out, SEL(u, "slc"), V("wf", lo + u + 1, hi + 1, 16), False, u == 15) for u in range(16)])
+            ts(V("al", lo // 16, hi // 16), out, 15.0, None, OP.add)
+        if t == 2:
             for lo, hi in cuts(KN["fh"]):
+                phase(10 * t + 3, lo - KN["lag"][0])
                 hand(2, V("al2", lo // 16, hi // 16), V("al", lo // 16, hi // 16))
         clear(t, 0)
-        for i, (lo, hi) in enumerate(cuts(KN["loop"])):
-            gat = (W(pool, 0, S), V("al2" if far(t, 0) else "al", lo // 16, hi // 16))
-            copy(KN["fg"][t][i], V("win", F0 + lo, F0 + hi), gat)
+        for lo, hi in cuts(KN["fc"]):
+            phase(10 * t + 3, lo - KN["lag"][2])
+            copy("a", V("win", F0 + lo, F0 + hi), (W(pool, 0, S), V("al2" if t == 2 else "al", lo // 16, hi // 16)))
 
     def b_ancestors(t, base):
-        p = who(t)
+        for i, (lo, hi) in enumerate(cuts(KN["bl"])):
+            for k, (a, b) in enumerate(cuts(KN["lc"])):
+                if lo <= a < hi:
+                    phase(10 * t + 3, lo - KN["lag"][1])
+                    cut(KN["look"][k], V("xl", a, b), (V("sb", 0, K), V("pu%d" % t, a // 16, b // 16)))
+            out = P((5, 3)[i % 2], lo // 16, hi // 16)
+            rows(out, "xl", lo, hi, "sls" if t else "sel")
+            cp(V("jl", lo // 16, hi // 16), out)
+        phase(10 * t + 3, 2048)
+        out = P(0, 256, 320)
+        mm([(out, SEL(u, nm), V(src, 4 * u + z, K, 64), u == 0 and nm == "slb", u == 15 and nm == "slc")
+            for nm, src, z in (("slb", "sb", 0), ("sld", "sb", 1), ("slc", "wb", 1)) for u in range(16)])
+        ts(V("fbu", 0, 64) if t else V("fb", 64, 128), out, base + 15.0 - JUNK * KN["gee"], None, OP.add)
         clear(t, 1)
-        for lo, hi in cuts(KN["bl"]):
-            for z in range(lo, hi, 512):
-                cut(KN["look"][t][z // 512], V("xl", z, z + 512), (V("sb", 0, K), V(p["pu"], z // 16, z // 16 + 32)))
-            rows(P(5, lo // 16, hi // 16), "xl", lo, hi)
-            cp(V("jl", lo // 16, hi // 16), P(5, lo // 16, hi // 16))
-        cut(KN["bx"][t], V("xb", 0, S), V("sb", 0, K, 4))
-        rows(P(5, 256, 320), "xb", 0, S)
-        ts(V("fb", 64, 128), P(5, 256, 320), float(base), None, OP.add)
-        if far(t, 1):
+        if t == 1:
             for lo, hi in cuts(KN["bh"]):
+                phase(10 * t + 3, lo - KN["lag"][1])
                 hand(-2, V("jl1", lo // 16, hi // 16), V("jl", lo // 16, hi // 16))
-            hand(-2, V("fb1", 64, 128), V("fb", 64, 128))
+            hand(-2, V("fb1", 0, 64), V("fbu", 0, 64))
+        phase(10 * t + 3, 2048)
+        if t:
+            turn(V("fb", 64, 128), V("fb1" if t == 1 else "fbu", 0, 64), 16)
 
     def pairs(t, pool):
         p = who(t)
         ends = {hi: lo for lo, hi in cuts(KN["cnt"])}
         for i, (lo, hi) in enumerate(cuts(KN["loop"])):
-            z, o = hi - lo, 512 * (i % 4)
+            phase(10 * t + 3, lo)
+            z, o = hi - lo, lo % 2048
             d, f, m, x = V("dd", lo, hi), V("win", F0 + lo, F0 + hi), V("win", lo, hi), V("miss", lo, hi)
-            a, s = V("ab", o, o + z), V("sg", o, o + z)
-            tt(d, (W(pool, 0, S), V("jl1" if far(t, 1) else "jl", lo // 16, hi // 16)), f, OP.subtract)
-            prod = P(i % 2, 0, z) if KN["add"][t][i] == "d" else m
-            scale(KN["mul"][t][i], prod, d, p["lam"])
+            tt(d, (W(pool, 0, S), V("jl1" if t == 1 else "jl", lo // 16, hi // 16)), f, OP.subtract)
             if KN["add"][t][i] == "d":
-                tt(m, f, prod, OP.add)
+                scale("a", P(i % 2, 0, z), d, p["lam"])
+                tt(m, f, P(i % 2, 0, z), OP.add)
             else:
+                scale("a", m, d, p["lam"])
                 adds(m, f)
-            act(a, m, AF.Abs, p["y"], -1.0)
-            if KN["cmp"][t][i] == "s":
-                act(s, a, AF.Sign, p["neps"], 1.0)
-                ts(x, s, 0.0, None, OP.max)
-            else:
-                ts(x, a, p["eps"], None, OP.is_gt)
+            act(V("ab", o, o + z), m, AF.Abs, p["y"], -1.0)
+            ts(x, V("ab", o, o + z), p["eps"], None, OP.is_gt)
+            if lo >= KN["late"]:
+                ops[-1]["r"].append(("cw", 0, 1))
             s = max(k for k in range(len(PARTS)) if PARTS[k][0] <= lo)
             a, b = PARTS[s]
             w = (b - a) // 16
@@ -457,9 +466,20 @@ def rank_program(g, core, T, topo):
         if s:
             mm([(P(5, 400 + s, 401 + s), V("blk", 0, 128), tot[k], k == 0, False) for k in range(s)])
         mm([(P(5, 400 + s, 401 + s), T_LT, tot[s], s == 0, True)])
-        tt(V("emp", o, o + nc), V("el", e, e + w, 16), V("el", e + 16, e + w + 1, 16), OP.is_equal)
-        tt(V("emp", o + 20, o + 20 + ne), V("emp", o, o + ne), V("kd", 24 * s, 24 * s + ne), OP.mult)
-        tt(V("emp", o + 40, o + 40 + ne), V("emp", o + 20, o + 20 + ne), V("el", e, e + 16 * ne - 15, 16), OP.add)
+        if last and KN["gee"]:
+            mm([(P(5, 404, 405), V("blk", 0, 128), tot[k], k == 0, k == s) for k in range(s + 1)])
+            ts(V("ix", 0, 128), V("nl", 0, 128), P(5, 404, 405), None, OP.is_ge)
+            tt(V("ix", 0, 128), V("ix", 0, 128), V("fb", 0, 128), OP.mult)
+        if KN["zed"]:
+            z = P(7 - 4 * s, 256, 256 + ne)
+            mm([(z, I_F, V("kd", 24 * s, 24 * s + ne), True, False)])
+            mm([(P(7 - 4 * s, 256, 256 + nc), V("big", 0, 128), V("el", e, e + w, 16), False, False),
+                (P(7 - 4 * s, 256, 256 + nc), V("big", 128, 256), V("el", e + 16, e + w + 1, 16), False, True)])
+            tt(V("emp", o + 40, o + 40 + ne), V("el", e, e + 16 * ne - 15, 16), z, OP.max)
+        else:
+            tt(V("emp", o, o + nc), V("el", e, e + w, 16), V("el", e + 16, e + w + 1, 16), OP.is_equal)
+            tt(V("emp", o + 20, o + 20 + ne), V("emp", o, o + ne), V("kd", 24 * s, 24 * s + ne), OP.mult)
+            tt(V("emp", o + 40, o + 40 + ne), V("emp", o + 20, o + 20 + ne), V("el", e, e + 16 * ne - 15, 16), OP.add)
         ts(V("pl", 18 * s, 18 * s + ne), V("emp", o + 40, o + 40 + ne), P(5, 400 + s, 401 + s), None, OP.add)
         if KN["oka"][t][s] == "a":
             act(V("oks", c, c + w), P(6 - 4 * s, c, c + w), AF.Sign, V("rc", 3, 4), -1.0)
@@ -472,69 +492,63 @@ def rank_program(g, core, T, topo):
         cp((V("cw", 0, CWN), V("pl", 18 * s, 18 * s + ne)), V("pv", c, c + 16 * ne))
 
     def places(t):
-        order = (KN["first"][t], 1 - KN["first"][t])
+        phase(10 * t + 4)
         for lo, hi in cuts(KN["pp"][0]):
             scan(V("cn", 2 * lo, 2 * hi), V("cw", 2 * lo, 2 * hi), V("dec", 0, 2 * (hi - lo)),
                  V("cn", 2 * lo - 1, 2 * lo) if lo else -1.0, OP.max, OP.add)
-            ops[-1]["mark"] = lo == 0
         if t < 2:
             move(V("cw", 0, 2048), V("zer", 0, 2048))
-        z = 0
-        for k, h in enumerate(order):
+        z = 2
+        for k, h in enumerate((KN["first"][t], 1 - KN["first"][t])):
             for lo, hi in cuts(KN["pp"][k]):
                 a, b = 64 * h + lo // 16, 64 * h + hi // 16
-                cut(KN["px"][t][z], V("cmp", S * h + lo, S * h + hi), V("cn", 2 * lo + h, 2 * hi, 2))
-                rows(P(2 + z, 0, b - a), "cmp", S * h + lo, S * h + hi)
-                tt(V("ix", a, b), V("fb1" if h and far(t, 1) else "fb", a, b), P(2 + z, 0, b - a), OP.min)
-                cp(V("il", a, b), V("ix", a, b))
+                cut("da"[k], V("cmp", S * h + lo, S * h + hi), V("cn", 2 * lo + h, 2 * hi, 2))
+                if KN["gee"]:
+                    mm([(P(z, 0, b - a), I_F, V("ix", a, b), True, False)])
+                    mm([(P(z, 0, b - a), SEL(u), V("cmp", S * h + lo + u, S * h + hi, 16), False, u == 15) for u in range(16)])
+                    cp(V("il", a, b), P(z, 0, b - a))
+                else:
+                    rows(P(z, 0, b - a), "cmp", S * h + lo, S * h + hi)
+                    tt(V("ix", a, b), V("fb", a, b), P(z, 0, b - a), OP.min)
+                    cp(V("il", a, b), V("ix", a, b))
                 z += 1
 
     def step(t, h, end, dst, done):
-        p, z = who(t), KN["sc"]
+        p = who(t)
         bk = 0 if h == KN["first"][t] else 2
-        shift = h == 1 and t < 2
-        for lo in range(0, S, z):
-            hi = lo + z
-            gat = (V("win", 0, end), V("il", 64 * h + lo // 16, 64 * h + hi // 16))
-            hh, uu, tv = (V(nm, S * h + lo, S * h + hi) for nm in ("hh", "uu", "tt"))
-            act(hh, gat, AF.Square)
-            tt(uu, gat, hh, OP.subtract)
-            if KN["acc"] and not shift:
-                if lo % 512 == 0:
-                    mm([(P(bk, lo, lo + 512), I_B, V("zer", 0, 512), True, False)])
-                scale("a", P(bk, lo, hi), uu, p["r"][h])
-                mm([(P(bk, lo, hi), I_B, V(p["nz"], lo, hi), False, hi % 512 == 0)])
-            else:
-                scale("a", tv, uu, p["r"][h])
-                mm([(P(bk, lo, hi), SH_F if shift else I_F, tv, True, False),
-                    (P(bk, lo, hi), SH_B if shift else I_B, V(p["nz"], lo, hi), False, True)])
-            for a, b in cuts(KN["cl"][t]):
-                if b == hi:
-                    ts(W(dst, a, b), P(bk, a, b), 0.0, 1.0, OP.max, OP.min)
-                    if t == 2 or b % 512 == 0:
-                        done(a if t == 2 else b - 512, b)
+        phase(10 * t + 5 + bk)
+        for a, b in cuts(KN["cl"][t]):
+            mm([(P(bk, a, b), I_B, V("zer", 0, b - a), True, False)])
+            for lo, hi in cuts(KN["sc"]):
+                if a <= lo < b:
+                    gat = (V("win", 0, end), V("il", 64 * h + lo // 16, 64 * h + hi // 16))
+                    hh, uu = (V(nm, S * h + lo, S * h + hi) for nm in ("hh", "uu"))
+                    act(hh, gat, AF.Square)
+                    tt(uu, gat, hh, OP.subtract)
+                    if h != KN["first"][t] and t < 2 and lo >= KN["hold"][t]:
+                        ops[-1]["r"].append(("hold", t, t + 1))
+                    scale("a", P(bk, lo, hi), uu, p["r"][h])
+                    mm([(P(bk, lo, hi), I_B, V(p["nz"], lo, hi), False, hi == b)])
+            ts(W(dst, a, b), P(bk, a, b), 0.0, 1.0, OP.max, OP.min)
+            if t == 2 or b % 512 == 0:
+                done(a if t == 2 else b - 512, b)
 
     def energy():
         npe, z = KN["yepe"], KN["yes"]
-        if KN["yedma"]:
-            for i in range(4):
-                for lo in range(0, S, 512):
-                    v = V("dd", S * i + lo, S * i + lo + 512)
-                    act(v, v, AF.Square)
-                    act(v, v, AF.Exp, 0.0, -1.0, 1500.0 if i + lo == 0 else 0.0)
-                if i % 2:
-                    adds(V("dd", S * i - S, S * i), V("dd", S * i, S * i + S))
-            store("sp", T.ye[:], V("dd", 0, S))
-            ops[-1]["w"].append(("ye", 0, S))
-            a = V("dd", 2 * S, 3 * S)
-            rec("pool", lambda: g.dma_start(T.ye[:], ap(a), accum_op=OP.add), [a], [], ("dma", 256 * 4 * S), "dma")
-            ops[-1]["w"].append(("ye", 0, S))
-            return
+        phase(26)
         for lo in range(0, S, 512):
             for i in range(4):
                 v = V("dd", S * i + lo, S * i + lo + 512)
-                act(v, v, AF.Square)
+                either("a", lambda: act(v, v, AF.Square), lambda: tt(v, v, v, OP.mult))
+                if i >= 4 - KN["yem"]:
+                    act(v, v, AF.Exp, 0.0, -1.0)
+                    adds(V("yo" if KN["yem"] < 3 else "dd", lo, lo + 512), v)
+                    if i == 3:
+                        store(T.ye[:, lo:lo + 512], V("yo" if KN["yem"] < 3 else "dd", lo, lo + 512))
+                    continue
                 act(P(4, lo, lo + 512) if i > npe else v, v, AF.Exp, 0.0, -1.0, 1500.0 if i + lo == 0 else 0.0)
+                if KN["yem"] == 3:
+                    continue
                 if i < npe:
                     w = z if i else 512
                     for a in range(lo, lo + 512, w):
@@ -544,7 +558,7 @@ def rank_program(g, core, T, topo):
                 else:
                     tt(V("yo", lo, lo + 512), V("yo", lo, lo + 512), P(4, lo, lo + 512), OP.add)
                 if i == 3:
-                    store("sp", T.ye[:, lo:lo + 512], V("yo", lo, lo + 512))
+                    store(T.ye[:, lo:lo + 512], V("yo", lo, lo + 512))
 
     def nothing(lo, hi):
         return None
@@ -555,28 +569,35 @@ def rank_program(g, core, T, topo):
         pairs(t, b)
         places(t)
 
+    phase(1)
     starts(0, 1, ("b16", 0), 6, 7)
+    phase(2)
     starts(0, 0, ("f16", 0), 2, 3)
     ancestors(0, ("f16", 0), ("b16", 0), BA)
 
     def b_goes(lo, hi):
-        hand(-2, V("win", BB + lo, BB + hi), V("snd", lo, hi))
-    step(0, 1, BB, ("snd", 0), b_goes)
-    step(0, 0, BA, ("pf", 0), nothing)
-    starts(1, 1, ("snd", 0) if far(1, 1) else ("win", BB), 6, 7)
-    starts(1, 0, ("pf", 0), 4, 5)
+        hand(-2, V("lb", lo, hi), V("snd", lo, hi))
+        turn(V("win", BB + lo, BB + hi), V("lb", lo, hi), 16)
+    for h in (KN["first"][0], 1 - KN["first"][0]):
+        if h:
+            step(0, 1, BB, ("snd", 0), b_goes)
+            starts(1, 1, ("snd", 0), 6, 7)
+        else:
+            step(0, 0, BA, ("pf", 0), nothing)
+            starts(1, 0, ("pf", 0), 4, 5)
     ancestors(1, ("pf", 0), ("win", BB), BB)
 
-    def f_goes(lo, hi):
-        hand(2, V("lf", lo, hi), V("snd", lo, hi))
-    step(1, 0, BA, ("snd", 0), f_goes)
-    step(1, 1, BC, ("win", BC), nothing)
-    starts(2, 0, ("snd", 0) if far(2, 0) else ("lf", 0), 6, 7)
-    starts(2, 1, ("win", BC), 4, 5)
+    for h in (KN["first"][1], 1 - KN["first"][1]):
+        if h:
+            step(1, 1, BC, ("nb", 0), lambda lo, hi: turn(V("win", BC + lo, BC + hi), V("nb", lo, hi), 16))
+            starts(2, 1, ("nb", 0), 4, 5)
+        else:
+            step(1, 0, BA, ("snd", 0), lambda lo, hi: hand(2, V("lf", lo, hi), V("snd", lo, hi)))
+            starts(2, 0, ("snd", 0), 6, 7)
     ancestors(2, ("lf", 0), ("win", BC), BC)
     energy()
-    step(2, 0, BA, ("pf", 0), lambda lo, hi: store("sp", T.yf[:, lo:hi], V("pf", lo, hi)))
-    step(2, 1, BC + S, ("snd", 0), lambda lo, hi: store("sp", T.yb[:, lo:hi], V("snd", lo, hi)))
+    step(2, 0, BA, ("pf", 0), lambda lo, hi: store(T.yf[:, lo:hi], V("pf", lo, hi)))
+    step(2, 1, BC + S, ("snd", 0), lambda lo, hi: store(T.yb[:, lo:hi], V("snd", lo, hi)))
 
     if "order" not in PLAN:
         PLAN["ops"] = ops
@@ -596,8 +617,9 @@ def depends(ops):
             deps.append([j for j in range(i) if ops[j]["kind"] == "remote" and ops[j]["sem"][0] == o["sem"][0]])
             continue
         bank = [x for x in o["r"] if x[0] == "ps"]
-        deps.append([j for j in range(i) if hits(o["r"], ops[j]["w"]) or hits(o["w"], ops[j]["w"]) or hits(o["w"], ops[j]["r"])
-                     or ((ops[j]["q"] != o["q"] or "alt" in o or "alt" in ops[j]) and hits(bank, ops[j]["r"]))])
+        deps.append([j for j in range(i) if ("rows" not in o or o["rows"] != ops[j].get("rows")) and (
+            hits(o["r"], ops[j]["w"]) or hits(o["w"], ops[j]["w"]) or hits(o["w"], ops[j]["r"])
+            or ((ops[j]["q"] != o["q"] or "alt" in o or "alt" in ops[j]) and hits(bank, ops[j]["r"])))])
     return deps
 
 
@@ -629,57 +651,86 @@ def arrange(ops, deps, seed, tries):
         for j in near[i]:
             after[j].append(i)
     q = [["dve", "act", "pe", "pool", "sp", "ext"].index(o["q"]) for o in ops]
+    waits = [[j for j in near[i] if q[i] != 2 or q[j] != 2] for i in range(n)]
     tms = [[times(o, m) for o in ops] for m in SPEEDS]
     tm = tms[0]
     tail = [0.0] * n
     for i in range(n - 1, -1, -1):
         tail[i] = tm[i][1] + max([tail[j] for j in after[i]] + [0.0])
-    left, ready, free, order = [len(d) for d in near], [0.0] * n, [0.0] * 6, []
-    pool = [[i for i in range(n) if q[i] == k and not left[i]] for k in range(6)]
+    over = set()
+
+    def turn_over(i):
+        over.symmetric_difference_update([i])
+        o = dict(ops[i], **ops[i]["alt"]) if i in over else ops[i]
+        q[i] = ["dve", "act"].index(o["q"])
+        for t, sp in zip(tms, SPEEDS):
+            t[i] = times(o, sp)
+    rank = [ops[i]["rank"] + (i,) if KN["rule"] else (-tail[i],) for i in range(n)]
+    left, ready, free, order, ring = [len(d) for d in near], [0.0] * n, [0.0] * 6, [], 0.0
+    pool = [i for i in range(n) if not left[i]]
     while len(order) < n:
         best = None
         for k in range(6):
-            if pool[k]:
-                t0 = max(free[k], min(ready[i] for i in pool[k]))
-                i = max((i for i in pool[k] if ready[i] <= t0 + 0.1), key=lambda j: tail[j])
-                t = max(free[k], ready[i])
+            mine = [i for i in pool if q[i] == k or (k < 2 and KN["rule"] and "alt" in ops[i])]
+            if mine:
+                t0 = max(free[k], min(ready[i] for i in mine))
+                i = min((i for i in mine if ready[i] <= t0 + KN["ahead"]), key=lambda j: (k == 0 and "alt" in ops[j] and KN["rule"], rank[j]))
+                t = max(free[k], ready[i]) + (KN["lazy"] if k == 0 and "alt" in ops[i] and KN["rule"] else 0.0)
                 if best is None or t < best[0]:
-                    best = (t, i)
-        t, i = best
-        pool[q[i]].remove(i)
+                    best = (t, i, k)
+        t, i, k = best
+        if q[i] != k:
+            turn_over(i)
+        t = max(free[k], ready[i])
+        pool.remove(i)
         order.append(i)
-        free[q[i]] = t + tm[i][0]
+        free[k] = t + tm[i][0]
+        end = t + tm[i][1]
+        if tm[i][2]:
+            ring = end = max(ring + tm[i][2], end)
         for j in after[i]:
-            ready[j] = max(ready[j], t + tm[i][1])
+            ready[j] = max(ready[j], end)
             left[j] -= 1
             if not left[j]:
-                pool[q[j]].append(j)
+                pool.append(j)
 
-    def span(part, tm, done, free, start):
-        free, total = list(free), 0.0
+    def behind(later, tm):
+        way, last = [0.0] * n, [0.0] * 7
+        for j in reversed(later):
+            a, b, c = tm[j]
+            d = max([way[s] for s in after[j]] + [last[6] if c else 0.0])
+            way[j] = last[q[j]] = max(a + last[q[j]], b + d)
+            if c:
+                last[6] = c + d
+        return [max([way[s] for s in after[i]] + [0.0]) for i in range(n)], last
+
+    def span(part, tm, done, free, start, rest=([0.0] * n, [0.0] * 7)):
+        free, total, end, out = list(free), 0.0, 0.0, rest[0]
         for i in part:
             k = q[i]
             t = free[k]
-            for j in near[i]:
+            for j in waits[i]:
                 if done[j] > t:
                     t = done[j]
             a, b, c = tm[i]
             start[i] = t
             free[k] = t + a
             if c:
-                free[6] = done[i] = max(free[6] + c, t + b)
+                free[6] = done[i] = t = max(free[6] + c, t + b)
             else:
-                done[i] = t + b
-            total += done[i]
-        end = done[part[-1]] if ops[part[-1]].get("mark") else max(free)
-        return end + 0.1 * total / len(part) + 0.5 * sum(max(0.0, f - end) for f in free[:3]), free, end
+                done[i] = t = t + b
+            total += t
+            if t + out[i] > end:
+                end = t + out[i]
+        end = max([end] + [f + r for f, r in zip(free, rest[1])])
+        return end + KN["soft"] * total / len(part), free, end
 
-    def critical(part, tm, done, free):
+    def critical(part, tm, done, free, rest):
         free, prev, why = list(free), [None] * 7, {}
         for i in part:
             k = q[i]
             t, w = free[k], (prev[k], True)
-            for j in near[i]:
+            for j in waits[i]:
                 if done[j] > t:
                     t, w = done[j], (j, False)
             a, b, c = tm[i]
@@ -691,7 +742,7 @@ def arrange(ops, deps, seed, tries):
                 prev[6] = i
             else:
                 done[i] = t + b
-        i = part[-1] if ops[part[-1]].get("mark") else max(part, key=lambda j: done[j])
+        i = max([(done[j] + rest[0][j], j) for j in part] + [(free[k] + rest[1][k], prev[k]) for k in range(7) if prev[k] is not None])[1]
         pairs = []
         while i in why:
             j, same = why[i]
@@ -725,8 +776,7 @@ def arrange(ops, deps, seed, tries):
         c = [span(seq, t, [0.0] * n, [0.0] * 7, [0.0] * n)[2] for t in tms]
         return c[0] + sum(c)
 
-    best, key = (worth(order), order), {i: float(z) for z, i in enumerate(order)}
-    base = None
+    best, key, base = (worth(order), order), {i: float(z) for z, i in enumerate(order)}, None
     for k in range(KN["packs"]):
         if base is not None:
             key = list(base)
@@ -749,23 +799,18 @@ def arrange(ops, deps, seed, tries):
             best, base = (c, seq), at
     order = best[1]
     head = [i for i in range(n) if ops[i]["kind"] == "dma" and not near[i] and q[i] != 3]
-    order = [i for i in order if i not in head]
-    ends = [0] + [z + 1 for z, i in enumerate(order) if ops[i].get("mark")] + [len(order)]
+    order = head + [i for i in order if i not in head]
     start, dones = [0.0] * n, [[0.0] * n for _ in tms]
-    frees = [span(head, t, d, [0.0] * 7, start)[1] for t, d in zip(tms, dones)]
-    out, over = list(head), set()
-
-    def turn_over(i):
-        over.symmetric_difference_update([i])
-        o = dict(ops[i], **ops[i]["alt"]) if i in over else ops[i]
-        q[i] = ["dve", "act"].index(o["q"])
-        for t, sp in zip(tms, SPEEDS):
-            t[i] = times(o, sp)
-    for lo, hi in zip(ends, ends[1:]):
+    wide, sweeps = KN["wide"], KN["sweeps"]
+    windows = [(s, max(len(head), lo), min(n, lo + wide)) for s in range(sweeps)
+               for lo in range(len(head) - s % 2 * wide // 2, n, wide)]
+    for sweep, lo, hi in windows:
         part = order[lo:hi]
-        m = len(part) - (1 if ops[part[-1]].get("mark") else 0)
-        now = [span(part, t, d, f, start)[0] for t, d, f in zip(tms, dones, frees)]
-        turns, tight, top = tries * m // n, None, (now[0] + sum(now), part, set(over))
+        m = len(part)
+        frees = [span(order[:lo], t, d, [0.0] * 7, start)[1] for t, d in zip(tms, dones)]
+        rests = [behind(order[hi:], t) for t in tms]
+        now = [span(part, t, d, f, start, r)[0] for t, d, f, r in zip(tms, dones, frees, rests)]
+        turns, tight, top = tries * m // (n * sweeps), None, (now[0] + sum(now), part, set(over))
         for k in range(turns):
             seed = (seed * 1103515245 + 12345) % 2147483648
             a = (seed >> 8) % m
@@ -773,12 +818,10 @@ def arrange(ops, deps, seed, tries):
             hops, up = 1 + (seed >> 8) % 4, seed >> 20 & 1
             if tight is None:
                 z = (seed >> 12) % len(tms)
-                tight = critical(part, tms[z], dones[z], frees[z])
+                tight = critical(part, tms[z], dones[z], frees[z], rests[z])
             if tight and (seed >> 14) % 8 < KN["aim"]:
                 a = part.index(tight[a % len(tight)][up])
                 hops = 1 + (hops > 2) + (hops > 3)
-                if a >= m:
-                    continue
             i = part[a]
             if q[i] == 5:
                 continue
@@ -796,11 +839,11 @@ def arrange(ops, deps, seed, tries):
                     rest.append(j)
                     hops -= q[j] == q[i]
             new = part[:b] + block[::-1] + rest[::-1] + part[a + 1:] if up else part[:a] + rest + block + part[b + 1:]
-            heat = KN["heat"] * (1.0 - k / turns)
-            if span(new, tm, dones[0], frees[0], start)[0] <= now[0] + heat + 0.2:
+            heat = KN["heat"] * (1.0 - k / turns) * (1.0 - sweep / (sweeps + 1.0))
+            if span(new, tm, dones[0], frees[0], start, rests[0])[0] <= now[0] + heat + 0.2:
                 at = {j: z for z, j in enumerate(new)}
-                new = sorted(new[:m], key=lambda j: (start[j], at[j])) + new[m:]
-                c = [span(new, t, d, f, start)[0] for t, d, f in zip(tms, dones, frees)]
+                new = sorted(new, key=lambda j: (start[j], at[j]))
+                c = [span(new, t, d, f, start, r)[0] for t, d, f, r in zip(tms, dones, frees, rests)]
                 if c[0] + sum(c) <= now[0] + sum(now) + heat:
                     now, part, tight, other = c, new, None, False
                     if c[0] + sum(c) < top[0]:
@@ -810,11 +853,13 @@ def arrange(ops, deps, seed, tries):
         part = top[1]
         for i in over ^ top[2]:
             turn_over(i)
-        last = [span(part, t, d, f, start) for t, d, f in zip(tms, dones, frees)]
-        frees = [x[1] for x in last]
-        PLAN.setdefault("parts", []).append([round(x[2], 1) for x in last])
-        out += part
-    return out, over
+        order[lo:hi] = part
+        if hi == n:
+            PLAN.setdefault("parts", []).append(round(top[0], 1))
+            span(order, tm, dones[0], [0.0] * 7, start)
+            at = {j: z for z, j in enumerate(order)}
+            order = head + sorted(order[len(head):], key=lambda j: (start[j], at[j]))
+    return order, over
 
 
 def emit(g, T, ops, deps, order):

@@ -1,8 +1,10 @@
+import math
 from concourse.mybir import AluOpType as OP, ActivationFunctionType as AF
 
 S, K = 1024, 4096
 MAGIC = 12582912.0
 CWN = 8480
+WN, NC = 2240, 69
 JUNK = 16 * 1024 + 15
 F0, BA, BB, BC = K, 2 * K, 2 * K + S, 2 * K + 2 * S
 KN = {
@@ -10,54 +12,57 @@ KN = {
     "add": ("mmmmmmddd",) * 3,
     "cnt": (1024, 1024, 512, 1024, 512), "parts": (2560, 1536),
     "fl": (1024, 1024, 1024, 1024), "bl": (512, 512, 1024, 1024, 1024),
-    "fs": (1025, 1024, 2048), "bs": (2048, 2048),
-    "fc": (512,) * 7 + (256, 256), "lc": (512,) * 8, "look": "dadadada",
+    "fs": (513, 512, 1024), "bs": (2048,),
+    "fc": (512,) * 7 + (256, 256), "lc": (512,) * 8,
     "fh": (1024, 1024, 2048), "bh": (1024, 1024, 2048),
-    "sc": (256,) * 4, "cl": ((256,) * 4,) * 3, "wc": (256,) * 4, "ld": 512,
+    "sc": (256,) * 4, "wc": (256,) * 4, "ld": 512, "pp": ((512, 512), (1024,)), "old": 8,
     "first": (1, 0, 0),
-    "oka": ("ad", "ad", "dd"), "yepe": 3, "yem": 3, "gee": 1, "late": 4096, "zed": 0, "yes": 256, "pp": ((512, 512), (1024,)), "zero": "aa", "rule": 0, "ahead": 0.1, "lazy": 0.0, "lag": (0, 0, 0), "hold": (1024, 1024),
-    "seed": 1, "tries": 400000, "heat": 1.0, "aim": 6, "wide": 120, "sweeps": 24, "soft": 0.3,
-    "packs": 300, "shake": 0.5, "reach": 10.0,
+    "bank": ((0, 512, 1024, 1536), (256, 768, 1280, 1792)),
+    "how": (("g", "g"),) * 3, "hit": (("v", "v"),) * 3, "oka": ("ad", "ad", "dd"), "zero": "aa", "once": 0, "ilb": 2,
+    "seed": 1, "tries": 60000, "wide": 100, "sweeps": 20, "cand": 10, "far": 20, "ban": 10, "ahead": 0.1, "weights": (2, 1, 1),
 }
 
 SCRATCH = {
     "f16": ("sbuf", [128, S], "bfloat16"), "b16": ("sbuf", [128, S], "bfloat16"),
     "nz0": ("sbuf", [128, S], "bfloat16"), "nz1": ("sbuf", [128, S], "bfloat16"),
-    "prm0": ("sbuf", [128, 8], "float32"), "prm1": ("sbuf", [128, 8], "float32"), "prm2": ("sbuf", [128, 8], "float32"),
+    "prm0": ("sbuf", [128, 12], "float32"), "prm1": ("sbuf", [128, 12], "float32"), "prm2": ("sbuf", [128, 8], "float32"),
     "prs1": ("sbuf", [128, 4], "float32"), "prs2": ("sbuf", [128, 4], "float32"),
     "pi32": ("sbuf", [128, 256], "int32"),
     "pu0": ("sbuf", [128, 256], "uint16"), "pu1": ("sbuf", [128, 256], "uint16"), "pu2": ("sbuf", [128, 256], "uint16"),
+    "pa0": ("sbuf", [128, 256], "bfloat16"), "pa1": ("sbuf", [128, 256], "bfloat16"),
     "pf": ("sbuf", [128, S], "float32"), "snd": ("sbuf", [128, S], "float32"),
     "lf": ("sbuf", [128, S], "float32"), "lb": ("sbuf", [128, S], "float32"), "nb": ("sbuf", [128, S], "float32"),
     "win": ("sbuf", [128, 2 * K + 3 * S], "float32"), "dd": ("sbuf", [128, K], "float32"),
     "ab": ("sbuf", [128, 2048], "float32"), "miss": ("sbuf", [128, K], "bfloat16"),
-    "wf": ("sbuf", [128, K + 16], "bfloat16"), "wb": ("sbuf", [128, K + 16], "bfloat16"),
-    "sf": ("sbuf", [128, K + 16], "bfloat16"), "sb": ("sbuf", [128, K + 16], "bfloat16"),
+    "wf": ("sbuf", [128, WN], "bfloat16"), "wb": ("sbuf", [128, WN], "bfloat16"),
+    "sf": ("sbuf", [128, 2064], "bfloat16"), "sb": ("sbuf", [128, 2064], "bfloat16"),
     "xl": ("sbuf", [128, K], "bfloat16"),
-    "cw": ("sbuf", [128, CWN], "bfloat16"), "cn": ("sbuf", [128, 2048], "bfloat16"), "cmp": ("sbuf", [128, 2048], "bfloat16"),
-    "hit": ("sbuf", [128, 2048], "bfloat16"),
-    "hh": ("sbuf", [128, 2048], "float32"), "uu": ("sbuf", [128, 2048], "float32"), "yo": ("sbuf", [128, S], "float32"),
-    "wt": ("sbuf", [128, 144], "bfloat16"), "sm": ("sbuf", [128, 1024], "float32"),
-    "low": ("sbuf", [128, 128], "bfloat16"), "sv": ("sbuf", [128, 128], "bfloat16"), "sl": ("sbuf", [128, 8], "uint16"),
+    "cw": ("sbuf", [128, CWN], "bfloat16"), "cn": ("sbuf", [128, 2048], "bfloat16"), "cmp": ("sbuf", [128, 2080], "bfloat16"),
+    "hit": ("sbuf", [128, 2080], "bfloat16"),
+    "hh": ("sbuf", [128, 2048], "float32"), "uu": ("sbuf", [128, 2048], "float32"),
+    "wt": ("sbuf", [128, 144], "bfloat16"), "sm": ("sbuf", [128, 1280], "float32"),
+    "low": ("sbuf", [128, 160], "bfloat16"), "sv": ("sbuf", [128, 160], "bfloat16"), "sl": ("sbuf", [128, 12], "uint16"),
     "okw": ("sbuf", [128, 256], "bfloat16"), "okb": ("sbuf", [128, 256], "bfloat16"), "oks": ("sbuf", [128, 256], "bfloat16"),
-    "el": ("sbuf", [128, 280], "bfloat16"),
+    "el": ("sbuf", [128, 296], "bfloat16"),
     "al": ("sbuf", [128, 256], "uint16"), "jl": ("sbuf", [128, 256], "uint16"),
     "al2": ("sbuf", [128, 256], "uint16"), "jl1": ("sbuf", [128, 256], "uint16"),
     "fbu": ("sbuf", [128, 64], "float32"), "fb1": ("sbuf", [128, 64], "float32"),
-    "emp": ("sbuf", [128, 128], "float32"), "pl": ("sbuf", [128, 36], "uint16"), "pv": ("sbuf", [128, 272], "bfloat16"),
+    "emp": ("sbuf", [128, 256], "float32"), "pl": ("sbuf", [128, 72], "uint16"), "pv": ("sbuf", [128, 272], "bfloat16"),
     "ix": ("sbuf", [128, 128], "float32"), "il": ("sbuf", [128, 128], "uint16"),
-    "sel": ("sbuf", [128, 144], "bfloat16"), "sls": ("sbuf", [128, 144], "bfloat16"),
-    "sla": ("sbuf", [128, 144], "bfloat16"), "slb": ("sbuf", [128, 144], "bfloat16"),
-    "slc": ("sbuf", [128, 144], "bfloat16"), "sld": ("sbuf", [128, 144], "bfloat16"),
+    "sel": ("sbuf", [128, 144], "bfloat16"), "sls": ("sbuf", [128, 144], "bfloat16"), "slw": ("sbuf", [128, 144], "bfloat16"),
+    "slb": ("sbuf", [128, 144], "bfloat16"), "slc": ("sbuf", [128, 144], "bfloat16"), "sld": ("sbuf", [128, 144], "bfloat16"),
+    "s2a": ("sbuf", [128, 144], "bfloat16"), "s2b": ("sbuf", [128, 144], "bfloat16"),
+    "s2c": ("sbuf", [128, 144], "bfloat16"), "s2d": ("sbuf", [128, 144], "bfloat16"),
+    "sq4": ("sbuf", [128, 144], "bfloat16"), "sn4": ("sbuf", [128, 144], "bfloat16"),
     "blk": ("sbuf", [128, 128], "bfloat16"), "tri": ("sbuf", [128, 256], "bfloat16"),
     "eye": ("sbuf", [128, 128], "float32"), "eyb": ("sbuf", [128, 128], "bfloat16"),
     "top": ("sbuf", [128, 256], "float32"), "topb": ("sbuf", [128, 256], "bfloat16"),
     "off": ("sbuf", [128, 72], "bfloat16"), "one": ("sbuf", [128, 72], "float32"),
-    "zer": ("sbuf", [128, 2064], "bfloat16"), "dec": ("sbuf", [128, 4112], "bfloat16"),
-    "big": ("sbuf", [128, 256], "bfloat16"), "nl": ("sbuf", [128, 128], "float32"),
-    "kk": ("sbuf", [128, 128], "bfloat16"), "fb": ("sbuf", [128, 128], "float32"),
-    "kd": ("sbuf", [128, 48], "float32"), "cv": ("sbuf", [128, 256], "bfloat16"),
-    "ri": ("sbuf", [128, 8], "int32"), "rc": ("sbuf", [128, 16], "float32"),
+    "zer": ("sbuf", [128, 2064], "bfloat16"), "dec": ("sbuf", [128, 2064], "bfloat16"),
+    "nl": ("sbuf", [128, 128], "float32"),
+    "kk": ("sbuf", [128, 160], "bfloat16"), "fb": ("sbuf", [128, 128], "float32"),
+    "kd": ("sbuf", [128, 96], "float32"), "cv": ("sbuf", [128, 256], "bfloat16"),
+    "ri": ("sbuf", [128, 8], "int32"), "rc": ("sbuf", [128, 24], "float32"),
     "ps": ("psum", [128, 4096], "float32"),
 }
 NDMA = 110
@@ -114,12 +119,7 @@ def rank_program(g, core, T, topo):
                 w += regions([v[0]])
             else:
                 w += regions([v])
-        ops.append({"q": q, "fn": fn, "r": r, "w": w, "kind": kind, "sem": sem, "cost": cost, "rank": tuple(now)})
-
-    now = [0, 0]
-
-    def phase(k, at=0):
-        now[:] = [k, at]
+        ops.append({"q": q, "fn": fn, "r": r, "w": w, "kind": kind, "sem": sem, "cost": cost})
 
     def price(out, ins, per=1.0, fast=False):
         if len(out) == 2:
@@ -216,14 +216,15 @@ def rank_program(g, core, T, topo):
     def SEL(u, name="sel"):
         return V(name, 15 - u, 143 - u)
 
-    def rows(out, name, lo, hi, by="sel"):
-        mm([(out, SEL(u, by), V(name, lo + u, hi, 16), u == 0, u == 15) for u in range(16)])
+    def rows(out, name, lo, hi):
+        mm([(out, SEL(u), V(name, lo + u, hi, 16), u == 0, u == 15) for u in range(16)])
 
     def either(eng, on_act, on_dve):
         for fn in ((on_dve, on_act) if eng == "a" else (on_act, on_dve)):
             fn()
         alt = ops.pop(-2)
         ops[-1]["alt"] = {k: alt[k] for k in ("q", "fn", "cost")}
+        ops[-1]["r"] += [x for x in alt["r"] if x not in ops[-1]["r"]]
 
     def cut(eng, out, a):
         either(eng, lambda: act(out, a, AF.Relu, 0.0, SCL), lambda: ts(out, a, SCL, 0.0, OP.mult, OP.max))
@@ -238,9 +239,10 @@ def rank_program(g, core, T, topo):
         either(eng, lambda: act(out, a, AF.Identity, 0.0, s), lambda: ts(out, a, s, None, OP.mult))
 
     T_LT, T_GE = V("tri", 0, 128), V("tri", 128, 256)
-    I_B, I_F = V("eyb", 0, 128), V("eye", 0, 128)
-    ROW, IS0, DEC, SCL = (V("rc", i, i + 1) for i in (4, 5, 6, 7))
+    I_B, I_F, BLK = V("eyb", 0, 128), V("eye", 0, 128), V("blk", 0, 128)
+    ROW4, ROW17, LT15, C75, ROW, IS0, DEC, SCL, END, LESS, ROW2, MORE, HALF, SPARE, W15, W16, ODD = (V("rc", i, i + 1) for i in range(17))
     PARTS = cuts(KN["parts"])
+    NP = len(PARTS)
 
     load("sp", V("prm0", 0, 3), T.obs[:])
     load("sp", V("prm0", 3, 4), T.eps[:])
@@ -254,64 +256,87 @@ def rank_program(g, core, T, topo):
     load("sp", V("nz0", 0, S), T.nz[:])
 
     ms(V("sel", 0, 144), 0.0)
-    ms(V("blk", 0, 128), 1.0)
+    ms(BLK, 1.0)
+    ms(V("el", 0, 296), 0.0)
+    act(V("wt", 0, 144), V("el", 0, 144), AF.Exp, math.log(128.0), 1.0, 1250.0)
     iota(V("ri", 0, 1), [[0, 1]], 0, 1, small=False)
     sel(V("sel", 15, 143, 16), V("blk", 0, 8), [[-16, 8]], OP.is_ge, 0.0, 0, 1)
     sel(V("sel", 15, 143, 16), V("sel", 15, 143, 16), [[16, 8]], OP.is_ge, 0.0, 15, -1)
-    sel(I_B, V("blk", 0, 128), [[-1, 128]], OP.is_equal, 0.0, 0, 1)
-    sel(V("topb", 0, 128), V("blk", 0, 128), [[-16, 8], [0, 16]], OP.is_equal, 0.0, 0, 1)
-    sel(V("blk", 0, 128), V("blk", 0, 128), [[-16, 8], [0, 16]], OP.is_ge, 0.0, 0, 1)
-    sel(V("blk", 0, 128), V("blk", 0, 128), [[16, 8], [0, 16]], OP.is_ge, 0.0, 15, -1)
-    sel(T_LT, V("blk", 0, 128), [[1, 128]], OP.is_gt, 0.0, 0, -1)
-    sel(T_GE, V("blk", 0, 128), [[-1, 128]], OP.is_ge, 0.0, 0, 1)
-    iota(V("kk", 0, 128), [[0, 2], [0, 4], [1, 16]], 0, 0)
-    iota(V("kk", 64, 128), [[1, 64]], 0, 0)
+    sel(I_B, BLK, [[-1, 128]], OP.is_equal, 0.0, 0, 1)
+    sel(V("topb", 0, 128), BLK, [[-16, 8], [0, 16]], OP.is_equal, 0.0, 0, 1)
+    sel(BLK, BLK, [[-16, 8], [0, 16]], OP.is_ge, 0.0, 0, 1)
+    sel(BLK, BLK, [[16, 8], [0, 16]], OP.is_ge, 0.0, 15, -1)
+    sel(T_LT, BLK, [[1, 128]], OP.is_gt, 0.0, 0, -1)
+    sel(T_GE, BLK, [[-1, 128]], OP.is_ge, 0.0, 0, 1)
+    iota(V("kk", 0, 80), [[0, 5], [1, 16]], 0, 0)
+    iota(V("kk", 80, 160), [[1, 80]], 0, 0)
     for a, b in PARTS:
         iota(V("cv", a // 16, b // 16), [[1, (b - a) // 256], [(b - a) // 256, 16]], a // 16, 0)
-    iota(V("fb", 0, 64), [[64, 64]], K - JUNK * KN["gee"], 0)
-    if KN["gee"]:
-        iota(V("nl", 0, 128), [[1, 2], [32, 64]], 0, 0)
-    iota(V("kd", 0, 48), [[0, 2], [1, 24]], K + 1, 0)
+    iota(V("fb", 0, 64), [[64, 64]], K - JUNK, 0)
+    iota(V("nl", 0, 128), [[1, 2], [32, 64]], 0, 0)
+    iota(V("kd", 0, 24 * NP), [[0, NP], [1, 24]], K + 1, 0)
     load("pool", V("win", BA, BA + S), T.b0[:])
     for lo, hi in ((0, 1040), (1040, 2064)):
         ms(V("zer", lo, hi), 0.0)
     for nm, how in zip(("wb", "wf"), KN["zero"]):
-        move(V(nm, 0, 2048), V("zer", 0, 2048))
         if how == "m":
-            move(V(nm, 2048, K + 16), V("zer", 0, 2064))
+            move(V(nm, 0, 2064), V("zer", 0, 2064))
         else:
-            for lo, hi in ((2048, 3072), (3072, K + 16)):
+            for lo, hi in ((0, 1040), (1040, 2064)):
                 copy(how, V(nm, lo, hi), V("zer", 0, hi - lo))
+    for h in range(2):
+        ms(V("hit", 1040 * h + S, 1040 * h + 1040), 0.0)
     move(V("cw", 0, 2048), V("zer", 0, 2048))
-    ms(V("one", 0, 64), 1.0)
-    ms(V("one", 64, 65), 2.0 ** -12)
-    ms(V("wt", 0, 144), 128.0)
-    ms(V("off", 0, 72), -2048.0)
+    ms(V("one", 0, NC), 1.0)
+    ms(LESS, -MAGIC)
+    ms(MORE, MAGIC)
     copy("a", I_F, I_B)
     copy("a", V("top", 0, 128), V("topb", 0, 128))
     tt(V("topb", 128, 256), I_B, V("topb", 0, 128), OP.subtract)
-    copy("a", V("top", 128, 256), V("topb", 128, 256))
     ts(V("ri", 4, 5), V("ri", 0, 1), 15, None, OP.bitwise_and)
     cp(ROW, V("ri", 4, 5))
     ts(IS0, ROW, 0.0, None, OP.is_equal)
     ts(DEC, IS0, -1.0, None, OP.add)
     ts(SCL, IS0, 17.0, -1.0, OP.mult, OP.add)
-    for lo, hi in ((0, 1024), (1024, 2048), (2048, 2064)):
+    for lo, hi in ((0, 1024), (1024, 2048)):
         shift("a", V("dec", lo, hi), V("zer", 0, hi - lo), DEC)
-    if max(KN["bs"] + KN["fs"]) > 2064:
-        move(V("dec", 2064, 4112), V("dec", 0, 2048))
-    ts(V("kk", 0, 64), V("kk", 0, 64), ROW, -8192.0, OP.not_equal, OP.mult)
-    scale("a", V("kk", 64, 128), V("kk", 64, 128), IS0)
-    scale("a", V("slb", 0, 144), V("sel", 0, 144), SCL)
+    ts(V("one", NC, NC + 1), IS0, 2.0 ** -12, 2.0 ** -12, OP.mult, OP.add)
+    ts(V("off", 1, NC), V("zer", 1, NC), IS0, -128.0, OP.subtract, OP.add)
+    ms(V("off", 0, 1), -128.0)
+    ts(V("off", NC, NC + 1), IS0, -12.0, -128.0, OP.mult, OP.add)
+    if "b" in KN["hit"][0]:
+        scale("a", V("prm0", 7, 8), V("prm0", 3, 4), -1.0)
+        scale("a", V("sq4", 0, 144), V("sel", 0, 144), 0.25)
+        scale("a", V("sn4", 0, 144), V("sel", 0, 144), -0.25)
+        for h in range(2):
+            ms(V("cmp", 1040 * h + S, 1040 * h + 1040), 0.0)
+    ts(HALF, IS0, 0.5, 0.5, OP.mult, OP.add)
+    scale("a", V("topb", 128, 256), V("topb", 128, 256), HALF)
+    copy("a", V("top", 128, 256), V("topb", 128, 256))
+    ts(V("kk", 0, 80), V("kk", 0, 80), ROW, -8192.0, OP.not_equal, OP.mult)
+    ts(SPARE, ROW, 16.0, 1984.0, OP.mult, OP.add)
+    shift("a", V("kk", NC, 80), V("kk", NC, 80), SPARE)
+    scale("a", V("kk", 80, 160), V("kk", 80, 160), IS0)
+    ts(W15, IS0, 16.0, -1.0, OP.mult, OP.add)
+    ts(W16, IS0, -0.0625, 1.0, OP.mult, OP.add)
+    scale("a", V("slb", 0, 144), V("sel", 0, 144), W15)
     scale("a", V("slc", 0, 144), V("sel", 0, 144), DEC)
     scale("a", V("sld", 0, 144), V("slc", 0, 144), -1.0)
-    copy("a", V("sla", 0, 144), V("slb", 0, 144))
-    copy("a", V("sla", 14, 142, 16), V("sld", 15, 143, 16))
-    cp(V("pu0", 0, 256), V("pi32", 0, 256))
-    phase(2, 1)
-    copy("a", V("sls", 16, 144), V("sel", 0, 128))
-    copy("a", V("sls", 0, 16), V("sel", 112, 128))
-    copy("a", V("sls", 143, 144), V("sel", 0, 1))
+    scale("a", V("slw", 0, 144), V("sel", 0, 144), W16)
+    for two, one in (("s2b", "slb"), ("s2c", "slc"), ("s2d", "sld"), ("s2a", "slb")):
+        copy("a", V(two, 0, 144), V(one, 0, 144))
+        copy("a", V(two, 16, 144, 16), V(one, 15, 143, 16))
+    for z in (13, 14):
+        copy("a", V("s2a", z, z + 128, 16), V("sld", 15, 143, 16))
+    ts(V("ri", 5, 6), V("ri", 0, 1), 1, None, OP.bitwise_and)
+    ts(ODD, V("ri", 5, 6), 0.5, 14.75, OP.mult, OP.add)
+    ts(V("pu0", 0, 256), V("pi32", 0, 256), 0.5, -0.25, OP.mult, OP.add)
+    ts(V("pi32", 0, 256), V("pi32", 0, 256), 1, None, OP.bitwise_and)
+    ts(V("pa0", 0, 256), V("pi32", 0, 256), 0.5, -0.25, OP.mult, OP.add)
+    copy("a", V("sls", 16, 144), V("slw", 0, 128))
+    copy("a", V("sls", 0, 16), V("slw", 112, 128))
+    copy("a", V("sls", 143, 144), V("slw", 0, 1))
+    hand(1, V("pa1", 0, 256), V("pa0", 0, 256))
     turn(V("pu2", 0, 256), V("pu0", 0, 256), -16)
     turn(V("prs2", 0, 4), V("prm0", 0, 4), -16)
     hand(1, V("prs1", 0, 4), V("prs2", 0, 4))
@@ -319,111 +344,114 @@ def rank_program(g, core, T, topo):
     hand(-1, V("nz1", 0, S), V("nz0", 0, S))
     hand(-1, V("prm1", 0, 7), V("prm0", 0, 7))
     hand(2, V("prm2", 0, 4), V("prm0", 0, 4))
-    ms(V("rc", 3, 4), 7.5)
-    ms(V("el", 0, 280), 0.0)
-    ms(V("emp", 0, 128), 1.0)
-    scale("a", V("rc", 0, 1), ROW, 4.0)
-    scale("a", V("rc", 1, 2), ROW, 17.0)
-    ts(V("rc", 2, 3), ROW, 15.0, None, OP.is_lt)
-    scale("a", V("rc", 8, 9), IS0, 1024.0)
-    shift("a", V("pv", 256, 272), V("zer", 0, 16), V("rc", 8, 9))
+    if any(w != "g" for pair in KN["how"] for way in pair for w in way):
+        scale("a", V("prm0", 8, 10), V("prm0", 5, 7), -1.0)
+        scale("a", V("prm1", 8, 10), V("prm1", 5, 7), -1.0)
+    ms(C75, 7.5)
+    ms(V("emp", 64 * NP - 64, 64 * NP - 40), 1.0)
+    scale("a", ROW4, ROW, 4.0)
+    scale("a", ROW17, ROW, 17.0)
+    ts(LT15, ROW, 15.0, None, OP.is_lt)
+    scale("a", END, IS0, 1024.0)
+    shift("a", V("pv", 256, 272), V("zer", 0, 16), END)
     scale("a", V("cv", 0, 256), V("cv", 0, 256), IS0)
-    shift("a", V("fb", 0, 64), V("fb", 0, 64), V("rc", 0, 1))
-    if KN["gee"]:
-        scale("a", V("rc", 10, 11), ROW, 2.0)
-        shift("a", V("nl", 0, 128), V("nl", 0, 128), V("rc", 10, 11))
-    if KN["zed"]:
-        scale("a", V("big", 0, 128), I_B, 8192.0)
-        scale("a", V("big", 128, 256), I_B, -8192.0)
-    shift("a", V("kd", 0, 48), V("kd", 0, 48), V("rc", 1, 2))
-    z = 24 * (len(PARTS) - 1) + KN["parts"][-1] // 256
-    scale("a", V("kd", z, z + 1), V("kd", z, z + 1), V("rc", 2, 3))
+    shift("a", V("fb", 0, 64), V("fb", 0, 64), ROW4)
+    scale("a", ROW2, ROW, 2.0)
+    shift("a", V("nl", 0, 128), V("nl", 0, 128), ROW2)
+    shift("a", V("kd", 0, 24 * NP), V("kd", 0, 24 * NP), ROW17)
+    z = 24 * (NP - 1) + KN["parts"][-1] // 256
+    scale("a", V("kd", z, z + 1), V("kd", z, z + 1), LT15)
 
     def who(t):
         k = "1" if t == 1 else "0"
         pr = "prm" + k
-        return {"y": V(pr, t, t + 1), "eps": V(pr, 3, 4), "lam": V(pr, 4, 5), "r": (V(pr, 5, 6), V(pr, 6, 7)), "nz": "nz" + k}
+        return {"y": V(pr, t, t + 1), "eps": V(pr, 3, 4), "lam": V(pr, 4, 5), "r": (V(pr, 5, 6), V(pr, 6, 7)),
+                "n": (V(pr, 8, 9), V(pr, 9, 10)), "nz": "nz" + k}
 
     def starts(t, h, pool, bk, bk2):
         pr = (("prm0", "prm0"), ("prm1", "prs1"), ("prm2", "prs2"))[t][h]
-        for lo, hi in cuts(KN["wc"]):
-            a, x = (V(nm, S * h + lo, S * h + hi) for nm in ("ab", "hit"))
-            act(a, W(pool, lo, hi), AF.Abs, V(pr, t, t + 1), -1.0)
-            ts(x, a, V(pr, 3, 4), 0.25, OP.is_le, OP.mult)
-        if t and h == KN["first"][t - 1]:
-            ops[-1]["w"].append(("hold", t - 1, t))
-        rows(P(bk, 0, 64), "hit", S * h, S * h + S)
-        o, w, c = 512 * h, 72 * h, 64 * h
-        C, CT, RHO = V("sm", o, o + 64), V("sm", o + 64, o + 65), V("sm", o + 72, o + 73)
-        E, Q, E0, M = (V("sm", o + z, o + z + 64) for z in (128, 192, 256, 320))
-        L, vals, sl = V("low", c, c + 64), V("sv", c, c + 64), V("sl", 4 * h, 4 * h + 4)
-        mm([(P(bk2, 0, 65), I_B, V("off", 0, 65), True, False)])
-        ts(V("wt", w + 1, w + 65), P(bk, 0, 64), 127.625, 129.0, OP.add, OP.max)
-        mm([(P(bk2, 0, 65), T_LT, V("wt", w + 1, w + 66), False, False), (P(bk2, 0, 65), T_GE, V("wt", w, w + 65), False, True)])
-        scan(V("sm", o, o + 65), P(bk2, 0, 65), V("one", 0, 65), 0.0, OP.add, OP.mult)
+        y, eps, at = V(pr, t, t + 1), V(pr, 3, 4), 1040 * h
+        for k, (lo, hi) in enumerate(cuts(KN["wc"])):
+            a, x = V("ab", S * h + lo, S * h + hi), V("hit", at + lo, at + hi)
+            way = KN["hit"][t][h][k % len(KN["hit"][t][h])]
+            if way == "b":
+                ts(x, W(pool, lo, hi), y, eps, OP.subtract, OP.is_le)
+                ts(V("cmp", at + lo, at + hi), W(pool, lo, hi), y, V(pr, 7, 8), OP.subtract, OP.is_lt)
+                continue
+            act(a, W(pool, lo, hi), AF.Abs, y, -1.0)
+            if way == "v":
+                ts(x, a, eps, 0.25, OP.is_le, OP.mult)
+            else:
+                act(x, a, AF.Sign, eps, -1.0)
+                ts(x, x, -0.5, 0.25, OP.is_gt, OP.mult)
+        if KN["hit"][t][h] == "b":
+            mm([(P(bk, 0, NC), SEL(u, "sq4"), V("hit", at + u, at + 15 * NC, 15), u == 0, False) for u in range(15)])
+            mm([(P(bk, 0, NC), SEL(u, "sn4"), V("cmp", at + u, at + 15 * NC, 15), False, u == 14) for u in range(15)])
+        else:
+            mm([(P(bk, 0, NC), SEL(u), V("hit", at + u, at + 15 * NC, 15), u == 0, u == 14) for u in range(15)])
+        o, w, c = 640 * h, 72 * h, 80 * h
+        C, CT, RHO = V("sm", o, o + NC), V("sm", o + NC, o + NC + 1), V("sm", o + 72, o + 73)
+        E, Q, E0 = (V("sm", o + z, o + z + NC) for z in (80, 160, 240))
+        M, L, vals, sl = V("sm", o + 320, o + 400), V("low", c, c + NC), V("sv", c, c + 80), V("sl", 6 * h, 6 * h + 5)
+        mm([(P(bk2, 0, NC + 1), BLK, V("off", 0, NC + 1), True, False)])
+        ts(V("wt", w + 1, w + NC + 1), P(bk, 0, NC), 127.625, 129.0, OP.add, OP.max)
+        mm([(P(bk2, 0, NC + 1), T_LT, V("wt", w + 1, w + NC + 2), False, False), (P(bk2, 0, NC + 1), T_GE, V("wt", w, w + NC + 1), False, True)])
+        scan(V("sm", o, o + NC + 1), P(bk2, 0, NC + 1), V("one", 0, NC + 1), 0.0, OP.add, OP.mult)
         rec("dve", lambda: g.vector.reciprocal(ap(RHO), ap(CT)), [CT], [RHO], ("c", 230.0))
-        ts(E, C, RHO, MAGIC, OP.mult, OP.add)
+        either("d", lambda: act(E, C, AF.Identity, MORE, RHO), lambda: ts(E, C, RHO, MAGIC, OP.mult, OP.add))
         ts(Q, E, -MAGIC, CT, OP.add, OP.mult)
-        shift("a", E0, E, V("rc", 9, 10))
+        shift("a", E0, E, LESS)
         tt(L, Q, C, OP.is_lt)
-        for out, z in ((P(bk2, 128, 192), 0), (P(bk, 128, 192), 1)):
-            mm([(out, V("top", 128 * z, 128 * z + 128), E0, True, False), (out, I_B, V("kk", 64 * z, 64 * z + 64), False, False)])
-            mm([(out, V("topb", 128 * z, 128 * z + 128), L, False, True)])
-        scan(M, P(bk2, 128, 192), V("zer", 0, 64), 0.0, OP.max, OP.add)
-        cp(sl, V("sm", o + 335, o + 384, 16))
-        copy("a", vals, P(bk, 128, 192))
+        for b, z in ((bk2, 0), (bk, 1)):
+            mm([(P(b, 128, 208), I_B, V("kk", 80 * z, 80 * z + 80), True, False),
+                (P(b, 128, 128 + NC), V("top", 128 * z, 128 * z + 128), E0, False, False)])
+            mm([(P(b, 128, 128 + NC), V("topb", 128 * z, 128 * z + 128), L, False, True)])
+        scan(M, P(bk2, 128, 208), V("zer", 0, 80), 0.0, OP.max, OP.add)
+        cp(sl, V("sm", o + 335, o + 400, 16))
+        copy("a", vals, P(bk, 128, 208))
         wn, sn = ("wf", "wb")[h], ("sf", "sb")[h]
-        cp((V(wn, 0, K), sl), vals)
+        cp((V(wn, 0, WN), sl), vals)
         for lo, hi in cuts(KN["bs" if h else "fs"]):
-            if lo and not h:
-                phase(10 * t + 3, lo - KN["lag"][0] - 1)
             scan(V(sn, lo, hi), V(wn, lo, hi), V("dec", 0, hi - lo), V(sn, lo - 1, lo) if lo else -1.0, OP.max, OP.add)
-    phase(0)
-    ms(V("rc", 9, 10), -MAGIC)
 
     def clear(t, h):
         if t < 2:
-            phase(10 * t + 4, 1)
-            cp((V(("wf", "wb")[h], 0, K), V("sl", 4 * h, 4 * h + 4)), V("zer", 0, 64))
+            cp((V(("wf", "wb")[h], 0, WN), V("sl", 6 * h, 6 * h + 5)), V("zer", 0, 80))
 
     def f_ancestors(t, pool):
         for i, (lo, hi) in enumerate(cuts(KN["fl"])):
-            phase(10 * t + 3, lo - KN["lag"][0])
-            out = P((4, 2)[i % 2], lo // 16, hi // 16)
-            mm([(out, SEL(u, "sla" if u else "slb"), V("sf", lo + u, hi, 16), u == 0, False) for u in range(16)]
-               + [(out, SEL(15, "sld"), V("sf", lo + 16, hi + 1, 16), False, False)]
-               + [(out, SEL(u, "slc"), V("wf", lo + u + 1, hi + 1, 16), False, u == 15) for u in range(16)])
-            ts(V("al", lo // 16, hi // 16), out, 15.0, None, OP.add)
+            out, a, b = P((4, 2)[i % 2], lo // 16, hi // 16), lo // 2, hi // 2
+            mm([(out, SEL(2 * u, "s2a" if u else "s2b"), V("sf", a + u, b, 8), u == 0, False) for u in range(8)]
+               + [(out, SEL(14, "s2d"), V("sf", a + 8, b + 1, 8), False, False)]
+               + [(out, SEL(2 * u, "s2c"), V("wf", a + u + 1, b + 1, 8), False, u == 7) for u in range(8)])
+            ts(V("al", lo // 16, hi // 16), out, ODD, None, OP.add)
         if t == 2:
             for lo, hi in cuts(KN["fh"]):
-                phase(10 * t + 3, lo - KN["lag"][0])
                 hand(2, V("al2", lo // 16, hi // 16), V("al", lo // 16, hi // 16))
         clear(t, 0)
         for lo, hi in cuts(KN["fc"]):
-            phase(10 * t + 3, lo - KN["lag"][2])
             copy("a", V("win", F0 + lo, F0 + hi), (W(pool, 0, S), V("al2" if t == 2 else "al", lo // 16, hi // 16)))
 
     def b_ancestors(t, base):
         for i, (lo, hi) in enumerate(cuts(KN["bl"])):
             for k, (a, b) in enumerate(cuts(KN["lc"])):
                 if lo <= a < hi:
-                    phase(10 * t + 3, lo - KN["lag"][1])
-                    cut(KN["look"][k], V("xl", a, b), (V("sb", 0, K), V("pu%d" % t, a // 16, b // 16)))
+                    cut("da"[k % 2], V("xl", a, b), (V("sb", 0, K // 2), V("pu%d" % t, a // 16, b // 16)))
             out = P((5, 3)[i % 2], lo // 16, hi // 16)
-            rows(out, "xl", lo, hi, "sls" if t else "sel")
+            mm([(out, I_B, V("pa1" if t == 1 else "pa0", lo // 16, hi // 16), True, False)]
+               + [(out, SEL(u, "sls" if t else "slw"), V("xl", lo + u, hi, 16), False, u == 15) for u in range(16)])
             cp(V("jl", lo // 16, hi // 16), out)
-        phase(10 * t + 3, 2048)
         out = P(0, 256, 320)
-        mm([(out, SEL(u, nm), V(src, 4 * u + z, K, 64), u == 0 and nm == "slb", u == 15 and nm == "slc")
-            for nm, src, z in (("slb", "sb", 0), ("sld", "sb", 1), ("slc", "wb", 1)) for u in range(16)])
-        ts(V("fbu", 0, 64) if t else V("fb", 64, 128), out, base + 15.0 - JUNK * KN["gee"], None, OP.add)
+        items = [(out, SEL(u, nm), V(src, 2 * u + z, K // 2, 32), u == 0 and nm == "slb", u == 15 and nm == "slc")
+                 for nm, src, z in (("slb", "sb", 0), ("sld", "sb", 1), ("slc", "wb", 1)) for u in range(16)]
+        for z in range(0, 48, KN["old"]):
+            mm(items[z:z + KN["old"]])
+        ts(V("fbu", 0, 64) if t else V("fb", 64, 128), out, base + 14.75 - JUNK, None, OP.add)
         clear(t, 1)
         if t == 1:
             for lo, hi in cuts(KN["bh"]):
-                phase(10 * t + 3, lo - KN["lag"][1])
                 hand(-2, V("jl1", lo // 16, hi // 16), V("jl", lo // 16, hi // 16))
             hand(-2, V("fb1", 0, 64), V("fbu", 0, 64))
-        phase(10 * t + 3, 2048)
         if t:
             turn(V("fb", 64, 128), V("fb1" if t == 1 else "fbu", 0, 64), 16)
 
@@ -431,7 +459,6 @@ def rank_program(g, core, T, topo):
         p = who(t)
         ends = {hi: lo for lo, hi in cuts(KN["cnt"])}
         for i, (lo, hi) in enumerate(cuts(KN["loop"])):
-            phase(10 * t + 3, lo)
             z, o = hi - lo, lo % 2048
             d, f, m, x = V("dd", lo, hi), V("win", F0 + lo, F0 + hi), V("win", lo, hi), V("miss", lo, hi)
             tt(d, (W(pool, 0, S), V("jl1" if t == 1 else "jl", lo // 16, hi // 16)), f, OP.subtract)
@@ -443,122 +470,103 @@ def rank_program(g, core, T, topo):
                 adds(m, f)
             act(V("ab", o, o + z), m, AF.Abs, p["y"], -1.0)
             ts(x, V("ab", o, o + z), p["eps"], None, OP.is_gt)
-            if lo >= KN["late"]:
-                ops[-1]["r"].append(("cw", 0, 1))
-            s = max(k for k in range(len(PARTS)) if PARTS[k][0] <= lo)
+            s = max(k for k in range(NP) if PARTS[k][0] <= lo)
             a, b = PARTS[s]
             w = (b - a) // 16
-            mm([(P(7 - 4 * s, 0, w), SEL(r), V("miss", a + w * r, a + w * r + w), r == 0, r == 15)
+            mm([(P(7 - 4 * (s % 2), 0, w), SEL(r), V("miss", a + w * r, a + w * r + w), r == 0, r == 15)
                 for r in range((lo - a) // w, (hi - a) // w)])
             if hi in ends:
-                rows(P(6 - 4 * s, ends[hi] // 16, hi // 16), "miss", ends[hi], hi)
+                rows(P(6 - 4 * (s % 2), ends[hi] // 16, hi // 16), "miss", ends[hi], hi)
             if hi == b:
                 columns(t, s)
 
     def columns(t, s):
         a, b = PARTS[s]
-        w, c, last = (b - a) // 16, a // 16, s == len(PARTS) - 1
+        w, c, last = (b - a) // 16, a // 16, s == NP - 1
         nc, e, o = w // 16, c + 8 * s, 64 * s
         ne = nc + last
-        ts(V("okb", c, c + w), P(7 - 4 * s, 0, w), 7.5, None, OP.is_lt)
+        ts(V("okb", c, c + w), P(7 - 4 * (s % 2), 0, w), 7.5, None, OP.is_lt)
         scan(V("el", e + 1, e + w + 1), V("okb", c, c + w), V("okb", c, c + w), 0.0, OP.add, OP.max)
         tot = [V("el", PARTS[k][1] // 16 + 8 * k, PARTS[k][1] // 16 + 8 * k + 1) for k in range(s + 1)]
         if s:
-            mm([(P(5, 400 + s, 401 + s), V("blk", 0, 128), tot[k], k == 0, False) for k in range(s)])
+            mm([(P(5, 400 + s, 401 + s), BLK, tot[k], k == 0, False) for k in range(s)])
         mm([(P(5, 400 + s, 401 + s), T_LT, tot[s], s == 0, True)])
-        if last and KN["gee"]:
-            mm([(P(5, 404, 405), V("blk", 0, 128), tot[k], k == 0, k == s) for k in range(s + 1)])
-            ts(V("ix", 0, 128), V("nl", 0, 128), P(5, 404, 405), None, OP.is_ge)
+        if last:
+            mm([(P(5, 408, 409), BLK, tot[k], k == 0, k == s) for k in range(s + 1)])
+            ts(V("ix", 0, 128), V("nl", 0, 128), P(5, 408, 409), None, OP.is_ge)
             tt(V("ix", 0, 128), V("ix", 0, 128), V("fb", 0, 128), OP.mult)
-        if KN["zed"]:
-            z = P(7 - 4 * s, 256, 256 + ne)
-            mm([(z, I_F, V("kd", 24 * s, 24 * s + ne), True, False)])
-            mm([(P(7 - 4 * s, 256, 256 + nc), V("big", 0, 128), V("el", e, e + w, 16), False, False),
-                (P(7 - 4 * s, 256, 256 + nc), V("big", 128, 256), V("el", e + 16, e + w + 1, 16), False, True)])
-            tt(V("emp", o + 40, o + 40 + ne), V("el", e, e + 16 * ne - 15, 16), z, OP.max)
-        else:
-            tt(V("emp", o, o + nc), V("el", e, e + w, 16), V("el", e + 16, e + w + 1, 16), OP.is_equal)
-            tt(V("emp", o + 20, o + 20 + ne), V("emp", o, o + ne), V("kd", 24 * s, 24 * s + ne), OP.mult)
-            tt(V("emp", o + 40, o + 40 + ne), V("emp", o + 20, o + 20 + ne), V("el", e, e + 16 * ne - 15, 16), OP.add)
+        tt(V("emp", o, o + nc), V("el", e, e + w, 16), V("el", e + 16, e + w + 1, 16), OP.is_equal)
+        tt(V("emp", o + 20, o + 20 + ne), V("emp", o, o + ne), V("kd", 24 * s, 24 * s + ne), OP.mult)
+        tt(V("emp", o + 40, o + 40 + ne), V("emp", o + 20, o + 20 + ne), V("el", e, e + 16 * ne - 15, 16), OP.add)
         ts(V("pl", 18 * s, 18 * s + ne), V("emp", o + 40, o + 40 + ne), P(5, 400 + s, 401 + s), None, OP.add)
+        cnt = P(6 - 4 * (s % 2), c, c + w)
         if KN["oka"][t][s] == "a":
-            act(V("oks", c, c + w), P(6 - 4 * s, c, c + w), AF.Sign, V("rc", 3, 4), -1.0)
+            act(V("oks", c, c + w), cnt, AF.Sign, C75, -1.0)
             act(V("okw", c, c + w), V("oks", c, c + w), AF.Relu)
         else:
-            ts(V("okw", c, c + w), P(6 - 4 * s, c, c + w), 7.5, None, OP.is_lt)
+            ts(V("okw", c, c + w), cnt, 7.5, None, OP.is_lt)
         mm([(P(4, 256 + c, 256 + c + w), I_B, V("cv", c, c + w), True, False)])
         mm([(P(4, 256 + c + 16 * i, 272 + c + 16 * i), T_LT, V("okw", c + i, c + w, nc), False, i == nc - 1) for i in range(nc)])
         copy("a", V("pv", c, c + w), P(4, 256 + c, 256 + c + w))
         cp((V("cw", 0, CWN), V("pl", 18 * s, 18 * s + ne)), V("pv", c, c + 16 * ne))
 
     def places(t):
-        phase(10 * t + 4)
         for lo, hi in cuts(KN["pp"][0]):
             scan(V("cn", 2 * lo, 2 * hi), V("cw", 2 * lo, 2 * hi), V("dec", 0, 2 * (hi - lo)),
                  V("cn", 2 * lo - 1, 2 * lo) if lo else -1.0, OP.max, OP.add)
         if t < 2:
             move(V("cw", 0, 2048), V("zer", 0, 2048))
-        z = 2
+        z = KN["ilb"]
         for k, h in enumerate((KN["first"][t], 1 - KN["first"][t])):
             for lo, hi in cuts(KN["pp"][k]):
-                a, b = 64 * h + lo // 16, 64 * h + hi // 16
-                cut("da"[k], V("cmp", S * h + lo, S * h + hi), V("cn", 2 * lo + h, 2 * hi, 2))
-                if KN["gee"]:
-                    mm([(P(z, 0, b - a), I_F, V("ix", a, b), True, False)])
-                    mm([(P(z, 0, b - a), SEL(u), V("cmp", S * h + lo + u, S * h + hi, 16), False, u == 15) for u in range(16)])
-                    cp(V("il", a, b), P(z, 0, b - a))
-                else:
-                    rows(P(z, 0, b - a), "cmp", S * h + lo, S * h + hi)
-                    tt(V("ix", a, b), V("fb", a, b), P(z, 0, b - a), OP.min)
-                    cp(V("il", a, b), V("ix", a, b))
+                a, b, at = 64 * h + lo // 16, 64 * h + hi // 16, 1040 * h
+                cut("da"[k], V("cmp", at + lo, at + hi), V("cn", 2 * lo + h, 2 * hi, 2))
+                mm([(P(z, 0, b - a), I_F, V("ix", a, b), True, False)])
+                mm([(P(z, 0, b - a), SEL(u), V("cmp", at + lo + u, at + hi, 16), False, u == 15) for u in range(16)])
+                cp(V("il", a, b), P(z, 0, b - a))
                 z += 1
 
     def step(t, h, end, dst, done):
         p = who(t)
-        bk = 0 if h == KN["first"][t] else 2
-        phase(10 * t + 5 + bk)
-        for a, b in cuts(KN["cl"][t]):
-            mm([(P(bk, a, b), I_B, V("zer", 0, b - a), True, False)])
-            for lo, hi in cuts(KN["sc"]):
-                if a <= lo < b:
-                    gat = (V("win", 0, end), V("il", 64 * h + lo // 16, 64 * h + hi // 16))
-                    hh, uu = (V(nm, S * h + lo, S * h + hi) for nm in ("hh", "uu"))
-                    act(hh, gat, AF.Square)
-                    tt(uu, gat, hh, OP.subtract)
-                    if h != KN["first"][t] and t < 2 and lo >= KN["hold"][t]:
-                        ops[-1]["r"].append(("hold", t, t + 1))
-                    scale("a", P(bk, lo, hi), uu, p["r"][h])
-                    mm([(P(bk, lo, hi), I_B, V(p["nz"], lo, hi), False, hi == b)])
-            ts(W(dst, a, b), P(bk, a, b), 0.0, 1.0, OP.max, OP.min)
-            if t == 2 or b % 512 == 0:
-                done(a if t == 2 else b - 512, b)
+        late = int(h != KN["first"][t])
+        how = KN["how"][t][late]
+        for k, (lo, hi) in enumerate(cuts(KN["sc"])):
+            z = KN["bank"][late][k]
+            x = P(0, z, z + hi - lo)
+            if not KN["once"]:
+                mm([(x, I_B, V("zer", 0, hi - lo), True, False)])
+            elif not late:
+                mm([(P(0, z, z + 512), I_B, V("zer", 0, 512), True, False)])
+            gat = (V("win", 0, end), V("il", 64 * h + lo // 16, 64 * h + hi // 16))
+            hh, uu = (V(nm, S * h + lo, S * h + hi) for nm in ("hh", "uu"))
+            way = how[k % len(how)]
+            if way == "g":
+                act(hh, gat, AF.Square)
+                tt(uu, gat, hh, OP.subtract)
+            if way == "s":
+                copy("a", hh, gat)
+                act(uu, hh, AF.Square)
+                scan(uu, uu, hh, 0.0, OP.max, OP.subtract)
+            if way == "p":
+                uu = x
+                scale("a", hh, gat, -1.0)
+                act(uu, hh, AF.Square)
+                mm([(uu, I_F, hh, False, False)])
+            scale("a", x, uu, p["r" if way == "g" else "n"][h])
+            mm([(x, I_B, V(p["nz"], lo, hi), False, bool(late or not KN["once"]))])
+            ts(W(dst, lo, hi), x, 0.0, 1.0, OP.max, OP.min)
+            if t == 2 or hi % 512 == 0:
+                done(lo if t == 2 else hi - 512, hi)
 
     def energy():
-        npe, z = KN["yepe"], KN["yes"]
-        phase(26)
         for lo in range(0, S, 512):
             for i in range(4):
                 v = V("dd", S * i + lo, S * i + lo + 512)
-                either("a", lambda: act(v, v, AF.Square), lambda: tt(v, v, v, OP.mult))
-                if i >= 4 - KN["yem"]:
-                    act(v, v, AF.Exp, 0.0, -1.0)
-                    adds(V("yo" if KN["yem"] < 3 else "dd", lo, lo + 512), v)
-                    if i == 3:
-                        store(T.ye[:, lo:lo + 512], V("yo" if KN["yem"] < 3 else "dd", lo, lo + 512))
-                    continue
-                act(P(4, lo, lo + 512) if i > npe else v, v, AF.Exp, 0.0, -1.0, 1500.0 if i + lo == 0 else 0.0)
-                if KN["yem"] == 3:
-                    continue
-                if i < npe:
-                    w = z if i else 512
-                    for a in range(lo, lo + 512, w):
-                        mm([(P(6, a, a + w), I_F, V("dd", S * i + a, S * i + a + w), i == 0, i == npe - 1 and a + w == lo + 512)])
-                elif i == npe:
-                    tt(V("yo", lo, lo + 512), v, P(6, lo, lo + 512), OP.add)
-                else:
-                    tt(V("yo", lo, lo + 512), V("yo", lo, lo + 512), P(4, lo, lo + 512), OP.add)
-                if i == 3:
-                    store(T.ye[:, lo:lo + 512], V("yo", lo, lo + 512))
+                either("a", lambda v=v: act(v, v, AF.Square), lambda v=v: tt(v, v, v, OP.mult))
+                act(v, v, AF.Exp, 0.0, -1.0)
+                if i:
+                    adds(V("dd", lo, lo + 512), v)
+            store(T.ye[:, lo:lo + 512], V("dd", lo, lo + 512))
 
     def nothing(lo, hi):
         return None
@@ -569,9 +577,7 @@ def rank_program(g, core, T, topo):
         pairs(t, b)
         places(t)
 
-    phase(1)
     starts(0, 1, ("b16", 0), 6, 7)
-    phase(2)
     starts(0, 0, ("f16", 0), 2, 3)
     ancestors(0, ("f16", 0), ("b16", 0), BA)
 
@@ -596,8 +602,11 @@ def rank_program(g, core, T, topo):
             starts(2, 0, ("snd", 0), 6, 7)
     ancestors(2, ("lf", 0), ("win", BC), BC)
     energy()
-    step(2, 0, BA, ("pf", 0), lambda lo, hi: store(T.yf[:, lo:hi], V("pf", lo, hi)))
-    step(2, 1, BC + S, ("snd", 0), lambda lo, hi: store(T.yb[:, lo:hi], V("snd", lo, hi)))
+    for h in (KN["first"][2], 1 - KN["first"][2]):
+        if h:
+            step(2, 1, BC + S, ("snd", 0), lambda lo, hi: store(T.yb[:, lo:hi], V("snd", lo, hi)))
+        else:
+            step(2, 0, BA, ("pf", 0), lambda lo, hi: store(T.yf[:, lo:hi], V("pf", lo, hi)))
 
     if "order" not in PLAN:
         PLAN["ops"] = ops
@@ -636,9 +645,9 @@ def times(o, m):
 
 
 def arrange(ops, deps, seed, tries):
-    n = len(ops)
+    n0 = len(ops)
     reach, near = [], []
-    for i in range(n):
+    for i in range(n0):
         r = 0
         for j in deps[i]:
             r |= reach[j]
@@ -646,220 +655,236 @@ def arrange(ops, deps, seed, tries):
         for j in deps[i]:
             r |= 1 << j
         reach.append(r)
-    after = [[] for _ in range(n)]
-    for i in range(n):
-        for j in near[i]:
-            after[j].append(i)
     q = [["dve", "act", "pe", "pool", "sp", "ext"].index(o["q"]) for o in ops]
-    waits = [[j for j in near[i] if q[i] != 2 or q[j] != 2] for i in range(n)]
-    tms = [[times(o, m) for o in ops] for m in SPEEDS]
-    tm = tms[0]
-    tail = [0.0] * n
-    for i in range(n - 1, -1, -1):
-        tail[i] = tm[i][1] + max([tail[j] for j in after[i]] + [0.0])
-    over = set()
+    models = range(len(SPEEDS))
+    out, n = list(range(n0)), n0
+    for i in range(n0):
+        if ops[i]["kind"] in ("dma", "remote"):
+            out[i] = n
+            n += 1
+    pre = [[out[j] for j in near[i]] for i in range(n0)] + [[i] for i in range(n0) if out[i] != i]
+    q += [6] * (n - n0)
+    suc = [[] for _ in range(n)]
+    for i in range(n):
+        for j in pre[i]:
+            suc[j].append(i)
+    hold, lat, other = [[0.0] * n for _ in models], [[0.0] * n for _ in models], [[None] * n for _ in models]
+    for m in models:
+        for i, o in enumerate(ops):
+            a, b, c = times(o, SPEEDS[m])
+            hold[m][i], lat[m][i] = a, b - c
+            if c:
+                hold[m][out[i]] = lat[m][out[i]] = c
+            if "alt" in o:
+                other[m][i] = times(dict(o, **o["alt"]), SPEEDS[m])[:2]
+    over, wake, rnd = set(), [s[4] for s in SPEEDS], [seed]
+
+    def draw(k):
+        rnd[0] = (rnd[0] * 1103515245 + 12345) % 2147483648
+        return (rnd[0] >> 8) % k
 
     def turn_over(i):
         over.symmetric_difference_update([i])
-        o = dict(ops[i], **ops[i]["alt"]) if i in over else ops[i]
-        q[i] = ["dve", "act"].index(o["q"])
-        for t, sp in zip(tms, SPEEDS):
-            t[i] = times(o, sp)
-    rank = [ops[i]["rank"] + (i,) if KN["rule"] else (-tail[i],) for i in range(n)]
-    left, ready, free, order, ring = [len(d) for d in near], [0.0] * n, [0.0] * 6, [], 0.0
+        q[i] = 1 - q[i]
+        for m in models:
+            (hold[m][i], lat[m][i]), other[m][i] = other[m][i], (hold[m][i], lat[m][i])
+
+    tail = [0.0] * n
+    for i in sorted(range(n), key=lambda i: -(i if i < n0 else pre[i][0] + 0.5)):
+        tail[i] = lat[0][i] + max([tail[j] for j in suc[i]] + [0.0])
+    left, ready, free, order = [len(d) for d in pre], [0.0] * n, [0.0] * 7, []
     pool = [i for i in range(n) if not left[i]]
-    while len(order) < n:
+    while pool:
         best = None
-        for k in range(6):
-            mine = [i for i in pool if q[i] == k or (k < 2 and KN["rule"] and "alt" in ops[i])]
+        for k in range(7):
+            mine = [i for i in pool if q[i] == k]
             if mine:
                 t0 = max(free[k], min(ready[i] for i in mine))
-                i = min((i for i in mine if ready[i] <= t0 + KN["ahead"]), key=lambda j: (k == 0 and "alt" in ops[j] and KN["rule"], rank[j]))
-                t = max(free[k], ready[i]) + (KN["lazy"] if k == 0 and "alt" in ops[i] and KN["rule"] else 0.0)
+                i = min((i for i in mine if ready[i] <= t0 + (KN["ahead"] if k < 5 else 0.0)), key=lambda j: -tail[j])
+                t = max(free[k], ready[i])
                 if best is None or t < best[0]:
                     best = (t, i, k)
         t, i, k = best
-        if q[i] != k:
-            turn_over(i)
-        t = max(free[k], ready[i])
         pool.remove(i)
         order.append(i)
-        free[k] = t + tm[i][0]
-        end = t + tm[i][1]
-        if tm[i][2]:
-            ring = end = max(ring + tm[i][2], end)
-        for j in after[i]:
-            ready[j] = max(ready[j], end)
+        free[k] = t + hold[0][i]
+        for j in suc[i]:
+            ready[j] = max(ready[j], t + lat[0][i])
             left[j] -= 1
             if not left[j]:
                 pool.append(j)
-
-    def behind(later, tm):
-        way, last = [0.0] * n, [0.0] * 7
-        for j in reversed(later):
-            a, b, c = tm[j]
-            d = max([way[s] for s in after[j]] + [last[6] if c else 0.0])
-            way[j] = last[q[j]] = max(a + last[q[j]], b + d)
-            if c:
-                last[6] = c + d
-        return [max([way[s] for s in after[i]] + [0.0]) for i in range(n)], last
-
-    def span(part, tm, done, free, start, rest=([0.0] * n, [0.0] * 7)):
-        free, total, end, out = list(free), 0.0, 0.0, rest[0]
-        for i in part:
-            k = q[i]
-            t = free[k]
-            for j in waits[i]:
-                if done[j] > t:
-                    t = done[j]
-            a, b, c = tm[i]
-            start[i] = t
-            free[k] = t + a
-            if c:
-                free[6] = done[i] = t = max(free[6] + c, t + b)
-            else:
-                done[i] = t = t + b
-            total += t
-            if t + out[i] > end:
-                end = t + out[i]
-        end = max([end] + [f + r for f, r in zip(free, rest[1])])
-        return end + KN["soft"] * total / len(part), free, end
-
-    def critical(part, tm, done, free, rest):
-        free, prev, why = list(free), [None] * 7, {}
-        for i in part:
-            k = q[i]
-            t, w = free[k], (prev[k], True)
-            for j in waits[i]:
-                if done[j] > t:
-                    t, w = done[j], (j, False)
-            a, b, c = tm[i]
-            free[k], prev[k], why[i] = t + a, i, w
-            if c:
-                if free[6] + c > t + b:
-                    why[i] = (prev[6], False)
-                free[6] = done[i] = max(free[6] + c, t + b)
-                prev[6] = i
-            else:
-                done[i] = t + b
-        i = max([(done[j] + rest[0][j], j) for j in part] + [(free[k] + rest[1][k], prev[k]) for k in range(7) if prev[k] is not None])[1]
-        pairs = []
-        while i in why:
-            j, same = why[i]
-            if same and j is not None and not reach[i] >> j & 1:
-                pairs.append((j, i))
-            i = j
-        return pairs
-
-    def pack(seq, links, back):
-        at, lows, highs = [0.0] * n, [[] for _ in range(6)], [[] for _ in range(6)]
-        for i in seq:
-            a, b = tm[i][0], tm[i][1]
-            t = b - a if back else 0.0
-            for j in links[i]:
-                u = at[j] + (tm[j][0] + b - a if back else tm[j][1])
-                if u > t:
-                    t = u
-            lo, hi = lows[q[i]], highs[q[i]]
-            z = len(hi)
-            while z and hi[z - 1] > t:
-                z -= 1
-            while z < len(lo) and lo[z] < t + a:
-                t = max(t, hi[z])
-                z += 1
-            lo.insert(z, t)
-            hi.insert(z, t + a)
-            at[i] = t
-        return at
-
-    def worth(seq):
-        c = [span(seq, t, [0.0] * n, [0.0] * 7, [0.0] * n)[2] for t in tms]
-        return c[0] + sum(c)
-
-    best, key, base = (worth(order), order), {i: float(z) for z, i in enumerate(order)}, None
-    for k in range(KN["packs"]):
-        if base is not None:
-            key = list(base)
-            seed = (seed * 1103515245 + 12345) % 2147483648
-            mid, amp = (seed >> 8) % 1000 * max(base) / 1000.0, KN["shake"] * (1 + (seed >> 4) % 4)
-            for i in range(n):
-                seed = (seed * 1103515245 + 12345) % 2147483648
-                if abs(key[i] - mid) < KN["reach"]:
-                    key[i] += amp * ((seed >> 8) % 1000) / 1000.0
-                for j in near[i]:
-                    key[i] = max(key[i], key[j] + 1e-6)
-        for turn in range(2):
-            at = pack(sorted(range(n), key=lambda i: (key[i], i)), near, False)
-            bk = pack(sorted(range(n), key=lambda i: (-at[i] - tm[i][1], -i)), after, True)
-            key = [-bk[i] - tm[i][0] for i in range(n)]
-        at = pack(sorted(range(n), key=lambda i: (key[i], i)), near, False)
-        seq = sorted(range(n), key=lambda i: (at[i], i))
-        c = worth(seq)
-        if base is None or c <= best[0]:
-            best, base = (c, seq), at
-    order = best[1]
-    head = [i for i in range(n) if ops[i]["kind"] == "dma" and not near[i] and q[i] != 3]
+    head = [i for i in range(n0) if ops[i]["kind"] == "dma" and not near[i] and q[i] != 3]
     order = head + [i for i in order if i not in head]
-    start, dones = [0.0] * n, [[0.0] * n for _ in tms]
-    wide, sweeps = KN["wide"], KN["sweeps"]
-    windows = [(s, max(len(head), lo), min(n, lo + wide)) for s in range(sweeps)
-               for lo in range(len(head) - s % 2 * wide // 2, n, wide)]
-    for sweep, lo, hi in windows:
-        part = order[lo:hi]
-        m = len(part)
-        frees = [span(order[:lo], t, d, [0.0] * 7, start)[1] for t, d in zip(tms, dones)]
-        rests = [behind(order[hi:], t) for t in tms]
-        now = [span(part, t, d, f, start, r)[0] for t, d, f, r in zip(tms, dones, frees, rests)]
-        turns, tight, top = tries * m // (n * sweeps), None, (now[0] + sum(now), part, set(over))
-        for k in range(turns):
-            seed = (seed * 1103515245 + 12345) % 2147483648
-            a = (seed >> 8) % m
-            seed = (seed * 1103515245 + 12345) % 2147483648
-            hops, up = 1 + (seed >> 8) % 4, seed >> 20 & 1
-            if tight is None:
-                z = (seed >> 12) % len(tms)
-                tight = critical(part, tms[z], dones[z], frees[z], rests[z])
-            if tight and (seed >> 14) % 8 < KN["aim"]:
-                a = part.index(tight[a % len(tight)][up])
-                hops = 1 + (hops > 2) + (hops > 3)
-            i = part[a]
-            if q[i] == 5:
-                continue
-            other = "alt" in ops[i] and (seed >> 24) % 4 == 0
-            if other:
+    R, Q = [[0.0] * n for _ in models], [[0.0] * n for _ in models]
+    RD, QD = [[0.0] * n for _ in models], [[0.0] * n for _ in models]
+
+    def sweep(part, first, last):
+        ends = []
+        for m in models:
+            r, d, a, b, free, w = R[m], RD[m], hold[m], lat[m], list(first[m]), wake[m]
+            for i in part:
+                t, k = 0.0, q[i]
+                for j in pre[i]:
+                    u = r[j] + (a[j] if k == 2 == q[j] else b[j])
+                    if u > t:
+                        t = u
+                d[i] = t
+                if free[k] > t and k != 5:
+                    t = free[k]
+                r[i] = t
+                free[k] = t + a[i]
+            s, d, free, end = Q[m], QD[m], list(last[m]), 0.0
+            for i in reversed(part):
+                t, k = 0.0, q[i]
+                for j in suc[i]:
+                    u = s[j] - w if k == 2 == q[j] else s[j]
+                    if u > t:
+                        t = u
+                d[i] = t
+                t += b[i]
+                if k != 5 and free[k] + a[i] > t:
+                    t = free[k] + a[i]
+                s[i] = free[k] = t
+                if t + r[i] > end:
+                    end = t + r[i]
+            ends.append(end)
+        return ends
+
+    def relink(part, seqs):
+        cnt, nxt = {i: 0 for i in part}, {}
+        for i in part:
+            for j in suc[i]:
+                if j in cnt:
+                    cnt[j] += 1
+        for k, sq in enumerate(seqs):
+            if k != 5:
+                for x, y in zip(sq, sq[1:]):
+                    nxt[x] = y
+                    cnt[y] += 1
+        res = [i for i in part if not cnt[i]]
+        for i in res:
+            for j in suc[i] + ([nxt[i]] if i in nxt else []):
+                if j in cnt:
+                    cnt[j] -= 1
+                    if not cnt[j]:
+                        res.append(j)
+        return res if len(res) == len(part) else None
+
+    zero, wt = [[0.0] * 7 for _ in models], KN["weights"]
+
+    def settle(seq):
+        for _ in range(2):
+            sweep(seq, zero, zero)
+            at = {j: z for z, j in enumerate(seq)}
+            ring = sorted((j for j in seq if q[j] == 6), key=lambda j: (RD[0][j], at[j]))
+            seq = relink(seq, [[j for j in seq if q[j] == k] for k in range(6)] + [ring]) or seq
+        sweep(seq, zero, zero)
+        at = {j: z for z, j in enumerate(seq)}
+        seq = sorted(seq, key=lambda j: (R[0][j], at[j]))
+        return seq, sweep(seq, zero, zero)
+
+    def moves(v, seqs, first, last, low):
+        k, r0, q0 = q[v], R[0], Q[0]
+        rlim, qlim = r0[v] + lat[0][v] - wake[0] * (k == 2) - 1e-9, QD[0][v] + 1e-9
+        sq = seqs[k]
+        at = sq.index(v)
+        cur = [R[m][sq[at - 1]] + hold[m][sq[at - 1]] if at else first[m][k] for m in models]
+        for z in range(at + 1, min(len(sq), at + KN["far"] + 1)):
+            x, c = sq[z], 0.0
+            if not (r0[x] < rlim or q0[x] > qlim) or reach[x] >> v & 1:
+                break
+            for m in models:
+                t = max(cur[m], RD[m][x])
+                cur[m] = t + hold[m][x]
+                u = max(hold[m][v] + (Q[m][sq[z + 1]] if z + 1 < len(sq) else last[m][k]), lat[m][v] + QD[m][v])
+                c += wt[m] * max(max(cur[m], RD[m][v]) + u, t + lat[m][x] + QD[m][x], low[m])
+            yield c, k, z
+        cur = [Q[m][sq[at + 1]] if at + 1 < len(sq) else last[m][k] for m in models]
+        for z in range(at - 1, max(-1, at - KN["far"] - 1), -1):
+            y, c = sq[z], 0.0
+            if not (r0[y] >= RD[0][v] - 1e-9 or q0[y] <= q0[v]) or reach[v] >> y & 1 or y in fixed:
+                break
+            for m in models:
+                cur[m] = u = max(hold[m][y] + cur[m], lat[m][y] + QD[m][y])
+                t = max(R[m][sq[z - 1]] + hold[m][sq[z - 1]] if z else first[m][k], RD[m][v])
+                c += wt[m] * max(t + max(hold[m][v] + u, lat[m][v] + QD[m][v]), RD[m][y] + u, low[m])
+            yield c, k, z
+        if other[0][v]:
+            k = 1 - k
+            sq = seqs[k]
+            for z in range(len(sq) + 1):
+                if z < len(sq):
+                    y = sq[z]
+                    if not (r0[y] >= RD[0][v] - 1e-9 or q0[y] <= q0[v]) or reach[v] >> y & 1 or y in fixed:
+                        continue
+                if z:
+                    x = sq[z - 1]
+                    if not (r0[x] < rlim or q0[x] > qlim) or reach[x] >> v & 1:
+                        break
+                c = 0.0
+                for m in models:
+                    a, b = other[m][v]
+                    t = max(R[m][x] + hold[m][x] if z else first[m][k], RD[m][v])
+                    c += wt[m] * max(t + max(a + (Q[m][y] if z < len(sq) else last[m][k]), b + QD[m][v]), low[m])
+                yield c, k, z
+
+    order, ends = settle(order)
+    wide, sweeps, fixed = KN["wide"], KN["sweeps"], set(head)
+    for s in range(sweeps):
+        for lo in range(-(s % 2) * (wide // 2), n, wide):
+            lo, hi = max(lo, 0), min(n, lo + wide)
+            sweep(order, zero, zero)
+            first, last = [[0.0] * 7 for _ in models], [[0.0] * 7 for _ in models]
+            for m in models:
+                for i in order[:lo]:
+                    first[m][q[i]] = R[m][i] + hold[m][i]
+                for i in reversed(order[hi:]):
+                    last[m][q[i]] = Q[m][i]
+            part = order[lo:hi]
+            seqs = [[i for i in part if q[i] == k] for k in range(7)]
+            ends = sweep(part, first, last)
+            top, tabu = (sum(w * e for w, e in zip(wt, ends)), part, set(over)), {}
+            for it in range(tries * (hi - lo) // (n * sweeps)):
+                sets = [{i for i in part if R[m][i] + Q[m][i] > ends[m] - 1e-6} for m in models]
+                cand = sorted(i for i in set().union(*sets) if q[i] < 5 and i not in fixed)
+                if not cand:
+                    break
+                if len(cand) > KN["cand"]:
+                    z = draw(len(cand))
+                    cand = [cand[(z + k * 7919) % len(cand)] for k in range(KN["cand"])]
+                best = None
+                for v in cand:
+                    banned = tabu.get(v, -1) >= it
+                    for c, k, z in moves(v, seqs, first, last, [0.0 if v in sets[m] else ends[m] for m in models]):
+                        if (best is None or c < best[0]) and (not banned or c < top[0] - 1e-6):
+                            best = (c, v, k, z)
+                if best is None:
+                    tabu = {}
+                    continue
+                c, v, k, z = best
+                k0 = q[v]
+                at = seqs[k0].index(v)
+                seqs[k0].pop(at)
+                seqs[k].insert(z, v)
+                tabu[v] = it + KN["ban"] + draw(KN["ban"])
+                new = relink(part, seqs)
+                if new is None:
+                    seqs[k].remove(v)
+                    seqs[k0].insert(at, v)
+                    continue
+                if k != k0:
+                    turn_over(v)
+                part = new
+                ends = sweep(part, first, last)
+                now = sum(w * e for w, e in zip(wt, ends))
+                if now <= top[0] + 1e-9:
+                    top = (now, part, set(over))
+            for i in over ^ top[2]:
                 turn_over(i)
-                hops -= 1
-            b, block, rest = a, [i], []
-            while hops and (0 < b if up else b < m - 1):
-                b += -1 if up else 1
-                j = part[b]
-                if (reach[i] >> j if up else reach[j] >> i) & 1:
-                    block.append(j)
-                else:
-                    rest.append(j)
-                    hops -= q[j] == q[i]
-            new = part[:b] + block[::-1] + rest[::-1] + part[a + 1:] if up else part[:a] + rest + block + part[b + 1:]
-            heat = KN["heat"] * (1.0 - k / turns) * (1.0 - sweep / (sweeps + 1.0))
-            if span(new, tm, dones[0], frees[0], start, rests[0])[0] <= now[0] + heat + 0.2:
-                at = {j: z for z, j in enumerate(new)}
-                new = sorted(new, key=lambda j: (start[j], at[j]))
-                c = [span(new, t, d, f, start, r)[0] for t, d, f, r in zip(tms, dones, frees, rests)]
-                if c[0] + sum(c) <= now[0] + sum(now) + heat:
-                    now, part, tight, other = c, new, None, False
-                    if c[0] + sum(c) < top[0]:
-                        top = (c[0] + sum(c), new, set(over))
-            if other:
-                turn_over(i)
-        part = top[1]
-        for i in over ^ top[2]:
-            turn_over(i)
-        order[lo:hi] = part
-        if hi == n:
-            PLAN.setdefault("parts", []).append(round(top[0], 1))
-            span(order, tm, dones[0], [0.0] * 7, start)
-            at = {j: z for z, j in enumerate(order)}
-            order = head + sorted(order[len(head):], key=lambda j: (start[j], at[j]))
-    return order, over
+            order[lo:hi] = top[1]
+        order, ends = settle(order)
+        PLAN.setdefault("parts", []).append([round(e, 1) for e in ends])
+    return [i for i in order if i < n0], over
 
 
 def emit(g, T, ops, deps, order):

@@ -4,22 +4,23 @@ from concourse.mybir import AluOpType as OP, ActivationFunctionType as AF
 S, K = 1024, 4096
 MAGIC = 12582912.0
 CWN = 8480
-WN, NC = 2240, 69
+WN, NC, PC = 2080, 79, 13
 JUNK = 16 * 1024 + 15
 F0, BA, BB, BC = K, 2 * K, 2 * K + S, 2 * K + 2 * S
 KN = {
     "loop": (512, 512, 512, 512, 512, 512, 512, 256, 256),
-    "add": ("mmmmmmddd",) * 3,
-    "cnt": (1024, 1024, 512, 1024, 512), "parts": (2560, 1536),
-    "fl": (1024, 1024, 1024, 1024), "bl": (512, 512, 1024, 1024, 1024),
-    "fs": (513, 512, 1024), "bs": (2048,),
+    "add": ("dmmmmmddd",) * 3,
+    "cnt": (1024, 1536, 1024, 512), "parts": (2560, 1536),
+    "fl": (1024, 1024, 1024, 1024), "bl": (1024, 1024, 1024, 1024),
+    "fs": (513, 512, 1024), "bs": (1024, 1024), "tile": (1040, 260), "clear": "m", "rank": "ll", "early": 1024, "look": ("dadadada",) * 3, "abk": (0, 1, 0, 1, 0, 1, 0, 1, 7, 6),
     "fc": (512,) * 7 + (256, 256), "lc": (512,) * 8,
     "fh": (1024, 1024, 2048), "bh": (1024, 1024, 2048),
-    "sc": (256,) * 4, "wc": (256,) * 4, "ld": 512, "pp": ((512, 512), (1024,)), "old": 8,
+    "sc": (256,) * 4, "wc": (256,) * 4, "ld": 512, "pp": ((512, 512), (1024,)), "ps": (1024, 1024), "old": 0,
     "first": (1, 0, 0),
     "bank": ((0, 512, 1024, 1536), (256, 768, 1280, 1792)),
-    "how": (("g", "g"),) * 3, "hit": (("v", "v"),) * 3, "oka": ("ad", "ad", "dd"), "zero": "aa", "once": 0, "ilb": 2,
-    "seed": 1, "tries": 60000, "wide": 100, "sweeps": 20, "cand": 10, "far": 20, "ban": 10, "ahead": 0.1, "weights": (2, 1, 1),
+    "how": (("g", "g"),) * 3, "hit": (("v", "v"),) * 3, "oka": ("aa", "aa", "ad"), "zero": "mm", "once": 0, "ilb": 2,
+    "seed": 1, "tries": 150000, "wide": 100, "sweeps": 20, "cand": 10, "far": 20, "ban": 10, "few": 4,
+    "starts": ((0, 0.1), (1, 0.1), (2, 0.1), (0, 0.25), (2, 0.25)), "weights": (1, 1, 1),
 }
 
 SCRATCH = {
@@ -32,6 +33,7 @@ SCRATCH = {
     "pa0": ("sbuf", [128, 256], "bfloat16"), "pa1": ("sbuf", [128, 256], "bfloat16"),
     "pf": ("sbuf", [128, S], "float32"), "snd": ("sbuf", [128, S], "float32"),
     "lf": ("sbuf", [128, S], "float32"), "lb": ("sbuf", [128, S], "float32"), "nb": ("sbuf", [128, S], "float32"),
+    "lx": ("sbuf", [128, S], "float32"),
     "win": ("sbuf", [128, 2 * K + 3 * S], "float32"), "dd": ("sbuf", [128, K], "float32"),
     "ab": ("sbuf", [128, 2048], "float32"), "miss": ("sbuf", [128, K], "bfloat16"),
     "wf": ("sbuf", [128, WN], "bfloat16"), "wb": ("sbuf", [128, WN], "bfloat16"),
@@ -40,9 +42,9 @@ SCRATCH = {
     "cw": ("sbuf", [128, CWN], "bfloat16"), "cn": ("sbuf", [128, 2048], "bfloat16"), "cmp": ("sbuf", [128, 2080], "bfloat16"),
     "hit": ("sbuf", [128, 2080], "bfloat16"),
     "hh": ("sbuf", [128, 2048], "float32"), "uu": ("sbuf", [128, 2048], "float32"),
-    "wt": ("sbuf", [128, 144], "bfloat16"), "sm": ("sbuf", [128, 1280], "float32"),
-    "low": ("sbuf", [128, 160], "bfloat16"), "sv": ("sbuf", [128, 160], "bfloat16"), "sl": ("sbuf", [128, 12], "uint16"),
-    "okw": ("sbuf", [128, 256], "bfloat16"), "okb": ("sbuf", [128, 256], "bfloat16"), "oks": ("sbuf", [128, 256], "bfloat16"),
+    "wt": ("sbuf", [128, 176], "bfloat16"), "sm": ("sbuf", [128, 1280], "float32"),
+    "sv": ("sbuf", [128, 160], "bfloat16"), "sl": ("sbuf", [128, 12], "uint16"),
+    "okw": ("sbuf", [128, 256], "bfloat16"),
     "el": ("sbuf", [128, 296], "bfloat16"),
     "al": ("sbuf", [128, 256], "uint16"), "jl": ("sbuf", [128, 256], "uint16"),
     "al2": ("sbuf", [128, 256], "uint16"), "jl1": ("sbuf", [128, 256], "uint16"),
@@ -50,19 +52,21 @@ SCRATCH = {
     "emp": ("sbuf", [128, 256], "float32"), "pl": ("sbuf", [128, 72], "uint16"), "pv": ("sbuf", [128, 272], "bfloat16"),
     "ix": ("sbuf", [128, 128], "float32"), "il": ("sbuf", [128, 128], "uint16"),
     "sel": ("sbuf", [128, 144], "bfloat16"), "sls": ("sbuf", [128, 144], "bfloat16"), "slw": ("sbuf", [128, 144], "bfloat16"),
-    "slb": ("sbuf", [128, 144], "bfloat16"), "slc": ("sbuf", [128, 144], "bfloat16"), "sld": ("sbuf", [128, 144], "bfloat16"),
-    "s2a": ("sbuf", [128, 144], "bfloat16"), "s2b": ("sbuf", [128, 144], "bfloat16"),
-    "s2c": ("sbuf", [128, 144], "bfloat16"), "s2d": ("sbuf", [128, 144], "bfloat16"),
-    "sq4": ("sbuf", [128, 144], "bfloat16"), "sn4": ("sbuf", [128, 144], "bfloat16"),
-    "blk": ("sbuf", [128, 128], "bfloat16"), "tri": ("sbuf", [128, 256], "bfloat16"),
+    "sl1": ("sbuf", [128, 144], "bfloat16"), "sum": ("sbuf", [128, 128], "float32"), "wf1": ("sbuf", [128, WN], "bfloat16"), "wb1": ("sbuf", [128, WN], "bfloat16"),
+    "s2a": ("sbuf", [128, 160], "bfloat16"), "s2b": ("sbuf", [128, 160], "bfloat16"),
+    "s2c": ("sbuf", [128, 160], "bfloat16"), "s2d": ("sbuf", [128, 160], "bfloat16"),
+    "blk": ("sbuf", [128, 128], "bfloat16"), "tri": ("sbuf", [128, 512], "bfloat16"),
     "eye": ("sbuf", [128, 128], "float32"), "eyb": ("sbuf", [128, 128], "bfloat16"),
-    "top": ("sbuf", [128, 256], "float32"), "topb": ("sbuf", [128, 256], "bfloat16"),
-    "off": ("sbuf", [128, 72], "bfloat16"), "one": ("sbuf", [128, 72], "float32"),
-    "zer": ("sbuf", [128, 2064], "bfloat16"), "dec": ("sbuf", [128, 2064], "bfloat16"),
+    "top": ("sbuf", [128, 512], "float32"), "topb": ("sbuf", [128, 256], "bfloat16"),
+    "off": ("sbuf", [128, 88], "bfloat16"), "one": ("sbuf", [128, 80], "float32"), "hb": ("sbuf", [128, 80], "bfloat16"),
+    "zer": ("sbuf", [128, 1040], "bfloat16"), "dec": ("sbuf", [128, 1040], "bfloat16"),
     "nl": ("sbuf", [128, 128], "float32"),
     "kk": ("sbuf", [128, 160], "bfloat16"), "fb": ("sbuf", [128, 128], "float32"),
-    "kd": ("sbuf", [128, 96], "float32"), "cv": ("sbuf", [128, 256], "bfloat16"),
-    "ri": ("sbuf", [128, 8], "int32"), "rc": ("sbuf", [128, 24], "float32"),
+    "kd": ("sbuf", [128, 96], "float32"), "cv": ("sbuf", [128, 272], "bfloat16"),
+    "slm": ("sbuf", [128, 144], "bfloat16"), "slp": ("sbuf", [128, 144], "bfloat16"), "big": ("sbuf", [128, 256], "bfloat16"),
+    "mg": ("sbuf", [128, 256], "bfloat16"), "ng": ("sbuf", [128, 256], "bfloat16"),
+    "gro": ("sbuf", [128, 1040], "bfloat16"), "dfl": ("sbuf", [128, 1040], "bfloat16"),
+    "ri": ("sbuf", [128, 8], "int32"), "rc": ("sbuf", [128, 32], "float32"),
     "ps": ("psum", [128, 4096], "float32"),
 }
 NDMA = 110
@@ -216,9 +220,6 @@ def rank_program(g, core, T, topo):
     def SEL(u, name="sel"):
         return V(name, 15 - u, 143 - u)
 
-    def rows(out, name, lo, hi):
-        mm([(out, SEL(u), V(name, lo + u, hi, 16), u == 0, u == 15) for u in range(16)])
-
     def either(eng, on_act, on_dve):
         for fn in ((on_dve, on_act) if eng == "a" else (on_act, on_dve)):
             fn()
@@ -238,9 +239,17 @@ def rank_program(g, core, T, topo):
     def scale(eng, out, a, s):
         either(eng, lambda: act(out, a, AF.Identity, 0.0, s), lambda: ts(out, a, s, None, OP.mult))
 
-    T_LT, T_GE = V("tri", 0, 128), V("tri", 128, 256)
+    def lin(out, a, s, c):
+        either("a", lambda: act(out, a, AF.Identity, c, s), lambda: ts(out, a, s, c, OP.mult, OP.add))
+
+    def fill(out, c):
+        either("a", lambda: act(out, V("zer", 0, size(out)), AF.Identity, c), lambda: ms(out, c))
+
+    T_LT, T_GE, T_IN, T_NX = (V("tri", 128 * i, 128 * i + 128) for i in range(4))
+    LESS1, TWO, HB, WC = (V("rc", i, i + 1) for i in range(20, 24))
     I_B, I_F, BLK = V("eyb", 0, 128), V("eye", 0, 128), V("blk", 0, 128)
-    ROW4, ROW17, LT15, C75, ROW, IS0, DEC, SCL, END, LESS, ROW2, MORE, HALF, SPARE, W15, W16, ODD = (V("rc", i, i + 1) for i in range(17))
+    ROW4, ROW17, LT15, C75, ROW, IS0, DEC, SCL, END, LESS, ROW2, MORE, HALF, SPARE, W15, W16, ODD, TINY, GRO, DFL = (
+        V("rc", i, i + 1) for i in range(20))
     PARTS = cuts(KN["parts"])
     NP = len(PARTS)
 
@@ -257,10 +266,15 @@ def rank_program(g, core, T, topo):
 
     ms(V("sel", 0, 144), 0.0)
     ms(BLK, 1.0)
-    ms(V("el", 0, 296), 0.0)
-    act(V("wt", 0, 144), V("el", 0, 144), AF.Exp, math.log(128.0), 1.0, 1250.0)
+    ms(V("zer", 0, 176), 0.0)
+    ms(V("zer", 176, 1040), 0.0)
+    act(V("mg", 0, 160), V("zer", 0, 160), AF.Exp, math.log(MAGIC), 1.0, 1450.0)
+    iota(V("pv", 256, 272), [[0, 16]], 1, 0)
+    ms(V("wt", 0, 176), 0.0)
+    iota(V("el", 0, 296), [[0, 296]], 0, 0)
     iota(V("ri", 0, 1), [[0, 1]], 0, 1, small=False)
-    sel(V("sel", 15, 143, 16), V("blk", 0, 8), [[-16, 8]], OP.is_ge, 0.0, 0, 1)
+    ms(V("hb", 0, 8), 0.25)
+    sel(V("sel", 15, 143, 16), V("hb", 0, 8), [[-16, 8]], OP.is_ge, 0.0, 0, 1)
     sel(V("sel", 15, 143, 16), V("sel", 15, 143, 16), [[16, 8]], OP.is_ge, 0.0, 15, -1)
     sel(I_B, BLK, [[-1, 128]], OP.is_equal, 0.0, 0, 1)
     sel(V("topb", 0, 128), BLK, [[-16, 8], [0, 16]], OP.is_equal, 0.0, 0, 1)
@@ -268,66 +282,77 @@ def rank_program(g, core, T, topo):
     sel(BLK, BLK, [[16, 8], [0, 16]], OP.is_ge, 0.0, 15, -1)
     sel(T_LT, BLK, [[1, 128]], OP.is_gt, 0.0, 0, -1)
     sel(T_GE, BLK, [[-1, 128]], OP.is_ge, 0.0, 0, 1)
+    sel(T_NX, BLK, [[1, 128]], OP.is_gt, 0.0, -PC, -1)
+    sel(T_IN, T_LT, [[-1, 128]], OP.is_ge, 0.0, PC, 1)
+    iota(V("s2a", 0, 146), [[0, 146]], 0, 0)
+    sel(V("s2a", 15, 143), BLK, [[0, 8], [-1, 16]], OP.is_ge, 0.0, 1, 0)
     iota(V("kk", 0, 80), [[0, 5], [1, 16]], 0, 0)
     iota(V("kk", 80, 160), [[1, 80]], 0, 0)
     for a, b in PARTS:
-        iota(V("cv", a // 16, b // 16), [[1, (b - a) // 256], [(b - a) // 256, 16]], a // 16, 0)
+        iota(V("cv", a // 16, b // 16), [[-1, (b - a) // 256], [-(b - a) // 256, 16]], 256 - a // 16, 0)
     iota(V("fb", 0, 64), [[64, 64]], K - JUNK, 0)
     iota(V("nl", 0, 128), [[1, 2], [32, 64]], 0, 0)
     iota(V("kd", 0, 24 * NP), [[0, NP], [1, 24]], K + 1, 0)
     load("pool", V("win", BA, BA + S), T.b0[:])
-    for lo, hi in ((0, 1040), (1040, 2064)):
-        ms(V("zer", lo, hi), 0.0)
-    for nm, how in zip(("wb", "wf"), KN["zero"]):
-        if how == "m":
-            move(V(nm, 0, 2064), V("zer", 0, 2064))
-        else:
-            for lo, hi in ((0, 1040), (1040, 2064)):
+    def wipe(nm, how):
+        for lo, hi in ((0, 1040), (1040, 2064)):
+            if how == "m":
+                move(V(nm, lo, hi), V("zer", 0, hi - lo))
+            else:
                 copy(how, V(nm, lo, hi), V("zer", 0, hi - lo))
+
+    def spread(nm, col, wide):
+        shift("d", V(nm, 0, wide), V("zer", 0, wide), col)
+        for lo in range(wide, 1040, wide):
+            move(V(nm, lo, lo + wide), V(nm, 0, wide))
+
+    for nm, how in zip(("wb", "wf"), KN["zero"]):
+        wipe(nm, how)
     for h in range(2):
-        ms(V("hit", 1040 * h + S, 1040 * h + 1040), 0.0)
-    move(V("cw", 0, 2048), V("zer", 0, 2048))
-    ms(V("one", 0, NC), 1.0)
-    ms(LESS, -MAGIC)
-    ms(MORE, MAGIC)
+        fill(V("hit", 1040 * h + S, 1040 * h + 1040), 0.0)
+    fill(V("one", 0, NC), 1.0)
+    fill(LESS, -MAGIC)
+    fill(MORE, MAGIC)
     copy("a", I_F, I_B)
     copy("a", V("top", 0, 128), V("topb", 0, 128))
     tt(V("topb", 128, 256), I_B, V("topb", 0, 128), OP.subtract)
     ts(V("ri", 4, 5), V("ri", 0, 1), 15, None, OP.bitwise_and)
     cp(ROW, V("ri", 4, 5))
     ts(IS0, ROW, 0.0, None, OP.is_equal)
-    ts(DEC, IS0, -1.0, None, OP.add)
-    ts(SCL, IS0, 17.0, -1.0, OP.mult, OP.add)
-    for lo, hi in ((0, 1024), (1024, 2048)):
-        shift("a", V("dec", lo, hi), V("zer", 0, hi - lo), DEC)
-    ts(V("one", NC, NC + 1), IS0, 2.0 ** -12, 2.0 ** -12, OP.mult, OP.add)
-    ts(V("off", 1, NC), V("zer", 1, NC), IS0, -128.0, OP.subtract, OP.add)
-    ms(V("off", 0, 1), -128.0)
-    ts(V("off", NC, NC + 1), IS0, -12.0, -128.0, OP.mult, OP.add)
-    if "b" in KN["hit"][0]:
-        scale("a", V("prm0", 7, 8), V("prm0", 3, 4), -1.0)
-        scale("a", V("sq4", 0, 144), V("sel", 0, 144), 0.25)
-        scale("a", V("sn4", 0, 144), V("sel", 0, 144), -0.25)
-        for h in range(2):
-            ms(V("cmp", 1040 * h + S, 1040 * h + 1040), 0.0)
-    ts(HALF, IS0, 0.5, 0.5, OP.mult, OP.add)
-    scale("a", V("topb", 128, 256), V("topb", 128, 256), HALF)
-    copy("a", V("top", 128, 256), V("topb", 128, 256))
+    lin(DEC, IS0, 1.0, -1.0)
+    lin(SCL, IS0, 17.0, -1.0)
+    spread("dec", DEC, KN["tile"][0])
+    lin(V("one", NC, NC + 1), IS0, 2.0 ** -12, 2.0 ** -12)
+    copy("a", V("off", 0, 1), ROW)
+    fill(V("off", 1, NC), float(PC))
+    lin(V("off", NC, NC + 1), ROW, -1.0, float(S - PC * (NC - 1)))
+    lin(V("off", NC + 1, NC + 2), IS0, 0.25, 0.25)
+    scale("a", V("sum", 0, 128), BLK, 2.0 ** -12)
+    scale("a", V("sum", 0, 128, 16), V("sum", 0, 128, 16), 2.0)
+    fill(LESS1, -MAGIC - 1.0)
+    lin(HALF, IS0, 0.5, 0.5)
+    lin(END, IS0, -1.0, 1.0)
+    lin(TWO, IS0, 1.0, 1.0)
+    scale("a", V("top", 128, 256), V("topb", 128, 256), TWO)
+    scale("a", V("top", 256, 384), I_B, END)
+    scale("a", V("top", 384, 512), I_B, DEC)
     ts(V("kk", 0, 80), V("kk", 0, 80), ROW, -8192.0, OP.not_equal, OP.mult)
-    ts(SPARE, ROW, 16.0, 1984.0, OP.mult, OP.add)
-    shift("a", V("kk", NC, 80), V("kk", NC, 80), SPARE)
-    scale("a", V("kk", 80, 160), V("kk", 80, 160), IS0)
-    ts(W15, IS0, 16.0, -1.0, OP.mult, OP.add)
-    ts(W16, IS0, -0.0625, 1.0, OP.mult, OP.add)
-    scale("a", V("slb", 0, 144), V("sel", 0, 144), W15)
-    scale("a", V("slc", 0, 144), V("sel", 0, 144), DEC)
-    scale("a", V("sld", 0, 144), V("slc", 0, 144), -1.0)
+    shift("a", V("kk", 1, NC), V("kk", 1, NC), 1.0)
+    shift("a", V("kk", NC, 80), V("kk", NC, 80), WN - 16.0)
+    scale("a", SPARE, END, -2.0)
+    lin(V("kk", 81, 80 + NC), V("kk", 81, 80 + NC), IS0, SPARE)
+    scale("a", V("topb", 0, 128), I_B, END)
+    ts(HB, ROW, 1.0, -2.0 ** -13, OP.is_equal, OP.mult)
+    lin(HB, IS0, 0.5, HB)
+    shift("a", V("hb", 0, 80), V("zer", 0, 80), HB)
+    fill(V("ng", 0, 160), -MAGIC)
+    lin(W15, IS0, PC + 1.0, -1.0)
+    lin(W16, IS0, PC / 4.0 - 4.0, 4.0)
+    ts(WC, ROW, 15.5 - PC, -1.0, OP.is_gt, OP.mult)
     scale("a", V("slw", 0, 144), V("sel", 0, 144), W16)
-    for two, one in (("s2b", "slb"), ("s2c", "slc"), ("s2d", "sld"), ("s2a", "slb")):
-        copy("a", V(two, 0, 144), V(one, 0, 144))
-        copy("a", V(two, 16, 144, 16), V(one, 15, 143, 16))
-    for z in (13, 14):
-        copy("a", V("s2a", z, z + 128, 16), V("sld", 15, 143, 16))
+    for two, col in (("s2b", W15), ("s2c", WC), ("s2d", END)):
+        scale("a", V(two, 0, 146), V("s2a", 0, 146), col)
+    tt(V("s2a", 0, 144), V("s2b", 0, 144), V("s2d", 2, 146), OP.add)
     ts(V("ri", 5, 6), V("ri", 0, 1), 1, None, OP.bitwise_and)
     ts(ODD, V("ri", 5, 6), 0.5, 14.75, OP.mult, OP.add)
     ts(V("pu0", 0, 256), V("pi32", 0, 256), 0.5, -0.25, OP.mult, OP.add)
@@ -347,20 +372,30 @@ def rank_program(g, core, T, topo):
     if any(w != "g" for pair in KN["how"] for way in pair for w in way):
         scale("a", V("prm0", 8, 10), V("prm0", 5, 7), -1.0)
         scale("a", V("prm1", 8, 10), V("prm1", 5, 7), -1.0)
-    ms(C75, 7.5)
-    ms(V("emp", 64 * NP - 64, 64 * NP - 40), 1.0)
+    fill(TINY, 0.001)
+    iota(V("cv", 256, 272), [[0, 16]], 256 - S, 0)
     scale("a", ROW4, ROW, 4.0)
     scale("a", ROW17, ROW, 17.0)
     ts(LT15, ROW, 15.0, None, OP.is_lt)
-    scale("a", END, IS0, 1024.0)
-    shift("a", V("pv", 256, 272), V("zer", 0, 16), END)
-    scale("a", V("cv", 0, 256), V("cv", 0, 256), IS0)
+    lin(V("cv", 0, 272), V("cv", 0, 272), IS0, END)
     shift("a", V("fb", 0, 64), V("fb", 0, 64), ROW4)
     scale("a", ROW2, ROW, 2.0)
     shift("a", V("nl", 0, 128), V("nl", 0, 128), ROW2)
     shift("a", V("kd", 0, 24 * NP), V("kd", 0, 24 * NP), ROW17)
     z = 24 * (NP - 1) + KN["parts"][-1] // 256
     scale("a", V("kd", z, z + 1), V("kd", z, z + 1), LT15)
+    for s in range(NP):
+        fill(V("kd", 24 * s + 20, 24 * s + 24), 0.0)
+    scale("a", V("slm", 0, 144), V("sel", 0, 144), -7.0 / 16)
+    scale("a", V("sl1", 0, 144), V("sel", 0, 144), 4.0)
+    scale("a", C75, SCL, -4.0)
+    scale("a", V("slp", 0, 144), V("sel", 0, 144), C75)
+    iota(V("big", 0, 256), [[-16384, 2], [0, 128]], 8192, 0)
+    sel(V("big", 0, 256), V("big", 0, 256), [[0, 2], [-1, 128]], OP.is_equal, 0.0, 0, 1)
+    lin(GRO, IS0, -255.0, 256.0)
+    lin(DFL, IS0, 511.0, 1.0)
+    spread("gro", GRO, KN["tile"][1])
+    spread("dfl", DFL, KN["tile"][1])
 
     def who(t):
         k = "1" if t == 1 else "0"
@@ -368,54 +403,61 @@ def rank_program(g, core, T, topo):
         return {"y": V(pr, t, t + 1), "eps": V(pr, 3, 4), "lam": V(pr, 4, 5), "r": (V(pr, 5, 6), V(pr, 6, 7)),
                 "n": (V(pr, 8, 9), V(pr, 9, 10)), "nz": "nz" + k}
 
+    def window(t, h):
+        return ("wf", "wb")[h] + "1" * (t == 1 and KN["clear"] == "m")
+
     def starts(t, h, pool, bk, bk2):
         pr = (("prm0", "prm0"), ("prm1", "prs1"), ("prm2", "prs2"))[t][h]
         y, eps, at = V(pr, t, t + 1), V(pr, 3, 4), 1040 * h
         for k, (lo, hi) in enumerate(cuts(KN["wc"])):
             a, x = V("ab", S * h + lo, S * h + hi), V("hit", at + lo, at + hi)
             way = KN["hit"][t][h][k % len(KN["hit"][t][h])]
-            if way == "b":
-                ts(x, W(pool, lo, hi), y, eps, OP.subtract, OP.is_le)
-                ts(V("cmp", at + lo, at + hi), W(pool, lo, hi), y, V(pr, 7, 8), OP.subtract, OP.is_lt)
-                continue
             act(a, W(pool, lo, hi), AF.Abs, y, -1.0)
             if way == "v":
-                ts(x, a, eps, 0.25, OP.is_le, OP.mult)
+                ts(x, a, eps, -3.0 / 32, OP.is_le, OP.add)
             else:
                 act(x, a, AF.Sign, eps, -1.0)
-                ts(x, x, -0.5, 0.25, OP.is_gt, OP.mult)
-        if KN["hit"][t][h] == "b":
-            mm([(P(bk, 0, NC), SEL(u, "sq4"), V("hit", at + u, at + 15 * NC, 15), u == 0, False) for u in range(15)])
-            mm([(P(bk, 0, NC), SEL(u, "sn4"), V("cmp", at + u, at + 15 * NC, 15), False, u == 14) for u in range(15)])
-        else:
-            mm([(P(bk, 0, NC), SEL(u), V("hit", at + u, at + 15 * NC, 15), u == 0, u == 14) for u in range(15)])
-        o, w, c = 640 * h, 72 * h, 80 * h
-        C, CT, RHO = V("sm", o, o + NC), V("sm", o + NC, o + NC + 1), V("sm", o + 72, o + 73)
-        E, Q, E0 = (V("sm", o + z, o + z + NC) for z in (80, 160, 240))
-        M, L, vals, sl = V("sm", o + 320, o + 400), V("low", c, c + NC), V("sv", c, c + 80), V("sl", 6 * h, 6 * h + 5)
-        mm([(P(bk2, 0, NC + 1), BLK, V("off", 0, NC + 1), True, False)])
-        ts(V("wt", w + 1, w + NC + 1), P(bk, 0, NC), 127.625, 129.0, OP.add, OP.max)
-        mm([(P(bk2, 0, NC + 1), T_LT, V("wt", w + 1, w + NC + 2), False, False), (P(bk2, 0, NC + 1), T_GE, V("wt", w, w + NC + 1), False, True)])
-        scan(V("sm", o, o + NC + 1), P(bk2, 0, NC + 1), V("one", 0, NC + 1), 0.0, OP.add, OP.mult)
-        rec("dve", lambda: g.vector.reciprocal(ap(RHO), ap(CT)), [CT], [RHO], ("c", 230.0))
+                ts(x, x, -0.5, -3.0 / 32, OP.is_gt, OP.add)
+        mm([(P(bk, 0, NC), I_B, V("mg", 0, NC), True, False)])
+        mm([(P(bk, 0, NC), SEL(u), V("hit", at + u, at + PC * NC, PC), False, u == PC - 1) for u in range(PC)])
+        o, w, c = 640 * h, 88 * h, 80 * h
+        C, CT, RHO = V("sm", o, o + NC), V("sm", o + NC, o + NC + 1), V("sm", o + 88, o + 89)
+        E, Q = (V("sm", o + z, o + z + NC) for z in (96, 192))
+        M, vals, sl = V("sm", o + 320, o + 400), V("sv", c, c + 80), V("sl", 6 * h, 6 * h + 5)
+        sums, marks, dist = P(bk2, 0, NC + 1), P(bk2, 128, 128 + NC), P(bk, 128, 128 + NC)
+        wt, rows, whole = V("wt", w + 1, w + NC + 1), V("sm", o + 90, o + 91), P(bk2, NC + 1, NC + 2)
+        mm([(P(bk2, 0, NC + 2), I_B, V("off", 0, NC + 2), True, False)])
+        rec("act", lambda: g.scalar.activation(ap(wt), ap(P(bk, 0, NC)), AF.Relu, bias=ap(LESS1), scale=1.0, accum_out=ap(rows)),
+            [P(bk, 0, NC), LESS1], [wt, rows], ("c", NC + 25.0))
+        mm([(whole, V("sum", 0, 128), rows, False, False),
+            (sums, T_IN, V("wt", w + 1, w + NC + 2), False, False), (sums, T_GE, V("wt", w, w + NC + 1), False, False),
+            (P(bk2, 0, 1), T_NX, V("wt", w + 1, w + 2), False, False), (sums, T_NX, V("wt", w + 2, w + NC + 3), False, True)])
+        rec("dve", lambda: g.vector.reciprocal(ap(RHO), ap(whole)), [whole], [RHO], ("c", 230.0))
+        mm([(P(bk, 128, 208), I_B, V("kk", 80, 160), True, False), (dist, V("topb", 0, 128), V("mg", 0, NC), False, False)])
+        scan(V("sm", o, o + NC + 1), sums, V("one", 0, NC + 1), 0.0, OP.add, OP.mult)
+        mm([(P(bk2, 128, 208), I_B, V("kk", 0, 80), True, False), (marks, I_B, V("ng", 0, NC), False, False)])
+        mm([(dist, V("top", 256, 384), C, False, False)])
         either("d", lambda: act(E, C, AF.Identity, MORE, RHO), lambda: ts(E, C, RHO, MAGIC, OP.mult, OP.add))
         ts(Q, E, -MAGIC, CT, OP.add, OP.mult)
-        shift("a", E0, E, LESS)
-        tt(L, Q, C, OP.is_lt)
-        for b, z in ((bk2, 0), (bk, 1)):
-            mm([(P(b, 128, 208), I_B, V("kk", 80 * z, 80 * z + 80), True, False),
-                (P(b, 128, 128 + NC), V("top", 128 * z, 128 * z + 128), E0, False, False)])
-            mm([(P(b, 128, 128 + NC), V("topb", 128 * z, 128 * z + 128), L, False, True)])
+        mm([(marks, V("top", 0, 128), E, False, True)])
+        mm([(dist, V("top", 128, 256), E, False, False), (dist, BLK, V("hb", 0, NC), False, False)])
+        mm([(dist, V("top", 384, 512), Q, False, False), (dist, I_B, V("mg", 0, NC), False, False),
+            (dist, I_B, V("ng", 0, NC), False, True)])
         scan(M, P(bk2, 128, 208), V("zer", 0, 80), 0.0, OP.max, OP.add)
         cp(sl, V("sm", o + 335, o + 400, 16))
-        copy("a", vals, P(bk, 128, 208))
-        wn, sn = ("wf", "wb")[h], ("sf", "sb")[h]
+        either("a", lambda: act(vals, P(bk, 128, 208), AF.Relu, 0.0, HALF),
+               lambda: ts(vals, P(bk, 128, 208), HALF, 0.0, OP.mult, OP.max))
+        wn, sn = window(t, h), ("sf", "sb")[h]
         cp((V(wn, 0, WN), sl), vals)
         for lo, hi in cuts(KN["bs" if h else "fs"]):
             scan(V(sn, lo, hi), V(wn, lo, hi), V("dec", 0, hi - lo), V(sn, lo - 1, lo) if lo else -1.0, OP.max, OP.add)
 
     def clear(t, h):
-        if t < 2:
+        if KN["clear"] == "m":
+            if t == 0:
+                wipe(window(0, h), "m")
+                wipe(window(1, h), "m")
+        elif t < 2:
             cp((V(("wf", "wb")[h], 0, WN), V("sl", 6 * h, 6 * h + 5)), V("zer", 0, 80))
 
     def f_ancestors(t, pool):
@@ -423,30 +465,35 @@ def rank_program(g, core, T, topo):
             out, a, b = P((4, 2)[i % 2], lo // 16, hi // 16), lo // 2, hi // 2
             mm([(out, SEL(2 * u, "s2a" if u else "s2b"), V("sf", a + u, b, 8), u == 0, False) for u in range(8)]
                + [(out, SEL(14, "s2d"), V("sf", a + 8, b + 1, 8), False, False)]
-               + [(out, SEL(2 * u, "s2c"), V("wf", a + u + 1, b + 1, 8), False, u == 7) for u in range(8)])
+               + [(out, SEL(2 * u, "s2c"), V(window(t, 0), a + u + 1, b + 1, 8), False, u == 7) for u in range(8)])
             ts(V("al", lo // 16, hi // 16), out, ODD, None, OP.add)
         if t == 2:
             for lo, hi in cuts(KN["fh"]):
-                hand(2, V("al2", lo // 16, hi // 16), V("al", lo // 16, hi // 16))
+                if hi > KN["early"]:
+                    hand(2, V("al2", lo // 16, hi // 16), V("al", lo // 16, hi // 16))
         clear(t, 0)
         for lo, hi in cuts(KN["fc"]):
-            copy("a", V("win", F0 + lo, F0 + hi), (W(pool, 0, S), V("al2" if t == 2 else "al", lo // 16, hi // 16)))
+            if t == 2 and hi <= KN["early"]:
+                copy("a", V("hh", lo, hi), (V("snd", 0, S), V("al", lo // 16, hi // 16)))
+                hand(2, V("lx", lo, hi), V("hh", lo, hi))
+                move(V("win", F0 + lo, F0 + hi), V("lx", lo, hi))
+            else:
+                copy("a", V("win", F0 + lo, F0 + hi), (W(pool, 0, S), V("al2" if t == 2 else "al", lo // 16, hi // 16)))
 
     def b_ancestors(t, base):
         for i, (lo, hi) in enumerate(cuts(KN["bl"])):
             for k, (a, b) in enumerate(cuts(KN["lc"])):
                 if lo <= a < hi:
-                    cut("da"[k % 2], V("xl", a, b), (V("sb", 0, K // 2), V("pu%d" % t, a // 16, b // 16)))
+                    cut(KN["look"][t][k], V("xl", a, b), (V("sb", 0, K // 2), V("pu%d" % t, a // 16, b // 16)))
             out = P((5, 3)[i % 2], lo // 16, hi // 16)
             mm([(out, I_B, V("pa1" if t == 1 else "pa0", lo // 16, hi // 16), True, False)]
                + [(out, SEL(u, "sls" if t else "slw"), V("xl", lo + u, hi, 16), False, u == 15) for u in range(16)])
             cp(V("jl", lo // 16, hi // 16), out)
         out = P(0, 256, 320)
-        items = [(out, SEL(u, nm), V(src, 2 * u + z, K // 2, 32), u == 0 and nm == "slb", u == 15 and nm == "slc")
-                 for nm, src, z in (("slb", "sb", 0), ("sld", "sb", 1), ("slc", "wb", 1)) for u in range(16)]
-        for z in range(0, 48, KN["old"]):
-            mm(items[z:z + KN["old"]])
-        ts(V("fbu", 0, 64) if t else V("fb", 64, 128), out, base + 14.75 - JUNK, None, OP.add)
+        for lo in (0, 512):
+            cut("a", V("cmp", lo, lo + 512), V("sb", 2 * lo, 2 * lo + S, 2))
+        mm([(out, SEL(u, "slw"), V("cmp", u, S, 16), u == 0, u == 15) for u in range(16)])
+        shift("a", V("fbu", 0, 64) if t else V("fb", 64, 128), out, base - 0.25 - JUNK)
         clear(t, 1)
         if t == 1:
             for lo, hi in cuts(KN["bh"]):
@@ -461,22 +508,37 @@ def rank_program(g, core, T, topo):
         for i, (lo, hi) in enumerate(cuts(KN["loop"])):
             z, o = hi - lo, lo % 2048
             d, f, m, x = V("dd", lo, hi), V("win", F0 + lo, F0 + hi), V("win", lo, hi), V("miss", lo, hi)
+            if t == 2 and hi <= KN["early"]:
+                f = V("lx", lo, hi)
             tt(d, (W(pool, 0, S), V("jl1" if t == 1 else "jl", lo // 16, hi // 16)), f, OP.subtract)
-            if KN["add"][t][i] == "d":
-                scale("a", P(i % 2, 0, z), d, p["lam"])
-                tt(m, f, P(i % 2, 0, z), OP.add)
+            way, y = KN["add"][t][i], P(KN["abk"][i], 0, z)
+            if way == "d":
+                scale("a", y, d, p["lam"])
+                tt(m, f, y, OP.add)
+            elif way == "p":
+                mm([(y, I_B, V("zer", 0, z), True, False)])
+                scale("a", y, d, p["lam"])
+                mm([(y, I_F, f, False, True)])
             else:
                 scale("a", m, d, p["lam"])
                 adds(m, f)
-            act(V("ab", o, o + z), m, AF.Abs, p["y"], -1.0)
-            ts(x, V("ab", o, o + z), p["eps"], None, OP.is_gt)
+            act(V("ab", o, o + z), y if way == "p" else m, AF.Abs, p["y"], -1.0)
+            if way == "p":
+                copy("a", m, y)
+            ts(x, V("ab", o, o + z), p["eps"], -0.75, OP.is_gt, OP.add)
             s = max(k for k in range(NP) if PARTS[k][0] <= lo)
             a, b = PARTS[s]
             w = (b - a) // 16
-            mm([(P(7 - 4 * (s % 2), 0, w), SEL(r), V("miss", a + w * r, a + w * r + w), r == 0, r == 15)
-                for r in range((lo - a) // w, (hi - a) // w)])
+            if KN["rank"][s] == "l":
+                if lo == a:
+                    mm([(P(7 - 4 * (s % 2), 0, w), I_B, V("mg", 0, w), True, False)])
+                mm([(P(7 - 4 * (s % 2), 0, w), SEL(r, "slm"), V("miss", a + w * r, a + w * r + w), False, r == 15)
+                    for r in range((lo - a) // w, (hi - a) // w)])
             if hi in ends:
-                rows(P(6 - 4 * (s % 2), ends[hi] // 16, hi // 16), "miss", ends[hi], hi)
+                z = ends[hi]
+                out = P(6 - 4 * (s % 2), z // 16, hi // 16)
+                mm([(out, I_B, V("mg", 0, (hi - z) // 16), True, False)])
+                mm([(out, SEL(u, "slm"), V("miss", z + u, hi, 16), False, u == 15) for u in range(16)])
             if hi == b:
                 columns(t, s)
 
@@ -485,45 +547,46 @@ def rank_program(g, core, T, topo):
         w, c, last = (b - a) // 16, a // 16, s == NP - 1
         nc, e, o = w // 16, c + 8 * s, 64 * s
         ne = nc + last
-        ts(V("okb", c, c + w), P(7 - 4 * (s % 2), 0, w), 7.5, None, OP.is_lt)
-        scan(V("el", e + 1, e + w + 1), V("okb", c, c + w), V("okb", c, c + w), 0.0, OP.add, OP.max)
-        tot = [V("el", PARTS[k][1] // 16 + 8 * k, PARTS[k][1] // 16 + 8 * k + 1) for k in range(s + 1)]
-        if s:
-            mm([(P(5, 400 + s, 401 + s), BLK, tot[k], k == 0, False) for k in range(s)])
-        mm([(P(5, 400 + s, 401 + s), T_LT, tot[s], s == 0, True)])
-        if last:
-            mm([(P(5, 408, 409), BLK, tot[k], k == 0, k == s) for k in range(s + 1)])
-            ts(V("ix", 0, 128), V("nl", 0, 128), P(5, 408, 409), None, OP.is_ge)
-            tt(V("ix", 0, 128), V("ix", 0, 128), V("fb", 0, 128), OP.mult)
-        tt(V("emp", o, o + nc), V("el", e, e + w, 16), V("el", e + 16, e + w + 1, 16), OP.is_equal)
-        tt(V("emp", o + 20, o + 20 + ne), V("emp", o, o + ne), V("kd", 24 * s, 24 * s + ne), OP.mult)
-        tt(V("emp", o + 40, o + 40 + ne), V("emp", o + 20, o + 20 + ne), V("el", e, e + 16 * ne - 15, 16), OP.add)
-        ts(V("pl", 18 * s, 18 * s + ne), V("emp", o + 40, o + 40 + ne), P(5, 400 + s, 401 + s), None, OP.add)
-        cnt = P(6 - 4 * (s % 2), c, c + w)
-        if KN["oka"][t][s] == "a":
-            act(V("oks", c, c + w), cnt, AF.Sign, C75, -1.0)
-            act(V("okw", c, c + w), V("oks", c, c + w), AF.Relu)
+        shift(KN["oka"][t][s], V("okw", c, c + w), P(6 - 4 * (s % 2), c, c + w), LESS)
+        if KN["rank"][s] == "l":
+            scan(V("el", e + 1, e + w + 1), P(7 - 4 * (s % 2), 0, w), V("ng", 0, w), 0.0, OP.add, OP.add)
         else:
-            ts(V("okw", c, c + w), cnt, 7.5, None, OP.is_lt)
-        mm([(P(4, 256 + c, 256 + c + w), I_B, V("cv", c, c + w), True, False)])
-        mm([(P(4, 256 + c + 16 * i, 272 + c + 16 * i), T_LT, V("okw", c + i, c + w, nc), False, i == nc - 1) for i in range(nc)])
-        copy("a", V("pv", c, c + w), P(4, 256 + c, 256 + c + w))
-        cp((V("cw", 0, CWN), V("pl", 18 * s, 18 * s + ne)), V("pv", c, c + 16 * ne))
+            x = P(6 - 4 * (s % 2), 300, 300 + nc)
+            mm([(x, SEL(r, "sl1"), V("okw", c + nc * r, c + nc * r + nc), r == 0, r == 15) for r in range(16)])
+            scan(V("el", e + 16, e + w + 1, 16), x, V("zer", 0, nc), 0.0, OP.add, OP.add)
+        tot = [V("el", PARTS[k][1] // 16 + 8 * k, PARTS[k][1] // 16 + 8 * k + 1) for k in range(s + 1)]
+        z = 400 + 24 * s
+        spare, first, total = P(5, z, z + nc), P(5, z + 20, z + 21), P(5, z + 21, z + 22)
+        mm([(P(5, z, z + 24), I_F, V("kd", 24 * s, 24 * s + 24), True, False)]
+           + [(x, BLK, tot[k], False, False) for k in range(s) for x in ((first, total) if last else (first,))])
+        mm([(spare, V("big", 0, 128), V("el", e, e + w, 16), False, False),
+            (spare, V("big", 128, 256), V("el", e + 16, e + w + 1, 16), False, False)]
+           + [(total, BLK, tot[s], False, False)] * last + [(first, T_LT, tot[s], False, True)])
+        tt(V("emp", o, o + ne), V("el", e, e + 16 * ne - 15, 16), P(5, z, z + ne), OP.max)
+        ts(V("pl", 18 * s, 18 * s + ne), V("emp", o, o + ne), first, None, OP.add)
+        if last:
+            ts(V("ix", 0, 128), V("nl", 0, 128), total, None, OP.is_ge)
+            tt(V("ix", 0, 128), V("ix", 0, 128), V("fb", 0, 128), OP.mult)
+        mm([(P(4, 256 + c + 16 * i, 272 + c + 16 * i), T_LT, V("okw", c + i, c + w, nc), True, True) for i in range(nc)])
+        act(V("pv", c, c + w), P(4, 256 + c, 256 + c + w), AF.Exp, TINY, -8.0 * math.log(2.0))
+        tt((V("cw", 0, CWN), V("pl", 18 * s, 18 * s + ne)), V("pv", c, c + 16 * ne), V("cv", c, c + 16 * ne), OP.mult)
+
+    def fresh():
+        for lo in (0, S):
+            move(V("cw", lo, lo + S), V("dfl", 0, S))
 
     def places(t):
-        for lo, hi in cuts(KN["pp"][0]):
-            scan(V("cn", 2 * lo, 2 * hi), V("cw", 2 * lo, 2 * hi), V("dec", 0, 2 * (hi - lo)),
-                 V("cn", 2 * lo - 1, 2 * lo) if lo else -1.0, OP.max, OP.add)
+        for lo, hi in cuts(KN["ps"]):
+            scan(V("cn", lo, hi), V("gro", 0, hi - lo), V("cw", lo, hi), V("cn", lo - 1, lo) if lo else V("dfl", 0, 1), OP.mult, OP.min)
         if t < 2:
-            move(V("cw", 0, 2048), V("zer", 0, 2048))
+            fresh()
         z = KN["ilb"]
         for k, h in enumerate((KN["first"][t], 1 - KN["first"][t])):
             for lo, hi in cuts(KN["pp"][k]):
-                a, b, at = 64 * h + lo // 16, 64 * h + hi // 16, 1040 * h
-                cut("da"[k], V("cmp", at + lo, at + hi), V("cn", 2 * lo + h, 2 * hi, 2))
+                a, b = 64 * h + lo // 16, 64 * h + hi // 16
                 mm([(P(z, 0, b - a), I_F, V("ix", a, b), True, False)])
-                mm([(P(z, 0, b - a), SEL(u), V("cmp", at + lo + u, at + hi, 16), False, u == 15) for u in range(16)])
-                cp(V("il", a, b), P(z, 0, b - a))
+                mm([(P(z, 0, b - a), SEL(u, "slp"), V("cn", 2 * (lo + u) + h, 2 * hi, 32), False, u == 15) for u in range(16)])
+                ts(V("il", a, b), P(z, 0, b - a), float(K), None, OP.add)
                 z += 1
 
     def step(t, h, end, dst, done):
@@ -533,10 +596,7 @@ def rank_program(g, core, T, topo):
         for k, (lo, hi) in enumerate(cuts(KN["sc"])):
             z = KN["bank"][late][k]
             x = P(0, z, z + hi - lo)
-            if not KN["once"]:
-                mm([(x, I_B, V("zer", 0, hi - lo), True, False)])
-            elif not late:
-                mm([(P(0, z, z + 512), I_B, V("zer", 0, 512), True, False)])
+            mm([(x, I_B, V("zer", 0, hi - lo), True, False)])
             gat = (V("win", 0, end), V("il", 64 * h + lo // 16, 64 * h + hi // 16))
             hh, uu = (V(nm, S * h + lo, S * h + hi) for nm in ("hh", "uu"))
             way = how[k % len(how)]
@@ -553,7 +613,7 @@ def rank_program(g, core, T, topo):
                 act(uu, hh, AF.Square)
                 mm([(uu, I_F, hh, False, False)])
             scale("a", x, uu, p["r" if way == "g" else "n"][h])
-            mm([(x, I_B, V(p["nz"], lo, hi), False, bool(late or not KN["once"]))])
+            mm([(x, I_B, V(p["nz"], lo, hi), False, True)])
             ts(W(dst, lo, hi), x, 0.0, 1.0, OP.max, OP.min)
             if t == 2 or hi % 512 == 0:
                 done(lo if t == 2 else hi - 512, hi)
@@ -564,8 +624,9 @@ def rank_program(g, core, T, topo):
                 v = V("dd", S * i + lo, S * i + lo + 512)
                 either("a", lambda v=v: act(v, v, AF.Square), lambda v=v: tt(v, v, v, OP.mult))
                 act(v, v, AF.Exp, 0.0, -1.0)
-                if i:
-                    adds(V("dd", lo, lo + 512), v)
+                if i % 2:
+                    adds(V("dd", S * i - S + lo, S * i - S + lo + 512), v)
+            adds(V("dd", lo, lo + 512), V("dd", 2 * S + lo, 2 * S + lo + 512))
             store(T.ye[:, lo:lo + 512], V("dd", lo, lo + 512))
 
     def nothing(lo, hi):
@@ -577,6 +638,7 @@ def rank_program(g, core, T, topo):
         pairs(t, b)
         places(t)
 
+    fresh()
     starts(0, 1, ("b16", 0), 6, 7)
     starts(0, 0, ("f16", 0), 2, 3)
     ancestors(0, ("f16", 0), ("b16", 0), BA)
@@ -632,8 +694,8 @@ def depends(ops):
     return deps
 
 
-SPEEDS = ((1.56, 3.8, 1.8, 450e3, 0.2, 0.00045, 1.25), (1.1, 2.0, 1.6, 500e3, 0.1, 0.00042, 1.1),
-          (2.0, 5.6, 2.0, 400e3, 0.25, 0.0005, 1.4))
+SPEEDS = ((1.56, 3.8, 1.6, 450e3, 0.22, 0.0006, 1.05), (1.25, 3.0, 1.7, 430e3, 0.27, 0.00042, 1.3),
+          (1.85, 4.5, 1.7, 420e3, 0.18, 0.00045, 1.3))
 
 
 def times(o, m):
@@ -689,32 +751,35 @@ def arrange(ops, deps, seed, tries):
         for m in models:
             (hold[m][i], lat[m][i]), other[m][i] = other[m][i], (hold[m][i], lat[m][i])
 
-    tail = [0.0] * n
-    for i in sorted(range(n), key=lambda i: -(i if i < n0 else pre[i][0] + 0.5)):
-        tail[i] = lat[0][i] + max([tail[j] for j in suc[i]] + [0.0])
-    left, ready, free, order = [len(d) for d in pre], [0.0] * n, [0.0] * 7, []
-    pool = [i for i in range(n) if not left[i]]
-    while pool:
-        best = None
-        for k in range(7):
-            mine = [i for i in pool if q[i] == k]
-            if mine:
-                t0 = max(free[k], min(ready[i] for i in mine))
-                i = min((i for i in mine if ready[i] <= t0 + (KN["ahead"] if k < 5 else 0.0)), key=lambda j: -tail[j])
-                t = max(free[k], ready[i])
-                if best is None or t < best[0]:
-                    best = (t, i, k)
-        t, i, k = best
-        pool.remove(i)
-        order.append(i)
-        free[k] = t + hold[0][i]
-        for j in suc[i]:
-            ready[j] = max(ready[j], t + lat[0][i])
-            left[j] -= 1
-            if not left[j]:
-                pool.append(j)
     head = [i for i in range(n0) if ops[i]["kind"] == "dma" and not near[i] and q[i] != 3]
-    order = head + [i for i in order if i not in head]
+
+    def opening(m, ahead):
+        tail = [0.0] * n
+        for i in sorted(range(n), key=lambda i: -(i if i < n0 else pre[i][0] + 0.5)):
+            tail[i] = lat[m][i] + max([tail[j] for j in suc[i]] + [0.0])
+        left, ready, free, order = [len(d) for d in pre], [0.0] * n, [0.0] * 7, []
+        pool = [i for i in range(n) if not left[i]]
+        while pool:
+            best = None
+            for k in range(7):
+                mine = [i for i in pool if q[i] == k]
+                if mine:
+                    t0 = max(free[k], min(ready[i] for i in mine))
+                    i = min((i for i in mine if ready[i] <= t0 + (ahead if k < 5 else 0.0)), key=lambda j: -tail[j])
+                    t = max(free[k], ready[i])
+                    if best is None or t < best[0]:
+                        best = (t, i, k)
+            t, i, k = best
+            pool.remove(i)
+            order.append(i)
+            free[k] = t + hold[m][i]
+            for j in suc[i]:
+                ready[j] = max(ready[j], t + lat[m][i])
+                left[j] -= 1
+                if not left[j]:
+                    pool.append(j)
+        return head + [i for i in order if i not in head]
+
     R, Q = [[0.0] * n for _ in models], [[0.0] * n for _ in models]
     RD, QD = [[0.0] * n for _ in models], [[0.0] * n for _ in models]
 
@@ -828,9 +893,14 @@ def arrange(ops, deps, seed, tries):
                     c += wt[m] * max(t + max(a + (Q[m][y] if z < len(sq) else last[m][k]), b + QD[m][v]), low[m])
                 yield c, k, z
 
-    order, ends = settle(order)
-    wide, sweeps, fixed = KN["wide"], KN["sweeps"], set(head)
+    wide, few, fixed, kept = KN["wide"], KN["few"], set(head), []
+    trial = few * len(KN["starts"])
+    sweeps = trial + KN["sweeps"]
     for s in range(sweeps):
+        if s < trial and s % few == 0:
+            for i in set(over):
+                turn_over(i)
+            order, ends = settle(opening(*KN["starts"][s // few]))
         for lo in range(-(s % 2) * (wide // 2), n, wide):
             lo, hi = max(lo, 0), min(n, lo + wide)
             sweep(order, zero, zero)
@@ -884,6 +954,12 @@ def arrange(ops, deps, seed, tries):
             order[lo:hi] = top[1]
         order, ends = settle(order)
         PLAN.setdefault("parts", []).append([round(e, 1) for e in ends])
+        if s < trial and s % few == few - 1:
+            kept.append((sum(w * e for w, e in zip(wt, ends)), s, order, set(over)))
+        if s == trial - 1:
+            order = min(kept)[2]
+            for i in over ^ min(kept)[3]:
+                turn_over(i)
     return [i for i in order if i < n0], over
 
 

import math
from concourse.mybir import AluOpType as OP, ActivationFunctionType as AF

S, K = 1024, 4096
MAGIC = 12582912.0
CWN = 8480
WN, NC, PC = 2080, 79, 13
JUNK = 16 * 1024 + 15
F0, BA, BB, BC = K, 2 * K, 2 * K + S, 2 * K + 2 * S
KN = {
    "loop": (512, 512, 512, 512, 512, 512, 512, 256, 256),
    "add": ("dmmmmmddd",) * 3,
    "cnt": (1024, 1536, 1024, 512), "parts": (2560, 1536),
    "fl": (1024, 1024, 1024, 1024), "bl": (1024, 1024, 1024, 1024),
    "fs": (513, 512, 1024), "bs": (1024, 1024), "tile": (1040, 260), "clear": "m", "rank": "ll", "early": 1024, "look": ("dadadada",) * 3, "abk": (0, 1, 0, 1, 0, 1, 0, 1, 7, 6),
    "fc": (512,) * 7 + (256, 256), "lc": (512,) * 8,
    "fh": (1024, 1024, 2048), "bh": (1024, 1024, 2048),
    "sc": (256,) * 4, "wc": (256,) * 4, "ld": 512, "pp": ((512, 512), (1024,)), "ps": (1024, 1024), "old": 0,
    "first": (1, 0, 0),
    "bank": ((0, 512, 1024, 1536), (256, 768, 1280, 1792)),
    "how": (("g", "g"),) * 3, "hit": (("v", "v"),) * 3, "oka": ("aa", "aa", "ad"), "zero": "mm", "once": 0, "ilb": 2,
    "seed": 1, "tries": 150000, "wide": 100, "sweeps": 20, "cand": 10, "far": 20, "ban": 10, "few": 4,
    "starts": ((0, 0.1), (1, 0.1), (2, 0.1), (0, 0.25), (2, 0.25)), "weights": (1, 1, 1),
}

SCRATCH = {
    "f16": ("sbuf", [128, S], "bfloat16"), "b16": ("sbuf", [128, S], "bfloat16"),
    "nz0": ("sbuf", [128, S], "bfloat16"), "nz1": ("sbuf", [128, S], "bfloat16"),
    "prm0": ("sbuf", [128, 12], "float32"), "prm1": ("sbuf", [128, 12], "float32"), "prm2": ("sbuf", [128, 8], "float32"),
    "prs1": ("sbuf", [128, 4], "float32"), "prs2": ("sbuf", [128, 4], "float32"),
    "pi32": ("sbuf", [128, 256], "int32"),
    "pu0": ("sbuf", [128, 256], "uint16"), "pu1": ("sbuf", [128, 256], "uint16"), "pu2": ("sbuf", [128, 256], "uint16"),
    "pa0": ("sbuf", [128, 256], "bfloat16"), "pa1": ("sbuf", [128, 256], "bfloat16"),
    "pf": ("sbuf", [128, S], "float32"), "snd": ("sbuf", [128, S], "float32"),
    "lf": ("sbuf", [128, S], "float32"), "lb": ("sbuf", [128, S], "float32"), "nb": ("sbuf", [128, S], "float32"),
    "lx": ("sbuf", [128, S], "float32"),
    "win": ("sbuf", [128, 2 * K + 3 * S], "float32"), "dd": ("sbuf", [128, K], "float32"),
    "ab": ("sbuf", [128, 2048], "float32"), "miss": ("sbuf", [128, K], "bfloat16"),
    "wf": ("sbuf", [128, WN], "bfloat16"), "wb": ("sbuf", [128, WN], "bfloat16"),
    "sf": ("sbuf", [128, 2064], "bfloat16"), "sb": ("sbuf", [128, 2064], "bfloat16"),
    "xl": ("sbuf", [128, K], "bfloat16"),
    "cw": ("sbuf", [128, CWN], "bfloat16"), "cn": ("sbuf", [128, 2048], "bfloat16"), "cmp": ("sbuf", [128, 2080], "bfloat16"),
    "hit": ("sbuf", [128, 2080], "bfloat16"),
    "hh": ("sbuf", [128, 2048], "float32"), "uu": ("sbuf", [128, 2048], "float32"),
    "wt": ("sbuf", [128, 176], "bfloat16"), "sm": ("sbuf", [128, 1280], "float32"),
    "sv": ("sbuf", [128, 160], "bfloat16"), "sl": ("sbuf", [128, 12], "uint16"),
    "okw": ("sbuf", [128, 256], "bfloat16"),
    "el": ("sbuf", [128, 296], "bfloat16"),
    "al": ("sbuf", [128, 256], "uint16"), "jl": ("sbuf", [128, 256], "uint16"),
    "al2": ("sbuf", [128, 256], "uint16"), "jl1": ("sbuf", [128, 256], "uint16"),
    "fbu": ("sbuf", [128, 64], "float32"), "fb1": ("sbuf", [128, 64], "float32"),
    "emp": ("sbuf", [128, 256], "float32"), "pl": ("sbuf", [128, 72], "uint16"), "pv": ("sbuf", [128, 272], "bfloat16"),
    "ix": ("sbuf", [128, 128], "float32"), "il": ("sbuf", [128, 128], "uint16"),
    "sel": ("sbuf", [128, 144], "bfloat16"), "sls": ("sbuf", [128, 144], "bfloat16"), "slw": ("sbuf", [128, 144], "bfloat16"),
    "sl1": ("sbuf", [128, 144], "bfloat16"), "sum": ("sbuf", [128, 128], "float32"), "wf1": ("sbuf", [128, WN], "bfloat16"), "wb1": ("sbuf", [128, WN], "bfloat16"),
    "s2a": ("sbuf", [128, 160], "bfloat16"), "s2b": ("sbuf", [128, 160], "bfloat16"),
    "s2c": ("sbuf", [128, 160], "bfloat16"), "s2d": ("sbuf", [128, 160], "bfloat16"),
    "blk": ("sbuf", [128, 128], "bfloat16"), "tri": ("sbuf", [128, 512], "bfloat16"),
    "eye": ("sbuf", [128, 128], "float32"), "eyb": ("sbuf", [128, 128], "bfloat16"),
    "top": ("sbuf", [128, 512], "float32"), "topb": ("sbuf", [128, 256], "bfloat16"),
    "off": ("sbuf", [128, 88], "bfloat16"), "one": ("sbuf", [128, 80], "float32"), "hb": ("sbuf", [128, 80], "bfloat16"),
    "zer": ("sbuf", [128, 1040], "bfloat16"), "dec": ("sbuf", [128, 1040], "bfloat16"),
    "nl": ("sbuf", [128, 128], "float32"),
    "kk": ("sbuf", [128, 160], "bfloat16"), "fb": ("sbuf", [128, 128], "float32"),
    "kd": ("sbuf", [128, 96], "float32"), "cv": ("sbuf", [128, 272], "bfloat16"),
    "slm": ("sbuf", [128, 144], "bfloat16"), "slp": ("sbuf", [128, 144], "bfloat16"), "big": ("sbuf", [128, 256], "bfloat16"),
    "mg": ("sbuf", [128, 256], "bfloat16"), "ng": ("sbuf", [128, 256], "bfloat16"),
    "gro": ("sbuf", [128, 1040], "bfloat16"), "dfl": ("sbuf", [128, 1040], "bfloat16"),
    "ri": ("sbuf", [128, 8], "int32"), "rc": ("sbuf", [128, 32], "float32"),
    "ps": ("psum", [128, 4096], "float32"),
}
NDMA = 110
SEMAPHORES = ["pe", "dve", "act", "pool"] + ["x%d" % i for i in range(24)] + ["d%d" % i for i in range(NDMA)]
PLAN = {}


def rank_program(g, core, T, topo):
    rank = T.rank_of(core)
    if rank is None:
        return
    n = len(T.cores)
    ops = []

    def V(name, lo, hi, step=1):
        return (name, lo, hi, step)

    def P(bank, lo, hi, step=1):
        return ("ps", 512 * bank + lo, 512 * bank + hi, step)

    def W(pool, lo, hi):
        return V(pool[0], pool[1] + lo, pool[1] + hi)

    def num(v):
        return isinstance(v, (int, float)) or v is None

    def ap(v):
        if num(v):
            return v
        if len(v) == 2:
            return ap(v[0]).indirect(ap(v[1]))
        t = T[v[0]]
        return t[:, v[1]:v[2]] if v[3] == 1 else t[:, v[1]:v[2]:v[3]]

    def size(v):
        return 16 * size(v[1]) if len(v) == 2 else (v[2] - v[1] + v[3] - 1) // v[3]

    def width(v):
        return 2 if SCRATCH[v[0]][2] in ("bfloat16", "uint16") else 4

    def regions(vs):
        out = []
        for v in vs:
            if not num(v):
                for w in (v if len(v) == 2 else (v,)):
                    out.append(("ps", w[1] // 512 * 512, (w[2] + 511) // 512 * 512) if w[0] == "ps" else (w[0], w[1], w[2]))
        return out

    def rec(q, fn, rd, wr, cost, kind="c", sem=None):
        r, w = regions(rd), []
        for v in wr:
            if len(v) == 2:
                r += regions([v[1]])
                w += regions([v[0]])
            else:
                w += regions([v])
        ops.append({"q": q, "fn": fn, "r": r, "w": w, "kind": kind, "sem": sem, "cost": cost})

    def price(out, ins, per=1.0, fast=False):
        if len(out) == 2:
            return ("sc", size(out))
        if len(ins[0]) == 2:
            return ("g", size(out))
        if fast and all(width(v) == 2 for v in [out] + ins):
            per = 0.5
        return ("c", max(64.0, per * size(out)))

    def ts(out, a, s1, s2, o0, o1=None):
        if o1 is None:
            rec("dve", lambda: g.vector.tensor_scalar(ap(out), ap(a), ap(s1), None, o0), [a, s1], [out], price(out, [a], 1.0, True))
        else:
            rec("dve", lambda: g.vector.tensor_scalar(ap(out), ap(a), ap(s1), ap(s2), o0, o1), [a, s1, s2], [out], price(out, [a], 1.0, True))

    def tt(out, a, b, o):
        rec("dve", lambda: g.vector.tensor_tensor(ap(out), ap(a), ap(b), o), [a, b], [out],
            price(out, [a, b], 1.0 if "ps" in (a[0], b[0]) else 2.0))

    def cp(out, a):
        rec("dve", lambda: g.vector.tensor_copy(ap(out), ap(a)), [a], [out], price(out, [a], 1.0, True))

    def ms(out, c):
        rec("dve", lambda: g.vector.memset(ap(out), c), [], [out], price(out, [out], 1.0, True))

    def scan(out, a, b, init, o0, o1):
        rec("dve", lambda: g.vector.tensor_tensor_scan(ap(out), ap(a), ap(b), ap(init), o0, o1), [a, b, init], [out],
            price(out, [a, b], 1.0, True))

    def act(out, a, f, bias=0.0, scale=1.0, more=0.0):
        k, c = price(out, [a])
        rec("act", lambda: g.scalar.activation(ap(out), ap(a), f, bias=ap(bias), scale=ap(scale)), [a, bias, scale], [out], (k, c + more))

    def mm(items):
        def fn():
            for (o, l, r, st, sp) in items:
                last = g.tensor.matmul(ap(o), ap(l), ap(r), st, sp)
            return last
        rec("pe", fn, [x for it in items for x in it[1:3]], [it[0] for it in items],
            ("pe", sum(max(64, size(it[2])) * (4 if width(it[1]) == 4 else 1) for it in items)))

    def iota(out, pat, base, cm, small=True):
        c = ("c", 160 + 2 * size(out))
        if small:
            rec("pool", lambda: g.iota(ap(out), pat, base, cm, allow_small_or_imprecise_dtypes=True), [], [out], c)
        else:
            rec("pool", lambda: g.iota(ap(out), pat, base, cm), [], [out], c)

    def sel(out, a, pat, o, fill, base, cm):
        rec("pool", lambda: g.affine_select(ap(out), ap(a), pat, o, fill, base, cm), [a], [out], ("c", 200 + 2 * size(out)))

    def load(q, out, src):
        eng = {"sp": g.sync, "act": g.scalar, "pool": g}[q]
        rec(q, lambda: eng.dma_start(ap(out), src), [], [out], ("dma", 128 * size(out) * width(out)), "dma")

    def store(dst, a):
        rec("sp", lambda: g.sync.dma_start(dst, ap(a)), [a], [], ("dma", 128 * size(a) * width(a)), "dma")

    def move(out, a):
        rec("sp", lambda: g.sync.dma_start(ap(out), ap(a)), [a], [out], ("dma", 128 * size(a) * width(a)), "dma")

    def turn(out, a, by):
        def piece(src, dst, m, mark):
            rec("sp", lambda: g.sync.dma_start(T[out[0]][dst:dst + m, out[1]:out[2]], T[a[0]][src:src + m, a[1]:a[2]]),
                [a], [out], ("dma", m * size(a) * width(a)), "dma")
            ops[-1]["rows"] = mark
        sent[1] += 1
        piece(0, by % 128, 128 - by % 128, sent[1])
        piece(128 - by % 128, 0, by % 128, sent[1])

    def adds(out, a):
        rec("pool", lambda: g.dma_start(ap(out), ap(a), accum_op=OP.add), [a, out], [out], ("dma", 256 * size(a) * width(a)), "dma")

    sent = [0, 0]

    def hand(by, out, a):
        rsem = "x%d" % sent[0]
        sent[0] += 1
        dst = T.cores[(rank + by) % n]
        rid, pid, _ = topo.addr(dst)
        m = topo.mask(core, dst)
        rec("pool", lambda ls: g.remote_dma(ap(out), ap(a), T.sem[rsem], ls, pid, rid, m), [a], [],
            ("dma", 128 * size(a) * width(a)), "remote", (rsem, len(topo.engines(core, dst))))
        rec("ext", None, [], [out], ("c", 0.0), "ext", (rsem, len(topo.engines(T.cores[(rank - by) % n], core))))

    def cuts(sizes):
        out, lo = [], 0
        for z in sizes:
            out.append((lo, lo + z))
            lo += z
        return out

    def SEL(u, name="sel"):
        return V(name, 15 - u, 143 - u)

    def either(eng, on_act, on_dve):
        for fn in ((on_dve, on_act) if eng == "a" else (on_act, on_dve)):
            fn()
        alt = ops.pop(-2)
        ops[-1]["alt"] = {k: alt[k] for k in ("q", "fn", "cost")}
        ops[-1]["r"] += [x for x in alt["r"] if x not in ops[-1]["r"]]

    def cut(eng, out, a):
        either(eng, lambda: act(out, a, AF.Relu, 0.0, SCL), lambda: ts(out, a, SCL, 0.0, OP.mult, OP.max))

    def copy(eng, out, a):
        either(eng, lambda: act(out, a, AF.Copy), lambda: cp(out, a))

    def shift(eng, out, a, s):
        either(eng, lambda: act(out, a, AF.Identity, s), lambda: ts(out, a, s, None, OP.add))

    def scale(eng, out, a, s):
        either(eng, lambda: act(out, a, AF.Identity, 0.0, s), lambda: ts(out, a, s, None, OP.mult))

    def lin(out, a, s, c):
        either("a", lambda: act(out, a, AF.Identity, c, s), lambda: ts(out, a, s, c, OP.mult, OP.add))

    def fill(out, c):
        either("a", lambda: act(out, V("zer", 0, size(out)), AF.Identity, c), lambda: ms(out, c))

    T_LT, T_GE, T_IN, T_NX = (V("tri", 128 * i, 128 * i + 128) for i in range(4))
    LESS1, TWO, HB, WC = (V("rc", i, i + 1) for i in range(20, 24))
    I_B, I_F, BLK = V("eyb", 0, 128), V("eye", 0, 128), V("blk", 0, 128)
    ROW4, ROW17, LT15, C75, ROW, IS0, DEC, SCL, END, LESS, ROW2, MORE, HALF, SPARE, W15, W16, ODD, TINY, GRO, DFL = (
        V("rc", i, i + 1) for i in range(20))
    PARTS = cuts(KN["parts"])
    NP = len(PARTS)

    load("sp", V("prm0", 0, 3), T.obs[:])
    load("sp", V("prm0", 3, 4), T.eps[:])
    for nm, src in (("b16", T.b0), ("f16", T.f0)):
        for lo in range(0, S, KN["ld"]):
            load("act", V(nm, lo, lo + KN["ld"]), src[:, lo:lo + KN["ld"]])
    load("sp", V("pi32", 0, 256), T.pi[:])
    load("sp", V("prm0", 4, 5), T.lam[:])
    load("sp", V("prm0", 5, 6), T.rf[:])
    load("sp", V("prm0", 6, 7), T.rb[:])
    load("sp", V("nz0", 0, S), T.nz[:])

    ms(V("sel", 0, 144), 0.0)
    ms(BLK, 1.0)
    ms(V("zer", 0, 176), 0.0)
    ms(V("zer", 176, 1040), 0.0)
    act(V("mg", 0, 160), V("zer", 0, 160), AF.Exp, math.log(MAGIC), 1.0, 1450.0)
    iota(V("pv", 256, 272), [[0, 16]], 1, 0)
    ms(V("wt", 0, 176), 0.0)
    iota(V("el", 0, 296), [[0, 296]], 0, 0)
    iota(V("ri", 0, 1), [[0, 1]], 0, 1, small=False)
    ms(V("hb", 0, 8), 0.25)
    sel(V("sel", 15, 143, 16), V("hb", 0, 8), [[-16, 8]], OP.is_ge, 0.0, 0, 1)
    sel(V("sel", 15, 143, 16), V("sel", 15, 143, 16), [[16, 8]], OP.is_ge, 0.0, 15, -1)
    sel(I_B, BLK, [[-1, 128]], OP.is_equal, 0.0, 0, 1)
    sel(V("topb", 0, 128), BLK, [[-16, 8], [0, 16]], OP.is_equal, 0.0, 0, 1)
    sel(BLK, BLK, [[-16, 8], [0, 16]], OP.is_ge, 0.0, 0, 1)
    sel(BLK, BLK, [[16, 8], [0, 16]], OP.is_ge, 0.0, 15, -1)
    sel(T_LT, BLK, [[1, 128]], OP.is_gt, 0.0, 0, -1)
    sel(T_GE, BLK, [[-1, 128]], OP.is_ge, 0.0, 0, 1)
    sel(T_NX, BLK, [[1, 128]], OP.is_gt, 0.0, -PC, -1)
    sel(T_IN, T_LT, [[-1, 128]], OP.is_ge, 0.0, PC, 1)
    iota(V("s2a", 0, 146), [[0, 146]], 0, 0)
    sel(V("s2a", 15, 143), BLK, [[0, 8], [-1, 16]], OP.is_ge, 0.0, 1, 0)
    iota(V("kk", 0, 80), [[0, 5], [1, 16]], 0, 0)
    iota(V("kk", 80, 160), [[1, 80]], 0, 0)
    for a, b in PARTS:
        iota(V("cv", a // 16, b // 16), [[-1, (b - a) // 256], [-(b - a) // 256, 16]], 256 - a // 16, 0)
    iota(V("fb", 0, 64), [[64, 64]], K - JUNK, 0)
    iota(V("nl", 0, 128), [[1, 2], [32, 64]], 0, 0)
    iota(V("kd", 0, 24 * NP), [[0, NP], [1, 24]], K + 1, 0)
    load("pool", V("win", BA, BA + S), T.b0[:])
    def wipe(nm, how):
        for lo, hi in ((0, 1040), (1040, 2064)):
            if how == "m":
                move(V(nm, lo, hi), V("zer", 0, hi - lo))
            else:
                copy(how, V(nm, lo, hi), V("zer", 0, hi - lo))

    def spread(nm, col, wide):
        shift("d", V(nm, 0, wide), V("zer", 0, wide), col)
        for lo in range(wide, 1040, wide):
            move(V(nm, lo, lo + wide), V(nm, 0, wide))

    for nm, how in zip(("wb", "wf"), KN["zero"]):
        wipe(nm, how)
    for h in range(2):
        fill(V("hit", 1040 * h + S, 1040 * h + 1040), 0.0)
    fill(V("one", 0, NC), 1.0)
    fill(LESS, -MAGIC)
    fill(MORE, MAGIC)
    copy("a", I_F, I_B)
    copy("a", V("top", 0, 128), V("topb", 0, 128))
    tt(V("topb", 128, 256), I_B, V("topb", 0, 128), OP.subtract)
    ts(V("ri", 4, 5), V("ri", 0, 1), 15, None, OP.bitwise_and)
    cp(ROW, V("ri", 4, 5))
    ts(IS0, ROW, 0.0, None, OP.is_equal)
    lin(DEC, IS0, 1.0, -1.0)
    lin(SCL, IS0, 17.0, -1.0)
    spread("dec", DEC, KN["tile"][0])
    lin(V("one", NC, NC + 1), IS0, 2.0 ** -12, 2.0 ** -12)
    copy("a", V("off", 0, 1), ROW)
    fill(V("off", 1, NC), float(PC))
    lin(V("off", NC, NC + 1), ROW, -1.0, float(S - PC * (NC - 1)))
    lin(V("off", NC + 1, NC + 2), IS0, 0.25, 0.25)
    scale("a", V("sum", 0, 128), BLK, 2.0 ** -12)
    scale("a", V("sum", 0, 128, 16), V("sum", 0, 128, 16), 2.0)
    fill(LESS1, -MAGIC - 1.0)
    lin(HALF, IS0, 0.5, 0.5)
    lin(END, IS0, -1.0, 1.0)
    lin(TWO, IS0, 1.0, 1.0)
    scale("a", V("top", 128, 256), V("topb", 128, 256), TWO)
    scale("a", V("top", 256, 384), I_B, END)
    scale("a", V("top", 384, 512), I_B, DEC)
    ts(V("kk", 0, 80), V("kk", 0, 80), ROW, -8192.0, OP.not_equal, OP.mult)
    shift("a", V("kk", 1, NC), V("kk", 1, NC), 1.0)
    shift("a", V("kk", NC, 80), V("kk", NC, 80), WN - 16.0)
    scale("a", SPARE, END, -2.0)
    lin(V("kk", 81, 80 + NC), V("kk", 81, 80 + NC), IS0, SPARE)
    scale("a", V("topb", 0, 128), I_B, END)
    ts(HB, ROW, 1.0, -2.0 ** -13, OP.is_equal, OP.mult)
    lin(HB, IS0, 0.5, HB)
    shift("a", V("hb", 0, 80), V("zer", 0, 80), HB)
    fill(V("ng", 0, 160), -MAGIC)
    lin(W15, IS0, PC + 1.0, -1.0)
    lin(W16, IS0, PC / 4.0 - 4.0, 4.0)
    ts(WC, ROW, 15.5 - PC, -1.0, OP.is_gt, OP.mult)
    scale("a", V("slw", 0, 144), V("sel", 0, 144), W16)
    for two, col in (("s2b", W15), ("s2c", WC), ("s2d", END)):
        scale("a", V(two, 0, 146), V("s2a", 0, 146), col)
    tt(V("s2a", 0, 144), V("s2b", 0, 144), V("s2d", 2, 146), OP.add)
    ts(V("ri", 5, 6), V("ri", 0, 1), 1, None, OP.bitwise_and)
    ts(ODD, V("ri", 5, 6), 0.5, 14.75, OP.mult, OP.add)
    ts(V("pu0", 0, 256), V("pi32", 0, 256), 0.5, -0.25, OP.mult, OP.add)
    ts(V("pi32", 0, 256), V("pi32", 0, 256), 1, None, OP.bitwise_and)
    ts(V("pa0", 0, 256), V("pi32", 0, 256), 0.5, -0.25, OP.mult, OP.add)
    copy("a", V("sls", 16, 144), V("slw", 0, 128))
    copy("a", V("sls", 0, 16), V("slw", 112, 128))
    copy("a", V("sls", 143, 144), V("slw", 0, 1))
    hand(1, V("pa1", 0, 256), V("pa0", 0, 256))
    turn(V("pu2", 0, 256), V("pu0", 0, 256), -16)
    turn(V("prs2", 0, 4), V("prm0", 0, 4), -16)
    hand(1, V("prs1", 0, 4), V("prs2", 0, 4))
    hand(1, V("pu1", 0, 256), V("pu2", 0, 256))
    hand(-1, V("nz1", 0, S), V("nz0", 0, S))
    hand(-1, V("prm1", 0, 7), V("prm0", 0, 7))
    hand(2, V("prm2", 0, 4), V("prm0", 0, 4))
    if any(w != "g" for pair in KN["how"] for way in pair for w in way):
        scale("a", V("prm0", 8, 10), V("prm0", 5, 7), -1.0)
        scale("a", V("prm1", 8, 10), V("prm1", 5, 7), -1.0)
    fill(TINY, 0.001)
    iota(V("cv", 256, 272), [[0, 16]], 256 - S, 0)
    scale("a", ROW4, ROW, 4.0)
    scale("a", ROW17, ROW, 17.0)
    ts(LT15, ROW, 15.0, None, OP.is_lt)
    lin(V("cv", 0, 272), V("cv", 0, 272), IS0, END)
    shift("a", V("fb", 0, 64), V("fb", 0, 64), ROW4)
    scale("a", ROW2, ROW, 2.0)
    shift("a", V("nl", 0, 128), V("nl", 0, 128), ROW2)
    shift("a", V("kd", 0, 24 * NP), V("kd", 0, 24 * NP), ROW17)
    z = 24 * (NP - 1) + KN["parts"][-1] // 256
    scale("a", V("kd", z, z + 1), V("kd", z, z + 1), LT15)
    for s in range(NP):
        fill(V("kd", 24 * s + 20, 24 * s + 24), 0.0)
    scale("a", V("slm", 0, 144), V("sel", 0, 144), -7.0 / 16)
    scale("a", V("sl1", 0, 144), V("sel", 0, 144), 4.0)
    scale("a", C75, SCL, -4.0)
    scale("a", V("slp", 0, 144), V("sel", 0, 144), C75)
    iota(V("big", 0, 256), [[-16384, 2], [0, 128]], 8192, 0)
    sel(V("big", 0, 256), V("big", 0, 256), [[0, 2], [-1, 128]], OP.is_equal, 0.0, 0, 1)
    lin(GRO, IS0, -255.0, 256.0)
    lin(DFL, IS0, 511.0, 1.0)
    spread("gro", GRO, KN["tile"][1])
    spread("dfl", DFL, KN["tile"][1])

    def who(t):
        k = "1" if t == 1 else "0"
        pr = "prm" + k
        return {"y": V(pr, t, t + 1), "eps": V(pr, 3, 4), "lam": V(pr, 4, 5), "r": (V(pr, 5, 6), V(pr, 6, 7)),
                "n": (V(pr, 8, 9), V(pr, 9, 10)), "nz": "nz" + k}

    def window(t, h):
        return ("wf", "wb")[h] + "1" * (t == 1 and KN["clear"] == "m")

    def starts(t, h, pool, bk, bk2):
        pr = (("prm0", "prm0"), ("prm1", "prs1"), ("prm2", "prs2"))[t][h]
        y, eps, at = V(pr, t, t + 1), V(pr, 3, 4), 1040 * h
        for k, (lo, hi) in enumerate(cuts(KN["wc"])):
            a, x = V("ab", S * h + lo, S * h + hi), V("hit", at + lo, at + hi)
            way = KN["hit"][t][h][k % len(KN["hit"][t][h])]
            act(a, W(pool, lo, hi), AF.Abs, y, -1.0)
            if way == "v":
                ts(x, a, eps, -3.0 / 32, OP.is_le, OP.add)
            else:
                act(x, a, AF.Sign, eps, -1.0)
                ts(x, x, -0.5, -3.0 / 32, OP.is_gt, OP.add)
        mm([(P(bk, 0, NC), I_B, V("mg", 0, NC), True, False)])
        mm([(P(bk, 0, NC), SEL(u), V("hit", at + u, at + PC * NC, PC), False, u == PC - 1) for u in range(PC)])
        o, w, c = 640 * h, 88 * h, 80 * h
        C, CT, RHO = V("sm", o, o + NC), V("sm", o + NC, o + NC + 1), V("sm", o + 88, o + 89)
        E, Q = (V("sm", o + z, o + z + NC) for z in (96, 192))
        M, vals, sl = V("sm", o + 320, o + 400), V("sv", c, c + 80), V("sl", 6 * h, 6 * h + 5)
        sums, marks, dist = P(bk2, 0, NC + 1), P(bk2, 128, 128 + NC), P(bk, 128, 128 + NC)
        wt, rows, whole = V("wt", w + 1, w + NC + 1), V("sm", o + 90, o + 91), P(bk2, NC + 1, NC + 2)
        mm([(P(bk2, 0, NC + 2), I_B, V("off", 0, NC + 2), True, False)])
        rec("act", lambda: g.scalar.activation(ap(wt), ap(P(bk, 0, NC)), AF.Relu, bias=ap(LESS1), scale=1.0, accum_out=ap(rows)),
            [P(bk, 0, NC), LESS1], [wt, rows], ("c", NC + 25.0))
        mm([(whole, V("sum", 0, 128), rows, False, False),
            (sums, T_IN, V("wt", w + 1, w + NC + 2), False, False), (sums, T_GE, V("wt", w, w + NC + 1), False, False),
            (P(bk2, 0, 1), T_NX, V("wt", w + 1, w + 2), False, False), (sums, T_NX, V("wt", w + 2, w + NC + 3), False, True)])
        rec("dve", lambda: g.vector.reciprocal(ap(RHO), ap(whole)), [whole], [RHO], ("c", 230.0))
        mm([(P(bk, 128, 208), I_B, V("kk", 80, 160), True, False), (dist, V("topb", 0, 128), V("mg", 0, NC), False, False)])
        scan(V("sm", o, o + NC + 1), sums, V("one", 0, NC + 1), 0.0, OP.add, OP.mult)
        mm([(P(bk2, 128, 208), I_B, V("kk", 0, 80), True, False), (marks, I_B, V("ng", 0, NC), False, False)])
        mm([(dist, V("top", 256, 384), C, False, False)])
        either("d", lambda: act(E, C, AF.Identity, MORE, RHO), lambda: ts(E, C, RHO, MAGIC, OP.mult, OP.add))
        ts(Q, E, -MAGIC, CT, OP.add, OP.mult)
        mm([(marks, V("top", 0, 128), E, False, True)])
        mm([(dist, V("top", 128, 256), E, False, False), (dist, BLK, V("hb", 0, NC), False, False)])
        mm([(dist, V("top", 384, 512), Q, False, False), (dist, I_B, V("mg", 0, NC), False, False),
            (dist, I_B, V("ng", 0, NC), False, True)])
        scan(M, P(bk2, 128, 208), V("zer", 0, 80), 0.0, OP.max, OP.add)
        cp(sl, V("sm", o + 335, o + 400, 16))
        either("a", lambda: act(vals, P(bk, 128, 208), AF.Relu, 0.0, HALF),
               lambda: ts(vals, P(bk, 128, 208), HALF, 0.0, OP.mult, OP.max))
        wn, sn = window(t, h), ("sf", "sb")[h]
        cp((V(wn, 0, WN), sl), vals)
        for lo, hi in cuts(KN["bs" if h else "fs"]):
            scan(V(sn, lo, hi), V(wn, lo, hi), V("dec", 0, hi - lo), V(sn, lo - 1, lo) if lo else -1.0, OP.max, OP.add)

    def clear(t, h):
        if KN["clear"] == "m":
            if t == 0:
                wipe(window(0, h), "m")
                wipe(window(1, h), "m")
        elif t < 2:
            cp((V(("wf", "wb")[h], 0, WN), V("sl", 6 * h, 6 * h + 5)), V("zer", 0, 80))

    def f_ancestors(t, pool):
        for i, (lo, hi) in enumerate(cuts(KN["fl"])):
            out, a, b = P((4, 2)[i % 2], lo // 16, hi // 16), lo // 2, hi // 2
            mm([(out, SEL(2 * u, "s2a" if u else "s2b"), V("sf", a + u, b, 8), u == 0, False) for u in range(8)]
               + [(out, SEL(14, "s2d"), V("sf", a + 8, b + 1, 8), False, False)]
               + [(out, SEL(2 * u, "s2c"), V(window(t, 0), a + u + 1, b + 1, 8), False, u == 7) for u in range(8)])
            ts(V("al", lo // 16, hi // 16), out, ODD, None, OP.add)
        if t == 2:
            for lo, hi in cuts(KN["fh"]):
                if hi > KN["early"]:
                    hand(2, V("al2", lo // 16, hi // 16), V("al", lo // 16, hi // 16))
        clear(t, 0)
        for lo, hi in cuts(KN["fc"]):
            if t == 2 and hi <= KN["early"]:
                copy("a", V("hh", lo, hi), (V("snd", 0, S), V("al", lo // 16, hi // 16)))
                hand(2, V("lx", lo, hi), V("hh", lo, hi))
                move(V("win", F0 + lo, F0 + hi), V("lx", lo, hi))
            else:
                copy("a", V("win", F0 + lo, F0 + hi), (W(pool, 0, S), V("al2" if t == 2 else "al", lo // 16, hi // 16)))

    def b_ancestors(t, base):
        for i, (lo, hi) in enumerate(cuts(KN["bl"])):
            for k, (a, b) in enumerate(cuts(KN["lc"])):
                if lo <= a < hi:
                    cut(KN["look"][t][k], V("xl", a, b), (V("sb", 0, K // 2), V("pu%d" % t, a // 16, b // 16)))
            out = P((5, 3)[i % 2], lo // 16, hi // 16)
            mm([(out, I_B, V("pa1" if t == 1 else "pa0", lo // 16, hi // 16), True, False)]
               + [(out, SEL(u, "sls" if t else "slw"), V("xl", lo + u, hi, 16), False, u == 15) for u in range(16)])
            cp(V("jl", lo // 16, hi // 16), out)
        out = P(0, 256, 320)
        for lo in (0, 512):
            cut("a", V("cmp", lo, lo + 512), V("sb", 2 * lo, 2 * lo + S, 2))
        mm([(out, SEL(u, "slw"), V("cmp", u, S, 16), u == 0, u == 15) for u in range(16)])
        shift("a", V("fbu", 0, 64) if t else V("fb", 64, 128), out, base - 0.25 - JUNK)
        clear(t, 1)
        if t == 1:
            for lo, hi in cuts(KN["bh"]):
                hand(-2, V("jl1", lo // 16, hi // 16), V("jl", lo // 16, hi // 16))
            hand(-2, V("fb1", 0, 64), V("fbu", 0, 64))
        if t:
            turn(V("fb", 64, 128), V("fb1" if t == 1 else "fbu", 0, 64), 16)

    def pairs(t, pool):
        p = who(t)
        ends = {hi: lo for lo, hi in cuts(KN["cnt"])}
        for i, (lo, hi) in enumerate(cuts(KN["loop"])):
            z, o = hi - lo, lo % 2048
            d, f, m, x = V("dd", lo, hi), V("win", F0 + lo, F0 + hi), V("win", lo, hi), V("miss", lo, hi)
            if t == 2 and hi <= KN["early"]:
                f = V("lx", lo, hi)
            tt(d, (W(pool, 0, S), V("jl1" if t == 1 else "jl", lo // 16, hi // 16)), f, OP.subtract)
            way, y = KN["add"][t][i], P(KN["abk"][i], 0, z)
            if way == "d":
                scale("a", y, d, p["lam"])
                tt(m, f, y, OP.add)
            elif way == "p":
                mm([(y, I_B, V("zer", 0, z), True, False)])
                scale("a", y, d, p["lam"])
                mm([(y, I_F, f, False, True)])
            else:
                scale("a", m, d, p["lam"])
                adds(m, f)
            act(V("ab", o, o + z), y if way == "p" else m, AF.Abs, p["y"], -1.0)
            if way == "p":
                copy("a", m, y)
            ts(x, V("ab", o, o + z), p["eps"], -0.75, OP.is_gt, OP.add)
            s = max(k for k in range(NP) if PARTS[k][0] <= lo)
            a, b = PARTS[s]
            w = (b - a) // 16
            if KN["rank"][s] == "l":
                if lo == a:
                    mm([(P(7 - 4 * (s % 2), 0, w), I_B, V("mg", 0, w), True, False)])
                mm([(P(7 - 4 * (s % 2), 0, w), SEL(r, "slm"), V("miss", a + w * r, a + w * r + w), False, r == 15)
                    for r in range((lo - a) // w, (hi - a) // w)])
            if hi in ends:
                z = ends[hi]
                out = P(6 - 4 * (s % 2), z // 16, hi // 16)
                mm([(out, I_B, V("mg", 0, (hi - z) // 16), True, False)])
                mm([(out, SEL(u, "slm"), V("miss", z + u, hi, 16), False, u == 15) for u in range(16)])
            if hi == b:
                columns(t, s)

    def columns(t, s):
        a, b = PARTS[s]
        w, c, last = (b - a) // 16, a // 16, s == NP - 1
        nc, e, o = w // 16, c + 8 * s, 64 * s
        ne = nc + last
        shift(KN["oka"][t][s], V("okw", c, c + w), P(6 - 4 * (s % 2), c, c + w), LESS)
        if KN["rank"][s] == "l":
            scan(V("el", e + 1, e + w + 1), P(7 - 4 * (s % 2), 0, w), V("ng", 0, w), 0.0, OP.add, OP.add)
        else:
            x = P(6 - 4 * (s % 2), 300, 300 + nc)
            mm([(x, SEL(r, "sl1"), V("okw", c + nc * r, c + nc * r + nc), r == 0, r == 15) for r in range(16)])
            scan(V("el", e + 16, e + w + 1, 16), x, V("zer", 0, nc), 0.0, OP.add, OP.add)
        tot = [V("el", PARTS[k][1] // 16 + 8 * k, PARTS[k][1] // 16 + 8 * k + 1) for k in range(s + 1)]
        z = 400 + 24 * s
        spare, first, total = P(5, z, z + nc), P(5, z + 20, z + 21), P(5, z + 21, z + 22)
        mm([(P(5, z, z + 24), I_F, V("kd", 24 * s, 24 * s + 24), True, False)]
           + [(x, BLK, tot[k], False, False) for k in range(s) for x in ((first, total) if last else (first,))])
        mm([(spare, V("big", 0, 128), V("el", e, e + w, 16), False, False),
            (spare, V("big", 128, 256), V("el", e + 16, e + w + 1, 16), False, False)]
           + [(total, BLK, tot[s], False, False)] * last + [(first, T_LT, tot[s], False, True)])
        tt(V("emp", o, o + ne), V("el", e, e + 16 * ne - 15, 16), P(5, z, z + ne), OP.max)
        ts(V("pl", 18 * s, 18 * s + ne), V("emp", o, o + ne), first, None, OP.add)
        if last:
            ts(V("ix", 0, 128), V("nl", 0, 128), total, None, OP.is_ge)
            tt(V("ix", 0, 128), V("ix", 0, 128), V("fb", 0, 128), OP.mult)
        mm([(P(4, 256 + c + 16 * i, 272 + c + 16 * i), T_LT, V("okw", c + i, c + w, nc), True, True) for i in range(nc)])
        act(V("pv", c, c + w), P(4, 256 + c, 256 + c + w), AF.Exp, TINY, -8.0 * math.log(2.0))
        tt((V("cw", 0, CWN), V("pl", 18 * s, 18 * s + ne)), V("pv", c, c + 16 * ne), V("cv", c, c + 16 * ne), OP.mult)

    def fresh():
        for lo in (0, S):
            move(V("cw", lo, lo + S), V("dfl", 0, S))

    def places(t):
        for lo, hi in cuts(KN["ps"]):
            scan(V("cn", lo, hi), V("gro", 0, hi - lo), V("cw", lo, hi), V("cn", lo - 1, lo) if lo else V("dfl", 0, 1), OP.mult, OP.min)
        if t < 2:
            fresh()
        z = KN["ilb"]
        for k, h in enumerate((KN["first"][t], 1 - KN["first"][t])):
            for lo, hi in cuts(KN["pp"][k]):
                a, b = 64 * h + lo // 16, 64 * h + hi // 16
                mm([(P(z, 0, b - a), I_F, V("ix", a, b), True, False)])
                mm([(P(z, 0, b - a), SEL(u, "slp"), V("cn", 2 * (lo + u) + h, 2 * hi, 32), False, u == 15) for u in range(16)])
                ts(V("il", a, b), P(z, 0, b - a), float(K), None, OP.add)
                z += 1

    def step(t, h, end, dst, done):
        p = who(t)
        late = int(h != KN["first"][t])
        how = KN["how"][t][late]
        for k, (lo, hi) in enumerate(cuts(KN["sc"])):
            z = KN["bank"][late][k]
            x = P(0, z, z + hi - lo)
            mm([(x, I_B, V("zer", 0, hi - lo), True, False)])
            gat = (V("win", 0, end), V("il", 64 * h + lo // 16, 64 * h + hi // 16))
            hh, uu = (V(nm, S * h + lo, S * h + hi) for nm in ("hh", "uu"))
            way = how[k % len(how)]
            if way == "g":
                act(hh, gat, AF.Square)
                tt(uu, gat, hh, OP.subtract)
            if way == "s":
                copy("a", hh, gat)
                act(uu, hh, AF.Square)
                scan(uu, uu, hh, 0.0, OP.max, OP.subtract)
            if way == "p":
                uu = x
                scale("a", hh, gat, -1.0)
                act(uu, hh, AF.Square)
                mm([(uu, I_F, hh, False, False)])
            scale("a", x, uu, p["r" if way == "g" else "n"][h])
            mm([(x, I_B, V(p["nz"], lo, hi), False, True)])
            ts(W(dst, lo, hi), x, 0.0, 1.0, OP.max, OP.min)
            if t == 2 or hi % 512 == 0:
                done(lo if t == 2 else hi - 512, hi)

    def energy():
        for lo in range(0, S, 512):
            for i in range(4):
                v = V("dd", S * i + lo, S * i + lo + 512)
                either("a", lambda v=v: act(v, v, AF.Square), lambda v=v: tt(v, v, v, OP.mult))
                act(v, v, AF.Exp, 0.0, -1.0)
                if i % 2:
                    adds(V("dd", S * i - S + lo, S * i - S + lo + 512), v)
            adds(V("dd", lo, lo + 512), V("dd", 2 * S + lo, 2 * S + lo + 512))
            store(T.ye[:, lo:lo + 512], V("dd", lo, lo + 512))

    def nothing(lo, hi):
        return None

    def ancestors(t, f, b, base):
        f_ancestors(t, f)
        b_ancestors(t, base)
        pairs(t, b)
        places(t)

    fresh()
    starts(0, 1, ("b16", 0), 6, 7)
    starts(0, 0, ("f16", 0), 2, 3)
    ancestors(0, ("f16", 0), ("b16", 0), BA)

    def b_goes(lo, hi):
        hand(-2, V("lb", lo, hi), V("snd", lo, hi))
        turn(V("win", BB + lo, BB + hi), V("lb", lo, hi), 16)
    for h in (KN["first"][0], 1 - KN["first"][0]):
        if h:
            step(0, 1, BB, ("snd", 0), b_goes)
            starts(1, 1, ("snd", 0), 6, 7)
        else:
            step(0, 0, BA, ("pf", 0), nothing)
            starts(1, 0, ("pf", 0), 4, 5)
    ancestors(1, ("pf", 0), ("win", BB), BB)

    for h in (KN["first"][1], 1 - KN["first"][1]):
        if h:
            step(1, 1, BC, ("nb", 0), lambda lo, hi: turn(V("win", BC + lo, BC + hi), V("nb", lo, hi), 16))
            starts(2, 1, ("nb", 0), 4, 5)
        else:
            step(1, 0, BA, ("snd", 0), lambda lo, hi: hand(2, V("lf", lo, hi), V("snd", lo, hi)))
            starts(2, 0, ("snd", 0), 6, 7)
    ancestors(2, ("lf", 0), ("win", BC), BC)
    energy()
    for h in (KN["first"][2], 1 - KN["first"][2]):
        if h:
            step(2, 1, BC + S, ("snd", 0), lambda lo, hi: store(T.yb[:, lo:hi], V("snd", lo, hi)))
        else:
            step(2, 0, BA, ("pf", 0), lambda lo, hi: store(T.yf[:, lo:hi], V("pf", lo, hi)))

    if "order" not in PLAN:
        PLAN["ops"] = ops
        PLAN["deps"] = depends(ops)
        PLAN["order"], PLAN["over"] = arrange(ops, PLAN["deps"], KN["seed"], KN["tries"])
    for i in PLAN["over"]:
        ops[i].update(ops[i]["alt"])
    emit(g, T, ops, PLAN["deps"], PLAN["order"])


def depends(ops):
    def hits(a, b):
        return any(x[0] == y[0] and x[1] < y[2] and y[1] < x[2] for x in a for y in b)
    deps = []
    for i, o in enumerate(ops):
        if o["kind"] == "ext":
            deps.append([j for j in range(i) if ops[j]["kind"] == "remote" and ops[j]["sem"][0] == o["sem"][0]])
            continue
        bank = [x for x in o["r"] if x[0] == "ps"]
        deps.append([j for j in range(i) if ("rows" not in o or o["rows"] != ops[j].get("rows")) and (
            hits(o["r"], ops[j]["w"]) or hits(o["w"], ops[j]["w"]) or hits(o["w"], ops[j]["r"])
            or ((ops[j]["q"] != o["q"] or "alt" in o or "alt" in ops[j]) and hits(bank, ops[j]["r"])))])
    return deps


SPEEDS = ((1.56, 3.8, 1.6, 450e3, 0.22, 0.0006, 1.05), (1.25, 3.0, 1.7, 430e3, 0.27, 0.00042, 1.3),
          (1.85, 4.5, 1.7, 420e3, 0.18, 0.00045, 1.3))


def times(o, m):
    k, c = o["cost"]
    if k == "dma":
        return (0.3 if o["kind"] == "remote" else 1.0 if o["q"] == "pool" else 0.06), m[2] + c / m[3] + m[4], 0.05 + c / m[3]
    t = m[6] * {"c": c * 0.00083, "g": 0.055 + c * 0.00083 * m[0], "sc": 0.055 + c * 0.00083 * m[1], "pe": c * m[5]}[k]
    return t, t + m[4], 0.0


def arrange(ops, deps, seed, tries):
    n0 = len(ops)
    reach, near = [], []
    for i in range(n0):
        r = 0
        for j in deps[i]:
            r |= reach[j]
        near.append([j for j in deps[i] if not r >> j & 1])
        for j in deps[i]:
            r |= 1 << j
        reach.append(r)
    q = [["dve", "act", "pe", "pool", "sp", "ext"].index(o["q"]) for o in ops]
    models = range(len(SPEEDS))
    out, n = list(range(n0)), n0
    for i in range(n0):
        if ops[i]["kind"] in ("dma", "remote"):
            out[i] = n
            n += 1
    pre = [[out[j] for j in near[i]] for i in range(n0)] + [[i] for i in range(n0) if out[i] != i]
    q += [6] * (n - n0)
    suc = [[] for _ in range(n)]
    for i in range(n):
        for j in pre[i]:
            suc[j].append(i)
    hold, lat, other = [[0.0] * n for _ in models], [[0.0] * n for _ in models], [[None] * n for _ in models]
    for m in models:
        for i, o in enumerate(ops):
            a, b, c = times(o, SPEEDS[m])
            hold[m][i], lat[m][i] = a, b - c
            if c:
                hold[m][out[i]] = lat[m][out[i]] = c
            if "alt" in o:
                other[m][i] = times(dict(o, **o["alt"]), SPEEDS[m])[:2]
    over, wake, rnd = set(), [s[4] for s in SPEEDS], [seed]

    def draw(k):
        rnd[0] = (rnd[0] * 1103515245 + 12345) % 2147483648
        return (rnd[0] >> 8) % k

    def turn_over(i):
        over.symmetric_difference_update([i])
        q[i] = 1 - q[i]
        for m in models:
            (hold[m][i], lat[m][i]), other[m][i] = other[m][i], (hold[m][i], lat[m][i])

    head = [i for i in range(n0) if ops[i]["kind"] == "dma" and not near[i] and q[i] != 3]

    def opening(m, ahead):
        tail = [0.0] * n
        for i in sorted(range(n), key=lambda i: -(i if i < n0 else pre[i][0] + 0.5)):
            tail[i] = lat[m][i] + max([tail[j] for j in suc[i]] + [0.0])
        left, ready, free, order = [len(d) for d in pre], [0.0] * n, [0.0] * 7, []
        pool = [i for i in range(n) if not left[i]]
        while pool:
            best = None
            for k in range(7):
                mine = [i for i in pool if q[i] == k]
                if mine:
                    t0 = max(free[k], min(ready[i] for i in mine))
                    i = min((i for i in mine if ready[i] <= t0 + (ahead if k < 5 else 0.0)), key=lambda j: -tail[j])
                    t = max(free[k], ready[i])
                    if best is None or t < best[0]:
                        best = (t, i, k)
            t, i, k = best
            pool.remove(i)
            order.append(i)
            free[k] = t + hold[m][i]
            for j in suc[i]:
                ready[j] = max(ready[j], t + lat[m][i])
                left[j] -= 1
                if not left[j]:
                    pool.append(j)
        return head + [i for i in order if i not in head]

    R, Q = [[0.0] * n for _ in models], [[0.0] * n for _ in models]
    RD, QD = [[0.0] * n for _ in models], [[0.0] * n for _ in models]

    def sweep(part, first, last):
        ends = []
        for m in models:
            r, d, a, b, free, w = R[m], RD[m], hold[m], lat[m], list(first[m]), wake[m]
            for i in part:
                t, k = 0.0, q[i]
                for j in pre[i]:
                    u = r[j] + (a[j] if k == 2 == q[j] else b[j])
                    if u > t:
                        t = u
                d[i] = t
                if free[k] > t and k != 5:
                    t = free[k]
                r[i] = t
                free[k] = t + a[i]
            s, d, free, end = Q[m], QD[m], list(last[m]), 0.0
            for i in reversed(part):
                t, k = 0.0, q[i]
                for j in suc[i]:
                    u = s[j] - w if k == 2 == q[j] else s[j]
                    if u > t:
                        t = u
                d[i] = t
                t += b[i]
                if k != 5 and free[k] + a[i] > t:
                    t = free[k] + a[i]
                s[i] = free[k] = t
                if t + r[i] > end:
                    end = t + r[i]
            ends.append(end)
        return ends

    def relink(part, seqs):
        cnt, nxt = {i: 0 for i in part}, {}
        for i in part:
            for j in suc[i]:
                if j in cnt:
                    cnt[j] += 1
        for k, sq in enumerate(seqs):
            if k != 5:
                for x, y in zip(sq, sq[1:]):
                    nxt[x] = y
                    cnt[y] += 1
        res = [i for i in part if not cnt[i]]
        for i in res:
            for j in suc[i] + ([nxt[i]] if i in nxt else []):
                if j in cnt:
                    cnt[j] -= 1
                    if not cnt[j]:
                        res.append(j)
        return res if len(res) == len(part) else None

    zero, wt = [[0.0] * 7 for _ in models], KN["weights"]

    def settle(seq):
        for _ in range(2):
            sweep(seq, zero, zero)
            at = {j: z for z, j in enumerate(seq)}
            ring = sorted((j for j in seq if q[j] == 6), key=lambda j: (RD[0][j], at[j]))
            seq = relink(seq, [[j for j in seq if q[j] == k] for k in range(6)] + [ring]) or seq
        sweep(seq, zero, zero)
        at = {j: z for z, j in enumerate(seq)}
        seq = sorted(seq, key=lambda j: (R[0][j], at[j]))
        return seq, sweep(seq, zero, zero)

    def moves(v, seqs, first, last, low):
        k, r0, q0 = q[v], R[0], Q[0]
        rlim, qlim = r0[v] + lat[0][v] - wake[0] * (k == 2) - 1e-9, QD[0][v] + 1e-9
        sq = seqs[k]
        at = sq.index(v)
        cur = [R[m][sq[at - 1]] + hold[m][sq[at - 1]] if at else first[m][k] for m in models]
        for z in range(at + 1, min(len(sq), at + KN["far"] + 1)):
            x, c = sq[z], 0.0
            if not (r0[x] < rlim or q0[x] > qlim) or reach[x] >> v & 1:
                break
            for m in models:
                t = max(cur[m], RD[m][x])
                cur[m] = t + hold[m][x]
                u = max(hold[m][v] + (Q[m][sq[z + 1]] if z + 1 < len(sq) else last[m][k]), lat[m][v] + QD[m][v])
                c += wt[m] * max(max(cur[m], RD[m][v]) + u, t + lat[m][x] + QD[m][x], low[m])
            yield c, k, z
        cur = [Q[m][sq[at + 1]] if at + 1 < len(sq) else last[m][k] for m in models]
        for z in range(at - 1, max(-1, at - KN["far"] - 1), -1):
            y, c = sq[z], 0.0
            if not (r0[y] >= RD[0][v] - 1e-9 or q0[y] <= q0[v]) or reach[v] >> y & 1 or y in fixed:
                break
            for m in models:
                cur[m] = u = max(hold[m][y] + cur[m], lat[m][y] + QD[m][y])
                t = max(R[m][sq[z - 1]] + hold[m][sq[z - 1]] if z else first[m][k], RD[m][v])
                c += wt[m] * max(t + max(hold[m][v] + u, lat[m][v] + QD[m][v]), RD[m][y] + u, low[m])
            yield c, k, z
        if other[0][v]:
            k = 1 - k
            sq = seqs[k]
            for z in range(len(sq) + 1):
                if z < len(sq):
                    y = sq[z]
                    if not (r0[y] >= RD[0][v] - 1e-9 or q0[y] <= q0[v]) or reach[v] >> y & 1 or y in fixed:
                        continue
                if z:
                    x = sq[z - 1]
                    if not (r0[x] < rlim or q0[x] > qlim) or reach[x] >> v & 1:
                        break
                c = 0.0
                for m in models:
                    a, b = other[m][v]
                    t = max(R[m][x] + hold[m][x] if z else first[m][k], RD[m][v])
                    c += wt[m] * max(t + max(a + (Q[m][y] if z < len(sq) else last[m][k]), b + QD[m][v]), low[m])
                yield c, k, z

    wide, few, fixed, kept = KN["wide"], KN["few"], set(head), []
    trial = few * len(KN["starts"])
    sweeps = trial + KN["sweeps"]
    for s in range(sweeps):
        if s < trial and s % few == 0:
            for i in set(over):
                turn_over(i)
            order, ends = settle(opening(*KN["starts"][s // few]))
        for lo in range(-(s % 2) * (wide // 2), n, wide):
            lo, hi = max(lo, 0), min(n, lo + wide)
            sweep(order, zero, zero)
            first, last = [[0.0] * 7 for _ in models], [[0.0] * 7 for _ in models]
            for m in models:
                for i in order[:lo]:
                    first[m][q[i]] = R[m][i] + hold[m][i]
                for i in reversed(order[hi:]):
                    last[m][q[i]] = Q[m][i]
            part = order[lo:hi]
            seqs = [[i for i in part if q[i] == k] for k in range(7)]
            ends = sweep(part, first, last)
            top, tabu = (sum(w * e for w, e in zip(wt, ends)), part, set(over)), {}
            for it in range(tries * (hi - lo) // (n * sweeps)):
                sets = [{i for i in part if R[m][i] + Q[m][i] > ends[m] - 1e-6} for m in models]
                cand = sorted(i for i in set().union(*sets) if q[i] < 5 and i not in fixed)
                if not cand:
                    break
                if len(cand) > KN["cand"]:
                    z = draw(len(cand))
                    cand = [cand[(z + k * 7919) % len(cand)] for k in range(KN["cand"])]
                best = None
                for v in cand:
                    banned = tabu.get(v, -1) >= it
                    for c, k, z in moves(v, seqs, first, last, [0.0 if v in sets[m] else ends[m] for m in models]):
                        if (best is None or c < best[0]) and (not banned or c < top[0] - 1e-6):
                            best = (c, v, k, z)
                if best is None:
                    tabu = {}
                    continue
                c, v, k, z = best
                k0 = q[v]
                at = seqs[k0].index(v)
                seqs[k0].pop(at)
                seqs[k].insert(z, v)
                tabu[v] = it + KN["ban"] + draw(KN["ban"])
                new = relink(part, seqs)
                if new is None:
                    seqs[k].remove(v)
                    seqs[k0].insert(at, v)
                    continue
                if k != k0:
                    turn_over(v)
                part = new
                ends = sweep(part, first, last)
                now = sum(w * e for w, e in zip(wt, ends))
                if now <= top[0] + 1e-9:
                    top = (now, part, set(over))
            for i in over ^ top[2]:
                turn_over(i)
            order[lo:hi] = top[1]
        order, ends = settle(order)
        PLAN.setdefault("parts", []).append([round(e, 1) for e in ends])
        if s < trial and s % few == few - 1:
            kept.append((sum(w * e for w, e in zip(wt, ends)), s, order, set(over)))
        if s == trial - 1:
            order = min(kept)[2]
            for i in over ^ min(kept)[3]:
                turn_over(i)
    return [i for i in order if i < n0], over


def emit(g, T, ops, deps, order):
    queue = {"dve": g.vector, "act": g.scalar, "pe": g.tensor, "pool": g, "sp": g.sync}
    known = {q: set() for q in queue}
    issued = {q: [] for q in queue}
    place = {i: k for k, i in enumerate(order)}
    before, waits, needed = {}, {}, set()
    for i in order:
        o = ops[i]
        before[i], waits[i] = set(), []
        if o["kind"] == "ext":
            continue
        kn = known[o["q"]]
        for j in sorted(deps[i], key=lambda k: -place[k]):
            if j not in kn and not (o["q"] == "pe" and ops[j]["q"] == "pe"):
                waits[i].append(j)
                kn.add(j)
                kn.update(before[j])
        before[i] = set(kn)
        if o["kind"] == "c":
            before[i].update(issued[o["q"]])
            issued[o["q"]].append(i)
        needed.update(waits[i])
    count = {q: 0 for q in queue}
    token, dmas, ends = {}, 0, []
    for i in order:
        o = ops[i]
        if o["kind"] == "ext":
            token[i] = (T.sem[o["sem"][0]], o["sem"][1])
            continue
        q = queue[o["q"]]
        for j in waits[i]:
            q.wait_ge(*token[j])
        if o["kind"] == "c":
            ins = o["fn"]()
            if i in needed:
                count[o["q"]] += 1
                ins.then_inc(T.sem[o["q"]], 1)
                token[i] = (T.sem[o["q"]], count[o["q"]])
            continue
        s = T.sem["d%d" % dmas]
        dmas += 1
        if o["kind"] == "dma":
            o["fn"]().then_inc(s, 16)
            token[i] = (s, 16)
        else:
            o["fn"](s)
            token[i] = (s, o["sem"][1])
        if i not in needed:
            ends.append(token[i])
    for tk in ends:
        g.sync.wait_ge(*tk)
